import numpy as np
import ml_dtypes


def mxq(x, axis, fmt="e4m3"):
    dtype, down = {"e4m3": (ml_dtypes.float8_e4m3fn, 7), "e5m2": (ml_dtypes.float8_e5m2, 14)}[fmt]
    v = np.moveaxis(np.asarray(x, np.float32).astype(ml_dtypes.bfloat16).astype(np.float64), axis, -1)
    blocks = v.reshape(v.shape[:-1] + (-1, 32))
    amax = np.abs(blocks).max(-1, keepdims=True)
    byte = np.maximum(np.where(amax > 0, np.frexp(amax)[1] - 1 + 127, 0) - down, 1)
    scale = np.exp2(byte - 127.0)
    codes = (blocks / scale).astype(np.float32).astype(dtype).astype(np.float64)
    return np.moveaxis((codes * scale).reshape(v.shape), -1, axis)


WIDE = False


def mx_kscale(k):
    if not WIDE:
        return np.ones(k)
    levels = np.array([10, -10, 5, -5, 0])
    if k % 512:
        return np.exp2(np.random.permutation(np.resize(levels, k // 32))).repeat(32)
    a = np.empty((k // 512, 16))
    for p in range(k // 512):
        a[p, :8] = np.random.permutation(np.resize(levels, 8))
        for g in range(8):
            far = levels[np.abs(levels - a[p, g]) >= 10]
            a[p, g + 8] = far[np.random.randint(len(far))]
    return np.exp2(a.ravel()).repeat(32)


BF16 = ml_dtypes.bfloat16


def bf(x):
    return np.asarray(x, np.float32).astype(BF16)


def f64(x):
    return np.asarray(x).astype(np.float64)


N, D, F = 1024, 2048, 1024
H = F // 2


def max_min(h):
    hl = h[:, :H]
    hr = h[:, H:]
    return np.concatenate([np.maximum(hl, hr), np.minimum(hl, hr)], axis=1)


def draw0():
    a, u = mx_kscale(D), mx_kscale(F)
    return {
        "x": bf(np.random.standard_normal((N, D)) * a[None, :]),
        "w": bf(np.random.standard_normal((D, F)) / np.sqrt(D) / a[:, None]),
        "d": bf((1.0 + 0.2 * np.random.standard_normal(D)) * a * a),
        "s": bf((1.0 + 0.1 * np.random.standard_normal(F)) * u),
        "t": bf((1.0 + 0.1 * np.random.standard_normal(F)) / u),
        "b": bf(0.4 * np.random.standard_normal(F)),
    }


def core(x, w, d, s, t, b):
    x, w, d, s, t, b = f64(x), f64(w), f64(d), f64(s), f64(t), f64(b)
    wq = mxq(w, 0, "e4m3")
    p = mxq(x, 1, "e4m3") @ wq
    wd = d[:, None] * w
    g = mxq(wd, 0, "e4m3").T @ wq
    ps = p * s[None, :]
    gt = g * t[:, None]
    r = mxq(ps, 1, "e4m3") @ mxq(gt, 0, "e4m3")
    h = 1.5 * p - 0.5 * r + b[None, :]
    return max_min(h)


def e4m3fn_bytes(y):
    return np.clip(np.asarray(y, np.float64), -448.0, 448.0).astype(np.float32).astype(ml_dtypes.float8_e4m3fn).view(np.uint8)


def e4m3fn_values(b):
    return np.asarray(b, np.uint8).view(ml_dtypes.float8_e4m3fn).astype(np.float64)


def setup_inputs():
    d = draw0()
    x0 = np.asarray(d['x']).astype(np.float64)
    s = (np.max(np.abs(x0), axis=(0,), keepdims=True) / 448.0).astype(np.float32)
    out = {}
    for k, v in d.items():
        if k == 'x':
            out['x_bytes'] = e4m3fn_bytes(x0 / s.astype(np.float64))
            out['x_scale'] = s
        else:
            out[k] = v
    return out


def reference(x_bytes, x_scale, w, d, s, t, b):
    return core(e4m3fn_values(x_bytes) * x_scale.astype(np.float64), w, d, s, t, b)

@@ -1,0 +1,476 @@
+from contextlib import ExitStack
+
+import concourse.mybir as mybir
+from concourse.masks import make_identity
+
+F32 = mybir.dt.float32
+BF16 = mybir.dt.bfloat16
+U32 = mybir.dt.uint32
+U8 = mybir.dt.uint8
+FP8 = mybir.dt.float8_e4m3fn
+FP8X4 = mybir.dt.float8_e4m3fn_x4
+ALU = mybir.AluOpType
+ACT = mybir.ActivationFunctionType
+
+P = 128
+N, D, F = 1024, 2048, 1024
+K_PASS = 512
+PASSES = D // K_PASS
+CHUNK = 512
+CHUNKS = F // CHUNK
+A, MEM, E = 16, 4, 8
+HALF = 512
+QUARTER = 256
+FLOPS = 2 * N * D * F + 2 * D * F * F + 2 * N * F * F
+
+VECTOR_PIECES = (
+    ((0, 0), (0, 2), (0, 3), (1, 0), (1, 2), (1, 3)),
+    ((0, 1), (0, 3)),
+    ((1, 0),),
+    ((0, 1),),
+)
+GPSIMD_SHARE = ((0, 0, 0), (1, 0, 0), (2, 0, 0), (3, 0, 0), (3, 0, 1), (3, 1, 0))
+
+
+def tile_bjorckmaxmindense_kernel(tc, x_bytes, x_scale, w, d, s, t, b, out):
+    nc = tc.nc
+    with ExitStack() as ctx:
+        keep = ctx.enter_context(tc.tile_pool(name="keep", bufs=1))
+        pool = ctx.enter_context(tc.tile_pool(name="pool", bufs=2))
+        psum = ctx.enter_context(tc.psum_pool(name="psum", bufs=1))
+        tiles = {}
+
+        def sbuf(key, shape, dtype, tag, bufs):
+            if key not in tiles:
+                tile = pool.tile(shape, dtype, name=tag, tag=tag, bufs=bufs, align_bytes=64)
+                tiles[key] = tile
+            return tiles[key]
+
+        def bank(key, shape, dtype=F32):
+            if key not in tiles:
+                tile = psum.tile(shape, dtype, name="bank", tag="bank", bufs=8)
+                tiles[key] = tile
+            return tiles[key]
+
+        wq = keep.tile([P, PASSES, F], U32, align_bytes=64)
+        wq_scales = keep.tile([P, PASSES, F], U8, align_bytes=64)
+        wdq_scales = keep.tile([P, PASSES, F], U8, align_bytes=64)
+        xq = keep.tile([P, 2, PASSES, HALF], U32, align_bytes=64)
+        xq_scales = keep.tile([P, 2, PASSES, HALF], U8, align_bytes=64)
+        gtq = keep.tile([P, CHUNKS, F], U32, align_bytes=64)
+        gtq_scales = keep.tile([P, CHUNKS, F], U8, align_bytes=64)
+        psq = keep.tile([P, CHUNKS, N], U32, align_bytes=64)
+        psq_scales = keep.tile([P, CHUNKS, N], U8, align_bytes=64)
+
+        x_scale_all = keep.tile([P, D], F32, align_bytes=64)
+        d_sb = keep.tile([P, PASSES, 4], BF16)
+        gain_rows = keep.tile([P, A, E], BF16)
+        gains = keep.tile([P, 3, CHUNKS, MEM], F32)
+        ident16 = keep.tile([P, P], BF16)
+        ident = keep.tile([P, P], F32)
+
+        nc.vector.memset(gain_rows[:], 0.0)
+        nc.gpsimd.dma_start(out=d_sb[:], in_=d.rearrange("(k p j) -> p k j", p=P, j=4))
+        make_identity(nc, ident16[:])
+        make_identity(nc, ident[:])
+
+
+        def load_w(k):
+            raw = sbuf(("w raw", k), [P, 4, F], BF16, "eight_kib", 4)
+            rows = w[K_PASS * k : K_PASS * (k + 1), :].rearrange("(p j) f -> p j f", j=4)
+            if k < 2:
+                for c in range(CHUNKS):
+                    cols = slice(CHUNK * c, CHUNK * (c + 1))
+                    nc.sync.dma_start(out=raw[:, :, cols], in_=rows[:, :, cols])
+            else:
+                nc.sync.dma_start(out=raw[:], in_=rows)
+
+        def load_x(i):
+            codes = sbuf(("x bytes", i), [P, D], U8, "x_bytes", 4)
+            nc.sync.dma_start(out=codes[:], in_=x_bytes[P * i : P * (i + 1), :])
+
+        def load_x_scale():
+            nc.sync.dma_start(out=x_scale_all[:], in_=x_scale.rearrange("o k -> (o k)").partition_broadcast(P))
+
+        def load_gains():
+            for i, v in enumerate((t, s, b)):
+                rows = v.rearrange("(c a m e) -> c m a e", c=CHUNKS, a=A, m=MEM)
+                for c in range(CHUNKS):
+                    r0 = MEM * (CHUNKS * i + c)
+                    nc.scalar.dma_start(out=gain_rows[r0 : r0 + MEM], in_=rows[c])
+
+        def turn_gains():
+            turned = bank("gains", [P, P], BF16)
+            nc.tensor.transpose(turned[:], gain_rows[:].rearrange("p a e -> p (a e)"), ident16[:])
+            nc.scalar.copy(out=gains[:].rearrange("p i c m -> p (i c m)"), in_=turned[:, 0 : 3 * CHUNKS * MEM])
+
+
+        def grouped_w(k):
+            return sbuf(("w grouped", k), [P, CHUNKS, MEM, P, 4], BF16, "grouped", 5)
+
+        def interleave_w(k):
+            src = tiles["w raw", k][:].rearrange("p j (c a m e) -> p c m a e j", c=CHUNKS, a=A, m=MEM)
+            for c in range(CHUNKS):
+                for m in range(MEM):
+                    dst = grouped_w(k)[:, c, m].rearrange("p (a e) j -> p a e j", a=A)
+                    if (c, m) in VECTOR_PIECES[k]:
+                        nc.vector.tensor_copy(out=dst, in_=src[:, c, m])
+                    else:
+                        nc.scalar.copy(out=dst, in_=src[:, c, m])
+
+        def quantise_w(k):
+            nc.vector.quantize_mx(
+                out=wq[:, k, :].bitcast(FP8X4),
+                scales=wq_scales[:, k, :],
+                in_=grouped_w(k)[:].rearrange("p c m q j -> p (c m q j)"),
+            )
+
+        def make_wd(k):
+            wd = sbuf(("wd", k), [P, F, 4], BF16, "grouped", 5)
+            nc.vector.tensor_tensor(
+                out=wd[:],
+                in0=grouped_w(k)[:].rearrange("p c m q j -> p (c m q) j"),
+                in1=d_sb[:, k : k + 1, :].to_broadcast([P, F, 4]),
+                op=ALU.mult,
+            )
+
+        def quantise_wd(k):
+            codes = sbuf(("wd codes", k), [P, F], U32, "four_kib", 4)
+            nc.vector.quantize_mx(
+                out=codes[:].bitcast(FP8X4),
+                scales=wdq_scales[:, k, :],
+                in_=tiles["wd", k][:].rearrange("p f j -> p (f j)"),
+            )
+
+
+        def g_matmuls(c, n, m, passes):
+            acc = bank(("g", c, n, m), [P, CHUNK])
+            rows = slice(CHUNK * c + P * m, CHUNK * c + P * (m + 1))
+            cols = slice(CHUNK * n, CHUNK * (n + 1))
+            for k in passes:
+                nc.tensor.matmul_mx(
+                    out=acc[:],
+                    lhsT=tiles["wd codes", k][:, rows].bitcast(FP8X4),
+                    lhsT_scale=wdq_scales[:, k, rows],
+                    rhs=wq[:, k, cols].bitcast(FP8X4),
+                    rhs_scale=wq_scales[:, k, cols],
+                    start=(k == 0),
+                    stop=(k == PASSES - 1),
+                )
+
+        def g_sweep(k):
+            for c in range(CHUNKS):
+                for m in range(MEM):
+                    g_matmuls(c, 0, m, (k,))
+
+        def g_pair(c, i):
+            for m in (2 * i, 2 * i + 1):
+                g_matmuls(c, 1, m, range(PASSES))
+
+        def gt_out(c, n, members):
+            planes = sbuf(("gt planes", c, n), [P, MEM, CHUNK], BF16, "planes", 6)
+            for m in members:
+                nc.scalar.activation(
+                    out=planes[:, m, :], in_=tiles["g", c, n, m][:], func=ACT.Copy, scale=gains[:, 0, c, m : m + 1]
+                )
+
+        def gt_pair_out(c, i):
+            gt_out(c, 1, (2 * i, 2 * i + 1))
+
+        def interleave_gt(c, n):
+            grouped = sbuf(("gt grouped", c, n), [P, CHUNK, MEM], BF16, "planes", 6)
+            src = tiles["gt planes", c, n][:].rearrange("p m f -> p f m")
+            if (c, n) == (0, 0):
+                nc.scalar.copy(out=grouped[:], in_=src)
+            else:
+                nc.vector.tensor_copy(out=grouped[:], in_=src)
+
+        def quantise_gt(c, n):
+            cols = slice(CHUNK * n, CHUNK * (n + 1))
+            nc.vector.quantize_mx(
+                out=gtq[:, c, cols].bitcast(FP8X4),
+                scales=gtq_scales[:, c, cols],
+                in_=tiles["gt grouped", c, n][:].rearrange("p f m -> p (f m)"),
+            )
+
+
+        def widen_x(i):
+            x16 = sbuf(("x", i), [P, D], BF16, "x", 2)
+            nc.vector.tensor_tensor(
+                out=x16[:], in0=tiles["x bytes", i][:].bitcast(FP8), in1=x_scale_all[:], op=ALU.mult
+            )
+
+        def transpose_x(i):
+            words = tiles["x", i][:].bitcast(F32)
+            for y in range(2):
+                turned = bank(("x turned", i, y), [P, 2, 2, P])
+                for z in range(2):
+                    w0 = K_PASS // 2 * (2 * y + z)
+                    for u in range(2):
+                        nc.tensor.transpose(turned[:, z, u, :], words[:, w0 + u : w0 + K_PASS // 2 : 2], ident[:])
+
+        def x_out(i):
+            grouped = sbuf(("x grouped", i // 4), [P, PASSES, HALF, 4], BF16, "x_grouped", 2)
+            r0 = P * (i % 4)
+            for y in range(2):
+                nc.scalar.copy(
+                    out=grouped[:].bitcast(F32)[:, 2 * y : 2 * y + 2, r0 : r0 + P, :],
+                    in_=tiles["x turned", i, y][:].rearrange("p z u r -> p z r u"),
+                )
+
+        def quantise_x(h, y):
+            ks = slice(2 * y, 2 * y + 2)
+            nc.vector.quantize_mx(
+                out=xq[:, h, ks, :].rearrange("p k r -> p (k r)").bitcast(FP8X4),
+                scales=xq_scales[:, h, ks, :].rearrange("p k r -> p (k r)"),
+                in_=tiles["x grouped", h][:, ks].rearrange("p k r j -> p (k r j)"),
+            )
+
+
+        def p_pair(h, c, i):
+            for m in (2 * i, 2 * i + 1):
+                acc = bank(("p", h, c, m), [P, HALF])
+                rows = slice(CHUNK * c + P * m, CHUNK * c + P * (m + 1))
+                for k in range(PASSES):
+                    nc.tensor.matmul_mx(
+                        out=acc[:],
+                        lhsT=wq[:, k, rows].bitcast(FP8X4),
+                        lhsT_scale=wq_scales[:, k, rows],
+                        rhs=xq[:, h, k, :].bitcast(FP8X4),
+                        rhs_scale=xq_scales[:, h, k, :],
+                        start=(k == 0),
+                        stop=(k == PASSES - 1),
+                    )
+
+        def p_pair_out(h, c, i):
+            planes = sbuf(("ps planes", h, c), [P, MEM, HALF], BF16, "planes", 6)
+            affine = sbuf(("1.5 p + b", h, c), [P, MEM, HALF], F32, "eight_kib", 4)
+            for m in (2 * i, 2 * i + 1):
+                acc = tiles["p", h, c, m]
+                nc.scalar.activation(
+                    out=planes[:, m, :], in_=acc[:], func=ACT.Copy, scale=gains[:, 1, c, m : m + 1]
+                )
+                nc.scalar.activation(
+                    out=affine[:, m, :], in_=acc[:], func=ACT.Identity, scale=1.5, bias=gains[:, 2, c, m : m + 1]
+                )
+
+        def interleave_ps(h, c):
+            grouped = sbuf(("ps grouped", h, c), [P, HALF, MEM], BF16, "planes", 6)
+            nc.vector.tensor_copy(out=grouped[:], in_=tiles["ps planes", h, c][:].rearrange("p m r -> p r m"))
+
+        def quantise_ps(h, c):
+            tok = slice(HALF * h, HALF * (h + 1))
+            nc.vector.quantize_mx(
+                out=psq[:, c, tok].bitcast(FP8X4),
+                scales=psq_scales[:, c, tok],
+                in_=tiles["ps grouped", h, c][:].rearrange("p r m -> p (r m)"),
+            )
+
+
+        def r_chunk(q, c):
+            tok = slice(QUARTER * q, QUARTER * (q + 1))
+            for i in range(2):
+                acc = bank(("r", q, c, i), [P, 2, QUARTER])
+                for z in range(2):
+                    m = 2 * i + z
+                    rows = slice(CHUNK * c + P * m, CHUNK * c + P * (m + 1))
+                    for k in range(CHUNKS):
+                        nc.tensor.matmul_mx(
+                            out=acc[:, z, :],
+                            lhsT=gtq[:, k, rows].bitcast(FP8X4),
+                            lhsT_scale=gtq_scales[:, k, rows],
+                            rhs=psq[:, k, tok].bitcast(FP8X4),
+                            rhs_scale=psq_scales[:, k, tok],
+                            start=(k == 0),
+                            stop=(k == CHUNKS - 1),
+                        )
+
+        def combine(q, c):
+            h_t = sbuf(("h", q, c), [P, MEM, QUARTER], F32, "four_kib", 4)
+            r0 = QUARTER * (q % 2)
+            for i in range(2):
+                members = slice(2 * i, 2 * i + 2)
+                acc = tiles["r", q, c, i]
+                affine = tiles["1.5 p + b", q // 2, c][:, members, r0 : r0 + QUARTER]
+                if (q, c, i) in GPSIMD_SHARE:
+                    half_r = sbuf(("half r", q, c, i), [P, 2, QUARTER], F32, "x", 2)
+                    nc.scalar.activation(out=half_r[:], in_=acc[:], func=ACT.Copy, scale=-0.5)
+                    nc.gpsimd.tensor_tensor(out=h_t[:, members, :], in0=half_r[:], in1=affine, op=ALU.add)
+                else:
+                    nc.vector.scalar_tensor_tensor(
+                        out=h_t[:, members, :], in0=acc[:], scalar=-0.5, in1=affine, op0=ALU.mult, op1=ALU.add
+                    )
+
+
+        def transpose_h(q, i):
+            for c in (1, 0):
+                turned = bank(("h turned", q, i, c), [P, MEM, P])
+                for m in range(MEM):
+                    nc.tensor.transpose(turned[:, m, :], tiles["h", q, c][:, m, P * i : P * (i + 1)], ident[:])
+
+        def by_channel(turned):
+            return turned[:].rearrange("p m (a e) -> p a m e", a=A)
+
+        def copy_right(q, i):
+            right = sbuf(("right", q, i), [P, A, MEM, E], F32, "right", 2)
+            nc.scalar.copy(out=right[:], in_=by_channel(tiles["h turned", q, i, 1]))
+
+        def max_min(q, i):
+            res = sbuf(("result", q, i), [P, 2, A, MEM, E], F32, "planes", 6)
+            tok = slice(QUARTER * q + P * i, QUARTER * q + P * (i + 1))
+            for c, op in enumerate((ALU.max, ALU.min)):
+                nc.vector.tensor_tensor(
+                    out=res[:, c], in0=by_channel(tiles["h turned", q, i, 0]), in1=tiles["right", q, i][:], op=op
+                )
+                nc.sync.dma_start(
+                    out=out[tok, CHUNK * c : CHUNK * (c + 1)], in_=res[:, c].rearrange("p a m e -> p (a m e)")
+                )
+
+        ctx.enter_context(tc.manual_schedule())
+
+        for k in range(PASSES):
+            load_w(k)
+        load_x_scale()
+        for i in (0, 1, 2, 4):
+            load_x(i)
+
+        interleave_w(0)
+        load_gains()
+        interleave_w(1)
+        make_wd(0)
+        quantise_w(0)
+        quantise_wd(0)
+        make_wd(1)
+        interleave_w(2)
+        turn_gains()
+        g_sweep(0)
+        quantise_wd(1)
+        quantise_w(1)
+        quantise_w(2)
+        make_wd(2)
+        interleave_w(3)
+        g_sweep(1)
+        quantise_wd(2)
+        g_sweep(2)
+        make_wd(3)
+        quantise_w(3)
+        quantise_wd(3)
+        widen_x(0)
+        g_sweep(3)
+        widen_x(1)
+
+        gt_out(0, 0, range(MEM))
+        transpose_x(0)
+        x_out(0)
+        load_x(5)
+        widen_x(2)
+        g_pair(0, 0)
+        transpose_x(1)
+        gt_out(1, 0, range(MEM))
+        load_x(3)
+        widen_x(4)
+        g_pair(1, 0)
+        x_out(1)
+        transpose_x(2)
+        interleave_gt(0, 0)
+        x_out(2)
+        load_x(6)
+        widen_x(5)
+        transpose_x(4)
+        gt_pair_out(0, 0)
+        widen_x(3)
+        g_pair(1, 1)
+        transpose_x(5)
+        x_out(4)
+        load_x(7)
+        widen_x(6)
+        transpose_x(3)
+        gt_pair_out(1, 0)
+        x_out(3)
+        gt_pair_out(1, 1)
+        g_pair(0, 1)
+        x_out(5)
+        transpose_x(6)
+        quantise_x(0, 0)
+        quantise_x(0, 1)
+        widen_x(7)
+        x_out(6)
+        interleave_gt(1, 0)
+        gt_pair_out(0, 1)
+
+        p_pair(0, 0, 0)
+        p_pair(0, 0, 1)
+        p_pair_out(0, 0, 0)
+        interleave_gt(0, 1)
+        interleave_gt(1, 1)
+        transpose_x(7)
+        quantise_gt(1, 0)
+        p_pair(0, 1, 0)
+        x_out(7)
+        quantise_x(1, 1)
+        quantise_x(1, 0)
+        p_pair_out(0, 0, 1)
+        p_pair(0, 1, 1)
+        interleave_ps(0, 0)
+        quantise_gt(0, 0)
+        quantise_gt(1, 1)
+        p_pair(1, 0, 0)
+        p_pair_out(0, 1, 0)
+        p_pair(1, 1, 0)
+        quantise_gt(0, 1)
+        p_pair_out(0, 1, 1)
+        interleave_ps(0, 1)
+        p_pair(1, 0, 1)
+        quantise_ps(0, 1)
+        p_pair_out(1, 0, 0)
+        p_pair_out(1, 0, 1)
+        quantise_ps(0, 0)
+
+        r_chunk(1, 0)
+        r_chunk(0, 0)
+        interleave_ps(1, 0)
+        combine(0, 0)
+        r_chunk(0, 1)
+        quantise_ps(1, 0)
+        p_pair(1, 1, 1)
+        combine(0, 1)
+        r_chunk(1, 1)
+        combine(1, 0)
+        transpose_h(0, 0)
+        combine(1, 1)
+        p_pair_out(1, 1, 0)
+        transpose_h(1, 0)
+        p_pair_out(1, 1, 1)
+        transpose_h(0, 1)
+        copy_right(0, 0)
+        interleave_ps(1, 1)
+        quantise_ps(1, 1)
+        copy_right(1, 0)
+        transpose_h(1, 1)
+        max_min(0, 0)
+        copy_right(1, 1)
+
+        r_chunk(2, 0)
+        max_min(1, 0)
+        combine(2, 0)
+        copy_right(0, 1)
+        r_chunk(3, 0)
+        r_chunk(2, 1)
+        max_min(1, 1)
+        r_chunk(3, 1)
+        combine(2, 1)
+        max_min(0, 1)
+        transpose_h(2, 0)
+        combine(3, 0)
+        combine(3, 1)
+        copy_right(2, 0)
+        transpose_h(2, 1)
+        copy_right(2, 1)
+        transpose_h(3, 0)
+        transpose_h(3, 1)
+        max_min(2, 0)
+        copy_right(3, 0)
+        max_min(2, 1)
+        copy_right(3, 1)
+        max_min(3, 0)
+        max_min(3, 1)

@@ -19,74 +19,86 @@ PASSES = D // K_PASS
 CHUNK = 512
 CHUNKS = F // CHUNK
 A, MEM, E = 16, 4, 8
-HALF = 512
 QUARTER = 256
+QUARTERS = N // QUARTER
+BANKS = 8
 FLOPS = 2 * N * D * F + 2 * D * F * F + 2 * N * F * F
 
-VECTOR_PIECES = (
-    ((0, 0), (0, 2), (0, 3), (1, 0), (1, 2), (1, 3)),
-    ((0, 1), (0, 3)),
-    ((1, 0),),
-    ((0, 1),),
-)
-GPSIMD_SHARE = ((0, 0, 0), (1, 0, 0), (2, 0, 0), (3, 0, 0), (3, 0, 1), (3, 1, 0))
+VECTOR_BLOCKS = (12, 4, 2, 2, 2, 2, 4, 2)
+ADDED_ON_TENSOR = (3,)
+ADDED_ON_GPSIMD = ()
+GT_ON_SCALAR = ((0, 0),)
+PS_ON_SCALAR = ((2, 0), (3, 0))
 
 
 def tile_bjorckmaxmindense_kernel(tc, x_bytes, x_scale, w, d, s, t, b, out):
     nc = tc.nc
     with ExitStack() as ctx:
-        keep = ctx.enter_context(tc.tile_pool(name="keep", bufs=1))
-        pool = ctx.enter_context(tc.tile_pool(name="pool", bufs=2))
+        pool = ctx.enter_context(tc.tile_pool(name="pool", bufs=1))
         psum = ctx.enter_context(tc.psum_pool(name="psum", bufs=1))
         tiles = {}
+        taken = {}
 
-        def sbuf(key, shape, dtype, tag, bufs):
+        def sbuf(key, shape, dtype, ring=None, slots=1):
             if key not in tiles:
-                tile = pool.tile(shape, dtype, name=tag, tag=tag, bufs=bufs, align_bytes=64)
+                if ring is None:
+                    tag = "keep%d" % len(tiles)
+                else:
+                    tag = "%s%d" % (ring, taken.get(ring, 0) % slots)
+                    taken[ring] = taken.get(ring, 0) + 1
+                tile = pool.tile(shape, dtype, name=tag, tag=tag, align_bytes=64)
                 tiles[key] = tile
             return tiles[key]
 
         def bank(key, shape, dtype=F32):
             if key not in tiles:
-                tile = psum.tile(shape, dtype, name="bank", tag="bank", bufs=8)
+                tag = "bank%d" % (taken.get("bank", 0) % BANKS)
+                taken["bank"] = taken.get("bank", 0) + 1
+                tile = psum.tile(shape, dtype, name=tag, tag=tag)
                 tiles[key] = tile
             return tiles[key]
 
-        wq = keep.tile([P, PASSES, F], U32, align_bytes=64)
-        wq_scales = keep.tile([P, PASSES, F], U8, align_bytes=64)
-        wdq_scales = keep.tile([P, PASSES, F], U8, align_bytes=64)
-        xq = keep.tile([P, 2, PASSES, HALF], U32, align_bytes=64)
-        xq_scales = keep.tile([P, 2, PASSES, HALF], U8, align_bytes=64)
-        gtq = keep.tile([P, CHUNKS, F], U32, align_bytes=64)
-        gtq_scales = keep.tile([P, CHUNKS, F], U8, align_bytes=64)
-        psq = keep.tile([P, CHUNKS, N], U32, align_bytes=64)
-        psq_scales = keep.tile([P, CHUNKS, N], U8, align_bytes=64)
+        def quantise(key, src, width, ring=None, slots=1):
+            codes = sbuf((key, "codes"), [P, width], U32, ring and ring + "_codes", slots)
+            scales = sbuf((key, "scales"), [P, width], U8, ring and ring + "_scales", slots)
+            nc.vector.quantize_mx(out=codes[:].bitcast(FP8X4), scales=scales[:], in_=src)
 
-        x_scale_all = keep.tile([P, D], F32, align_bytes=64)
-        d_sb = keep.tile([P, PASSES, 4], BF16)
-        gain_rows = keep.tile([P, A, E], BF16)
-        gains = keep.tile([P, 3, CHUNKS, MEM], F32)
-        ident16 = keep.tile([P, P], BF16)
-        ident = keep.tile([P, P], F32)
+        def matmul(acc, left, left_cols, right, right_cols, start, stop):
+            nc.tensor.matmul_mx(
+                out=acc,
+                lhsT=tiles[left, "codes"][:, left_cols].bitcast(FP8X4),
+                lhsT_scale=tiles[left, "scales"][:, left_cols],
+                rhs=tiles[right, "codes"][:, right_cols].bitcast(FP8X4),
+                rhs_scale=tiles[right, "scales"][:, right_cols],
+                start=start,
+                stop=stop,
+            )
+
+        def member(m):
+            return slice(P * m, P * (m + 1))
+
+        x_scale_all = sbuf("x scale", [P, D], F32)
+        d_sb = sbuf("d", [P, PASSES, 4], BF16)
+        gain_rows = sbuf("gain rows", [P, CHUNKS, A * E], BF16)
+        gains = sbuf("gains", [P, CHUNKS, 3, MEM], F32)
+        ident16 = sbuf("ident16", [P, P], BF16)
+        ident = sbuf("ident", [P, P], F32)
 
         nc.vector.memset(gain_rows[:], 0.0)
-        nc.gpsimd.dma_start(out=d_sb[:], in_=d.rearrange("(k p j) -> p k j", p=P, j=4))
+        nc.scalar.dma_start(out=d_sb[:], in_=d.rearrange("(k p j) -> p k j", p=P, j=4))
         make_identity(nc, ident16[:])
         make_identity(nc, ident[:])
 
 
-        def load_w(k):
-            raw = sbuf(("w raw", k), [P, 4, F], BF16, "eight_kib", 4)
-            rows = w[K_PASS * k : K_PASS * (k + 1), :].rearrange("(p j) f -> p j f", j=4)
-            if k < 2:
-                for c in range(CHUNKS):
-                    cols = slice(CHUNK * c, CHUNK * (c + 1))
-                    nc.sync.dma_start(out=raw[:, :, cols], in_=rows[:, :, cols])
-            else:
-                nc.sync.dma_start(out=raw[:], in_=rows)
+        def load_w(c, k, parts=1):
+            raw = sbuf(("w raw", c, k), [P, 4, CHUNK], BF16, "four_kib", 8)
+            rows = w[K_PASS * k : K_PASS * (k + 1), CHUNK * c : CHUNK * (c + 1)].rearrange("(p j) f -> p j f", j=4)
+            for i in range(parts):
+                cols = slice(CHUNK // parts * i, CHUNK // parts * (i + 1))
+                nc.sync.dma_start(out=raw[:, :, cols], in_=rows[:, :, cols])
 
         def load_x(i):
-            codes = sbuf(("x bytes", i), [P, D], U8, "x_bytes", 4)
+            codes = sbuf(("x bytes", i), [P, D], U8, "x_bytes", 8)
             nc.sync.dma_start(out=codes[:], in_=x_bytes[P * i : P * (i + 1), :])
 
         def load_x_scale():
@@ -94,108 +106,81 @@ def tile_bjorckmaxmindense_kernel(tc, x_bytes, x_scale, w, d, s, t, b, out):
 
         def load_gains():
             for i, v in enumerate((t, s, b)):
-                rows = v.rearrange("(c a m e) -> c m a e", c=CHUNKS, a=A, m=MEM)
-                for c in range(CHUNKS):
-                    r0 = MEM * (CHUNKS * i + c)
-                    nc.scalar.dma_start(out=gain_rows[r0 : r0 + MEM], in_=rows[c])
+                nc.sync.dma_start(
+                    out=gain_rows[MEM * i : MEM * (i + 1)].rearrange("m c (a e) -> m (c a) e", e=E),
+                    in_=v.rearrange("(ca m e) -> m ca e", m=MEM, e=E),
+                )
 
         def turn_gains():
-            turned = bank("gains", [P, P], BF16)
-            nc.tensor.transpose(turned[:], gain_rows[:].rearrange("p a e -> p (a e)"), ident16[:])
-            nc.scalar.copy(out=gains[:].rearrange("p i c m -> p (i c m)"), in_=turned[:, 0 : 3 * CHUNKS * MEM])
-
-
-        def grouped_w(k):
-            return sbuf(("w grouped", k), [P, CHUNKS, MEM, P, 4], BF16, "grouped", 5)
-
-        def interleave_w(k):
-            src = tiles["w raw", k][:].rearrange("p j (c a m e) -> p c m a e j", c=CHUNKS, a=A, m=MEM)
+            turned = bank("gains turned", [P, CHUNKS, P], BF16)
             for c in range(CHUNKS):
-                for m in range(MEM):
-                    dst = grouped_w(k)[:, c, m].rearrange("p (a e) j -> p a e j", a=A)
-                    if (c, m) in VECTOR_PIECES[k]:
-                        nc.vector.tensor_copy(out=dst, in_=src[:, c, m])
-                    else:
-                        nc.scalar.copy(out=dst, in_=src[:, c, m])
+                nc.tensor.transpose(turned[:, c, :], gain_rows[:, c, :], ident16[:])
+            nc.scalar.copy(out=gains[:].rearrange("p c i m -> p c (i m)"), in_=turned[:, :, 0 : 3 * MEM])
 
-        def quantise_w(k):
-            nc.vector.quantize_mx(
-                out=wq[:, k, :].bitcast(FP8X4),
-                scales=wq_scales[:, k, :],
-                in_=grouped_w(k)[:].rearrange("p c m q j -> p (c m q j)"),
-            )
+        def gain(i, c, m):
+            return gains[:, c, i, m : m + 1]
 
-        def make_wd(k):
-            wd = sbuf(("wd", k), [P, F, 4], BF16, "grouped", 5)
+
+        def interleave_w(c, k):
+            grouped = sbuf(("w grouped", c, k), [P, MEM, A, E, 4], BF16, "stage", 4)
+            src = tiles["w raw", c, k][:].rearrange("p j (a m e) -> p m a e j", a=A, m=MEM)
+            split = VECTOR_BLOCKS[PASSES * c + k]
+            for a0 in range(0, split, A // 2):
+                a1 = min(split, a0 + A // 2)
+                nc.vector.tensor_copy(out=grouped[:, :, a0:a1], in_=src[:, :, a0:a1])
+            nc.scalar.copy(out=grouped[:, :, split:A], in_=src[:, :, split:A])
+
+        def quantise_w(c, k):
+            grouped = tiles["w grouped", c, k]
+            last = (c, k) == (CHUNKS - 1, PASSES - 1)
+            if last:
+                quantise(("w", c, k), grouped[:].rearrange("p m a e j -> p (m a e j)"), CHUNK)
+            wd = sbuf(("wd", c, k), [P, CHUNK, 4], BF16, "wd", 2)
             nc.vector.tensor_tensor(
                 out=wd[:],
-                in0=grouped_w(k)[:].rearrange("p c m q j -> p (c m q) j"),
-                in1=d_sb[:, k : k + 1, :].to_broadcast([P, F, 4]),
+                in0=grouped[:].rearrange("p m a e j -> p (m a e) j"),
+                in1=d_sb[:, k : k + 1, :].to_broadcast([P, CHUNK, 4]),
                 op=ALU.mult,
             )
-
-        def quantise_wd(k):
-            codes = sbuf(("wd codes", k), [P, F], U32, "four_kib", 4)
-            nc.vector.quantize_mx(
-                out=codes[:].bitcast(FP8X4),
-                scales=wdq_scales[:, k, :],
-                in_=tiles["wd", k][:].rearrange("p f j -> p (f j)"),
-            )
+            if not last:
+                quantise(("w", c, k), grouped[:].rearrange("p m a e j -> p (m a e j)"), CHUNK)
+            quantise(("wd", c, k), wd[:].rearrange("p f j -> p (f j)"), CHUNK)
 
 
-        def g_matmuls(c, n, m, passes):
+        def g_passes(c, n, m, passes):
             acc = bank(("g", c, n, m), [P, CHUNK])
-            rows = slice(CHUNK * c + P * m, CHUNK * c + P * (m + 1))
-            cols = slice(CHUNK * n, CHUNK * (n + 1))
             for k in passes:
-                nc.tensor.matmul_mx(
-                    out=acc[:],
-                    lhsT=tiles["wd codes", k][:, rows].bitcast(FP8X4),
-                    lhsT_scale=wdq_scales[:, k, rows],
-                    rhs=wq[:, k, cols].bitcast(FP8X4),
-                    rhs_scale=wq_scales[:, k, cols],
-                    start=(k == 0),
-                    stop=(k == PASSES - 1),
-                )
+                matmul(acc[:], ("wd", c, k), member(m), ("w", n, k), slice(0, CHUNK), k == 0, k == PASSES - 1)
 
-        def g_sweep(k):
-            for c in range(CHUNKS):
-                for m in range(MEM):
-                    g_matmuls(c, 0, m, (k,))
+        def g_sweep(c, n, k):
+            for m in range(MEM):
+                g_passes(c, n, m, (k,))
 
-        def g_pair(c, i):
-            for m in (2 * i, 2 * i + 1):
-                g_matmuls(c, 1, m, range(PASSES))
+        def g_block(c, n, members):
+            for m in members:
+                g_passes(c, n, m, range(PASSES))
 
-        def gt_out(c, n, members):
-            planes = sbuf(("gt planes", c, n), [P, MEM, CHUNK], BF16, "planes", 6)
+        def gt_out(c, n, members=range(MEM)):
+            planes = sbuf(("gt planes", c, n), [P, MEM, CHUNK], BF16, "gt_planes", 3)
             for m in members:
                 nc.scalar.activation(
-                    out=planes[:, m, :], in_=tiles["g", c, n, m][:], func=ACT.Copy, scale=gains[:, 0, c, m : m + 1]
+                    out=planes[:, m, :], in_=tiles["g", c, n, m][:], func=ACT.Copy, scale=gain(0, c, m)
                 )
 
-        def gt_pair_out(c, i):
-            gt_out(c, 1, (2 * i, 2 * i + 1))
-
         def interleave_gt(c, n):
-            grouped = sbuf(("gt grouped", c, n), [P, CHUNK, MEM], BF16, "planes", 6)
+            grouped = sbuf(("gt grouped", c, n), [P, CHUNK, MEM], BF16, "stage", 4)
             src = tiles["gt planes", c, n][:].rearrange("p m f -> p f m")
-            if (c, n) == (0, 0):
+            if (c, n) in GT_ON_SCALAR:
                 nc.scalar.copy(out=grouped[:], in_=src)
             else:
                 nc.vector.tensor_copy(out=grouped[:], in_=src)
 
         def quantise_gt(c, n):
-            cols = slice(CHUNK * n, CHUNK * (n + 1))
-            nc.vector.quantize_mx(
-                out=gtq[:, c, cols].bitcast(FP8X4),
-                scales=gtq_scales[:, c, cols],
-                in_=tiles["gt grouped", c, n][:].rearrange("p f m -> p (f m)"),
-            )
+            quantise(("gt", c, n), tiles["gt grouped", c, n][:].rearrange("p f m -> p (f m)"), CHUNK)
 
 
         def widen_x(i):
-            x16 = sbuf(("x", i), [P, D], BF16, "x", 2)
+            x16 = sbuf(("x", i), [P, D], BF16, "x", 4)
             nc.vector.tensor_tensor(
                 out=x16[:], in0=tiles["x bytes", i][:].bitcast(FP8), in1=x_scale_all[:], op=ALU.mult
             )
@@ -210,267 +195,218 @@ def tile_bjorckmaxmindense_kernel(tc, x_bytes, x_scale, w, d, s, t, b, out):
                         nc.tensor.transpose(turned[:, z, u, :], words[:, w0 + u : w0 + K_PASS // 2 : 2], ident[:])
 
         def x_out(i):
-            grouped = sbuf(("x grouped", i // 4), [P, PASSES, HALF, 4], BF16, "x_grouped", 2)
-            r0 = P * (i % 4)
+            grouped = sbuf(("x grouped", i // 2), [P, PASSES, QUARTER, 4], BF16, "x_grouped", 2)
+            r0 = P * (i % 2)
             for y in range(2):
                 nc.scalar.copy(
                     out=grouped[:].bitcast(F32)[:, 2 * y : 2 * y + 2, r0 : r0 + P, :],
                     in_=tiles["x turned", i, y][:].rearrange("p z u r -> p z r u"),
                 )
 
-        def quantise_x(h, y):
-            ks = slice(2 * y, 2 * y + 2)
-            nc.vector.quantize_mx(
-                out=xq[:, h, ks, :].rearrange("p k r -> p (k r)").bitcast(FP8X4),
-                scales=xq_scales[:, h, ks, :].rearrange("p k r -> p (k r)"),
-                in_=tiles["x grouped", h][:, ks].rearrange("p k r j -> p (k r j)"),
-            )
+        def quantise_x(q):
+            quantise(("x", q), tiles["x grouped", q][:].rearrange("p k r j -> p (k r j)"), PASSES * QUARTER, "xq", 2)
 
 
-        def p_pair(h, c, i):
-            for m in (2 * i, 2 * i + 1):
-                acc = bank(("p", h, c, m), [P, HALF])
-                rows = slice(CHUNK * c + P * m, CHUNK * c + P * (m + 1))
+        def p_chunk(q, c):
+            for m in range(MEM):
+                acc = bank(("p", q, c, m // 2), [P, 2, QUARTER])
                 for k in range(PASSES):
-                    nc.tensor.matmul_mx(
-                        out=acc[:],
-                        lhsT=wq[:, k, rows].bitcast(FP8X4),
-                        lhsT_scale=wq_scales[:, k, rows],
-                        rhs=xq[:, h, k, :].bitcast(FP8X4),
-                        rhs_scale=xq_scales[:, h, k, :],
-                        start=(k == 0),
-                        stop=(k == PASSES - 1),
-                    )
+                    tok = slice(QUARTER * k, QUARTER * (k + 1))
+                    matmul(acc[:, m % 2, :], ("w", c, k), member(m), ("x", q), tok, k == 0, k == PASSES - 1)
 
-        def p_pair_out(h, c, i):
-            planes = sbuf(("ps planes", h, c), [P, MEM, HALF], BF16, "planes", 6)
-            affine = sbuf(("1.5 p + b", h, c), [P, MEM, HALF], F32, "eight_kib", 4)
-            for m in (2 * i, 2 * i + 1):
-                acc = tiles["p", h, c, m]
-                nc.scalar.activation(
-                    out=planes[:, m, :], in_=acc[:], func=ACT.Copy, scale=gains[:, 1, c, m : m + 1]
-                )
-                nc.scalar.activation(
-                    out=affine[:, m, :], in_=acc[:], func=ACT.Identity, scale=1.5, bias=gains[:, 2, c, m : m + 1]
-                )
+        def p_out(q, c):
+            planes = sbuf(("ps planes", q, c), [P, MEM, QUARTER], BF16, "ps_planes", 8)
+            affine = sbuf(("1.5 p + b", q, c), [P, MEM, QUARTER], F32, "four_kib", 8)
+            for m in range(MEM):
+                acc = tiles["p", q, c, m // 2][:, m % 2, :]
+                nc.scalar.activation(out=planes[:, m, :], in_=acc, func=ACT.Copy, scale=gain(1, c, m))
+                nc.scalar.activation(out=affine[:, m, :], in_=acc, func=ACT.Identity, scale=1.5, bias=gain(2, c, m))
 
-        def interleave_ps(h, c):
-            grouped = sbuf(("ps grouped", h, c), [P, HALF, MEM], BF16, "planes", 6)
-            nc.vector.tensor_copy(out=grouped[:], in_=tiles["ps planes", h, c][:].rearrange("p m r -> p r m"))
+        def interleave_ps(q, c):
+            grouped = sbuf(("ps grouped", q, c), [P, QUARTER, MEM], BF16, "x_bytes", 8)
+            src = tiles["ps planes", q, c][:].rearrange("p m r -> p r m")
+            if (q, c) in PS_ON_SCALAR:
+                nc.scalar.copy(out=grouped[:], in_=src)
+            else:
+                nc.vector.tensor_copy(out=grouped[:], in_=src)
 
-        def quantise_ps(h, c):
-            tok = slice(HALF * h, HALF * (h + 1))
-            nc.vector.quantize_mx(
-                out=psq[:, c, tok].bitcast(FP8X4),
-                scales=psq_scales[:, c, tok],
-                in_=tiles["ps grouped", h, c][:].rearrange("p r m -> p (r m)"),
-            )
+        def quantise_ps(q, chunks=range(CHUNKS)):
+            for c in chunks:
+                quantise(("ps", q, c), tiles["ps grouped", q, c][:].rearrange("p r m -> p (r m)"), QUARTER)
 
 
-        def r_chunk(q, c):
-            tok = slice(QUARTER * q, QUARTER * (q + 1))
-            for i in range(2):
-                acc = bank(("r", q, c, i), [P, 2, QUARTER])
-                for z in range(2):
-                    m = 2 * i + z
-                    rows = slice(CHUNK * c + P * m, CHUNK * c + P * (m + 1))
-                    for k in range(CHUNKS):
-                        nc.tensor.matmul_mx(
-                            out=acc[:, z, :],
-                            lhsT=gtq[:, k, rows].bitcast(FP8X4),
-                            lhsT_scale=gtq_scales[:, k, rows],
-                            rhs=psq[:, k, tok].bitcast(FP8X4),
-                            rhs_scale=psq_scales[:, k, tok],
-                            start=(k == 0),
-                            stop=(k == CHUNKS - 1),
-                        )
+        def r_chunk(q, n):
+            for m in range(MEM):
+                acc = bank(("r", q, n, m // 2), [P, 2, QUARTER])
+                for c in range(CHUNKS):
+                    tok = slice(0, QUARTER)
+                    matmul(acc[:, m % 2, :], ("gt", c, n), member(m), ("ps", q, c), tok, c == 0, c == CHUNKS - 1)
 
-        def combine(q, c):
-            h_t = sbuf(("h", q, c), [P, MEM, QUARTER], F32, "four_kib", 4)
-            r0 = QUARTER * (q % 2)
+        def combine(q, n):
+            term = sbuf(("h", q, n), [P, MEM, QUARTER], F32, "h", 4)
             for i in range(2):
                 members = slice(2 * i, 2 * i + 2)
-                acc = tiles["r", q, c, i]
-                affine = tiles["1.5 p + b", q // 2, c][:, members, r0 : r0 + QUARTER]
-                if (q, c, i) in GPSIMD_SHARE:
-                    half_r = sbuf(("half r", q, c, i), [P, 2, QUARTER], F32, "x", 2)
+                acc = tiles["r", q, n, i]
+                if q in ADDED_ON_TENSOR:
+                    nc.scalar.activation(out=term[:, members, :], in_=acc[:], func=ACT.Copy, scale=-0.5)
+                elif (q, n) in ADDED_ON_GPSIMD:
+                    half_r = sbuf(("half r", q, n, i), [P, 2, QUARTER], F32, "wd", 2)
                     nc.scalar.activation(out=half_r[:], in_=acc[:], func=ACT.Copy, scale=-0.5)
-                    nc.gpsimd.tensor_tensor(out=h_t[:, members, :], in0=half_r[:], in1=affine, op=ALU.add)
+                    nc.gpsimd.tensor_tensor(
+                        out=term[:, members, :], in0=half_r[:], in1=tiles["1.5 p + b", q, n][:, members, :], op=ALU.add
+                    )
                 else:
                     nc.vector.scalar_tensor_tensor(
-                        out=h_t[:, members, :], in0=acc[:], scalar=-0.5, in1=affine, op0=ALU.mult, op1=ALU.add
+                        out=term[:, members, :],
+                        in0=acc[:],
+                        scalar=-0.5,
+                        in1=tiles["1.5 p + b", q, n][:, members, :],
+                        op0=ALU.mult,
+                        op1=ALU.add,
                     )
 
 
-        def transpose_h(q, i):
-            for c in (1, 0):
-                turned = bank(("h turned", q, i, c), [P, MEM, P])
+        def transpose_h(i):
+            q, tok = i // 2, member(i % 2)
+            for n in (1, 0):
+                turned = bank(("h turned", i, n), [P, MEM, P])
+                terms = (["1.5 p + b"] if q in ADDED_ON_TENSOR else []) + ["h"]
                 for m in range(MEM):
-                    nc.tensor.transpose(turned[:, m, :], tiles["h", q, c][:, m, P * i : P * (i + 1)], ident[:])
+                    for z, term in enumerate(terms):
+                        nc.tensor.matmul(
+                            turned[:, m, :],
+                            lhsT=tiles[term, q, n][:, m, tok],
+                            rhs=ident[:],
+                            start=(z == 0),
+                            stop=(z == len(terms) - 1),
+                            is_transpose=True,
+                        )
 
         def by_channel(turned):
             return turned[:].rearrange("p m (a e) -> p a m e", a=A)
 
-        def copy_right(q, i):
-            right = sbuf(("right", q, i), [P, A, MEM, E], F32, "right", 2)
-            nc.scalar.copy(out=right[:], in_=by_channel(tiles["h turned", q, i, 1]))
+        def copy_right(i):
+            right = sbuf(("right", i), [P, A, MEM, E], F32, "right", 2)
+            nc.scalar.copy(out=right[:], in_=by_channel(tiles["h turned", i, 1]))
 
-        def max_min(q, i):
-            res = sbuf(("result", q, i), [P, 2, A, MEM, E], F32, "planes", 6)
-            tok = slice(QUARTER * q + P * i, QUARTER * q + P * (i + 1))
-            for c, op in enumerate((ALU.max, ALU.min)):
+        def max_min(i):
+            res = sbuf(("result", i), [P, 2, A, MEM, E], F32, "x", 4)
+            for n, op in enumerate((ALU.max, ALU.min)):
                 nc.vector.tensor_tensor(
-                    out=res[:, c], in0=by_channel(tiles["h turned", q, i, 0]), in1=tiles["right", q, i][:], op=op
+                    out=res[:, n], in0=by_channel(tiles["h turned", i, 0]), in1=tiles["right", i][:], op=op
                 )
-                nc.sync.dma_start(
-                    out=out[tok, CHUNK * c : CHUNK * (c + 1)], in_=res[:, c].rearrange("p a m e -> p (a m e)")
-                )
+                if i == N // P - 1:
+                    nc.sync.dma_start(
+                        out=out[P * i : P * (i + 1), CHUNK * n : CHUNK * (n + 1)],
+                        in_=res[:, n].rearrange("p a m e -> p (a m e)"),
+                    )
+            if i < N // P - 1:
+                nc.sync.dma_start(out=out[P * i : P * (i + 1), :], in_=res[:].rearrange("p n a m e -> p (n a m e)"))
 
         ctx.enter_context(tc.manual_schedule())
 
+        load_w(0, 0, parts=2)
+        for k in range(1, PASSES):
+            load_w(0, k)
+        load_gains()
         for k in range(PASSES):
-            load_w(k)
+            load_w(1, k)
         load_x_scale()
-        for i in (0, 1, 2, 4):
+        for i in range(N // P):
             load_x(i)
 
-        interleave_w(0)
-        load_gains()
-        interleave_w(1)
-        make_wd(0)
-        quantise_w(0)
-        quantise_wd(0)
-        make_wd(1)
-        interleave_w(2)
-        turn_gains()
-        g_sweep(0)
-        quantise_wd(1)
-        quantise_w(1)
-        quantise_w(2)
-        make_wd(2)
-        interleave_w(3)
-        g_sweep(1)
-        quantise_wd(2)
-        g_sweep(2)
-        make_wd(3)
-        quantise_w(3)
-        quantise_wd(3)
-        widen_x(0)
-        g_sweep(3)
-        widen_x(1)
+        bank("gains turned", [P, CHUNKS, P], BF16)
+        interleave_w(0, 0)
+        for k in range(PASSES):
+            interleave_w(*((0, k + 1) if k + 1 < PASSES else (1, 0)))
+            quantise_w(0, k)
+            if k == 2:
+                turn_gains()
+            g_sweep(0, 0, k)
+        for k in range(PASSES):
+            if k + 1 < PASSES:
+                interleave_w(1, k + 1)
+            if k == 0:
+                gt_out(0, 0)
+            quantise_w(1, k)
+            g_sweep(0, 1, k)
+            g_sweep(1, 0, k)
 
-        gt_out(0, 0, range(MEM))
-        transpose_x(0)
-        x_out(0)
-        load_x(5)
-        widen_x(2)
-        g_pair(0, 0)
-        transpose_x(1)
-        gt_out(1, 0, range(MEM))
-        load_x(3)
-        widen_x(4)
-        g_pair(1, 0)
-        x_out(1)
-        transpose_x(2)
         interleave_gt(0, 0)
-        x_out(2)
-        load_x(6)
-        widen_x(5)
-        transpose_x(4)
-        gt_pair_out(0, 0)
-        widen_x(3)
-        g_pair(1, 1)
-        transpose_x(5)
-        x_out(4)
-        load_x(7)
-        widen_x(6)
-        transpose_x(3)
-        gt_pair_out(1, 0)
-        x_out(3)
-        gt_pair_out(1, 1)
-        g_pair(0, 1)
-        x_out(5)
-        transpose_x(6)
-        quantise_x(0, 0)
-        quantise_x(0, 1)
-        widen_x(7)
-        x_out(6)
-        interleave_gt(1, 0)
-        gt_pair_out(0, 1)
+        for i in range(4):
+            widen_x(i)
+        gt_out(0, 1)
+        g_block(1, 1, (0, 1))
+        gt_out(1, 0)
+        transpose_x(0)
+        transpose_x(1)
+        x_out(0)
+        x_out(1)
+        quantise_x(0)
+        gt_out(1, 1, (0, 1))
+        g_block(1, 1, (2, 3))
+        gt_out(1, 1, (2, 3))
+        for q in range(3):
+            transpose_x(2 * q + 2)
+            transpose_x(2 * q + 3)
+            x_out(2 * q + 2)
+            x_out(2 * q + 3)
+            if q < 2:
+                widen_x(2 * q + 4)
+                widen_x(2 * q + 5)
+            if q == 2:
+                interleave_gt(1, 0)
+                interleave_gt(1, 1)
+                quantise_gt(1, 0)
+            quantise_x(q + 1)
+            if q == 0:
+                quantise_gt(0, 0)
+                interleave_gt(0, 1)
+            if q == 1:
+                quantise_gt(0, 1)
+            p_chunk(q, 0)
+            p_out(q, 0)
+            p_chunk(q, 1)
+            p_out(q, 1)
 
-        p_pair(0, 0, 0)
-        p_pair(0, 0, 1)
-        p_pair_out(0, 0, 0)
-        interleave_gt(0, 1)
-        interleave_gt(1, 1)
-        transpose_x(7)
-        quantise_gt(1, 0)
-        p_pair(0, 1, 0)
-        x_out(7)
-        quantise_x(1, 1)
-        quantise_x(1, 0)
-        p_pair_out(0, 0, 1)
-        p_pair(0, 1, 1)
         interleave_ps(0, 0)
-        quantise_gt(0, 0)
-        quantise_gt(1, 1)
-        p_pair(1, 0, 0)
-        p_pair_out(0, 1, 0)
-        p_pair(1, 1, 0)
-        quantise_gt(0, 1)
-        p_pair_out(0, 1, 1)
         interleave_ps(0, 1)
-        p_pair(1, 0, 1)
-        quantise_ps(0, 1)
-        p_pair_out(1, 0, 0)
-        p_pair_out(1, 0, 1)
-        quantise_ps(0, 0)
-
-        r_chunk(1, 0)
-        r_chunk(0, 0)
+        quantise_gt(1, 1)
+        quantise_ps(0)
+        p_chunk(3, 0)
+        interleave_ps(2, 0)
+        p_out(3, 0)
         interleave_ps(1, 0)
-        combine(0, 0)
+        interleave_ps(1, 1)
+        r_chunk(0, 0)
         r_chunk(0, 1)
-        quantise_ps(1, 0)
-        p_pair(1, 1, 1)
+        combine(0, 0)
+        quantise_ps(1)
         combine(0, 1)
+        p_chunk(3, 1)
+        p_out(3, 1)
+        interleave_ps(3, 0)
+        interleave_ps(2, 1)
+        r_chunk(1, 0)
         r_chunk(1, 1)
         combine(1, 0)
-        transpose_h(0, 0)
+        quantise_ps(2)
         combine(1, 1)
-        p_pair_out(1, 1, 0)
-        transpose_h(1, 0)
-        p_pair_out(1, 1, 1)
-        transpose_h(0, 1)
-        copy_right(0, 0)
-        interleave_ps(1, 1)
-        quantise_ps(1, 1)
-        copy_right(1, 0)
-        transpose_h(1, 1)
-        max_min(0, 0)
-        copy_right(1, 1)
-
-        r_chunk(2, 0)
-        max_min(1, 0)
-        combine(2, 0)
-        copy_right(0, 1)
-        r_chunk(3, 0)
-        r_chunk(2, 1)
-        max_min(1, 1)
-        r_chunk(3, 1)
-        combine(2, 1)
-        max_min(0, 1)
-        transpose_h(2, 0)
-        combine(3, 0)
-        combine(3, 1)
-        copy_right(2, 0)
-        transpose_h(2, 1)
-        copy_right(2, 1)
-        transpose_h(3, 0)
-        transpose_h(3, 1)
-        max_min(2, 0)
-        copy_right(3, 0)
-        max_min(2, 1)
-        copy_right(3, 1)
-        max_min(3, 0)
-        max_min(3, 1)
+        interleave_ps(3, 1)
+        for q in range(2, 4):
+            transpose_h(2 * q - 4)
+            transpose_h(2 * q - 3)
+            copy_right(2 * q - 4)
+            copy_right(2 * q - 3)
+            max_min(2 * q - 4)
+            if q == 2:
+                quantise_ps(3)
+            max_min(2 * q - 3)
+            r_chunk(q, 0)
+            r_chunk(q, 1)
+            combine(q, 0)
+            combine(q, 1)
+        for i in range(4, 8):
+            transpose_h(i)
+            copy_right(i)
+            max_min(i)

@@ -24,7 +24,7 @@ QUARTERS = N // QUARTER
 BANKS = 8
 FLOPS = 2 * N * D * F + 2 * D * F * F + 2 * N * F * F
 
-VECTOR_BLOCKS = (12, 4, 2, 2, 2, 2, 4, 2)
+VECTOR_BLOCKS = (6, 2, 1, 1, 1, 1, 2, 1)
 ADDED_ON_TENSOR = (3,)
 ADDED_ON_GPSIMD = ()
 GT_ON_SCALAR = ((0, 0),)
@@ -125,10 +125,15 @@ def tile_bjorckmaxmindense_kernel(tc, x_bytes, x_scale, w, d, s, t, b, out):
             grouped = sbuf(("w grouped", c, k), [P, MEM, A, E, 4], BF16, "stage", 4)
             src = tiles["w raw", c, k][:].rearrange("p j (a m e) -> p m a e j", a=A, m=MEM)
             split = VECTOR_BLOCKS[PASSES * c + k]
-            for a0 in range(0, split, A // 2):
-                a1 = min(split, a0 + A // 2)
-                nc.vector.tensor_copy(out=grouped[:, :, a0:a1], in_=src[:, :, a0:a1])
-            nc.scalar.copy(out=grouped[:, :, split:A], in_=src[:, :, split:A])
+            dst4 = grouped[:].rearrange("p m a (h i) j -> p m a h j i", i=4)
+            src4 = src.rearrange("p m a (h i) j -> p m a h j i", i=4)
+            for u in range(split):
+                blocks = slice(A // 2 * (u // MEM), A // 2 * (u // MEM + 1))
+                nc.vector.tensor_copy(out=dst4[:, u % MEM, blocks], in_=src4[:, u % MEM, blocks])
+            for m in range(MEM):
+                first = A // 2 * len(range(m, split, MEM))
+                if first < A:
+                    nc.scalar.copy(out=dst4[:, m, first:A], in_=src4[:, m, first:A])
 
         def quantise_w(c, k):
             grouped = tiles["w grouped", c, k]
@@ -169,11 +174,12 @@ def tile_bjorckmaxmindense_kernel(tc, x_bytes, x_scale, w, d, s, t, b, out):
 
         def interleave_gt(c, n):
             grouped = sbuf(("gt grouped", c, n), [P, CHUNK, MEM], BF16, "stage", 4)
-            src = tiles["gt planes", c, n][:].rearrange("p m f -> p f m")
+            src = tiles["gt planes", c, n][:].rearrange("p m (f i) -> p f m i", i=4)
+            dst = grouped[:].rearrange("p (f i) m -> p f m i", i=4)
             if (c, n) in GT_ON_SCALAR:
-                nc.scalar.copy(out=grouped[:], in_=src)
+                nc.scalar.copy(out=dst, in_=src)
             else:
-                nc.vector.tensor_copy(out=grouped[:], in_=src)
+                nc.vector.tensor_copy(out=dst, in_=src)
 
         def quantise_gt(c, n):
             quantise(("gt", c, n), tiles["gt grouped", c, n][:].rearrange("p f m -> p (f m)"), CHUNK)
@@ -224,11 +230,12 @@ def tile_bjorckmaxmindense_kernel(tc, x_bytes, x_scale, w, d, s, t, b, out):
 
         def interleave_ps(q, c):
             grouped = sbuf(("ps grouped", q, c), [P, QUARTER, MEM], BF16, "x_bytes", 8)
-            src = tiles["ps planes", q, c][:].rearrange("p m r -> p r m")
+            src = tiles["ps planes", q, c][:].rearrange("p m (r i) -> p r m i", i=4)
+            dst = grouped[:].rearrange("p (r i) m -> p r m i", i=4)
             if (q, c) in PS_ON_SCALAR:
-                nc.scalar.copy(out=grouped[:], in_=src)
+                nc.scalar.copy(out=dst, in_=src)
             else:
-                nc.vector.tensor_copy(out=grouped[:], in_=src)
+                nc.vector.tensor_copy(out=dst, in_=src)
 
         def quantise_ps(q, chunks=range(CHUNKS)):
             for c in chunks:

@@ -21,14 +21,10 @@ CHUNKS = F // CHUNK
 A, MEM, E = 16, 4, 8
 QUARTER = 256
 QUARTERS = N // QUARTER
+BLOCKS = N // P
 BANKS = 8
+RUN = 4
 FLOPS = 2 * N * D * F + 2 * D * F * F + 2 * N * F * F
-
-VECTOR_BLOCKS = (6, 2, 1, 1, 1, 1, 2, 1)
-ADDED_ON_TENSOR = (3,)
-ADDED_ON_GPSIMD = ()
-GT_ON_SCALAR = ((0, 0),)
-PS_ON_SCALAR = ((2, 0), (3, 0))
 
 
 def tile_bjorckmaxmindense_kernel(tc, x_bytes, x_scale, w, d, s, t, b, out):
@@ -39,21 +35,25 @@ def tile_bjorckmaxmindense_kernel(tc, x_bytes, x_scale, w, d, s, t, b, out):
         tiles = {}
         taken = {}
 
-        def sbuf(key, shape, dtype, ring=None, slots=1):
+        def sbuf(key, shape, dtype, ring=None, slots=1, slot=None, name=None):
             if key not in tiles:
                 if ring is None:
                     tag = "keep%d" % len(tiles)
-                else:
+                elif slot is None:
                     tag = "%s%d" % (ring, taken.get(ring, 0) % slots)
                     taken[ring] = taken.get(ring, 0) + 1
-                tile = pool.tile(shape, dtype, name=tag, tag=tag, align_bytes=64)
+                else:
+                    tag = "%s%d" % (ring, slot)
+                tile = pool.tile(shape, dtype, name=name or tag, tag=tag, align_bytes=64)
                 tiles[key] = tile
             return tiles[key]
 
-        def bank(key, shape, dtype=F32):
+        def bank(key, shape, dtype=F32, slot=None):
             if key not in tiles:
-                tag = "bank%d" % (taken.get("bank", 0) % BANKS)
-                taken["bank"] = taken.get("bank", 0) + 1
+                if slot is None:
+                    slot = taken.get("bank", 0) % BANKS
+                    taken["bank"] = slot + 1
+                tag = "bank%d" % slot
                 tile = psum.tile(shape, dtype, name=tag, tag=tag)
                 tiles[key] = tile
             return tiles[key]
@@ -90,15 +90,19 @@ def tile_bjorckmaxmindense_kernel(tc, x_bytes, x_scale, w, d, s, t, b, out):
         make_identity(nc, ident[:])
 
 
-        def load_w(c, k, parts=1):
-            raw = sbuf(("w raw", c, k), [P, 4, CHUNK], BF16, "four_kib", 8)
-            rows = w[K_PASS * k : K_PASS * (k + 1), CHUNK * c : CHUNK * (c + 1)].rearrange("(p j) f -> p j f", j=4)
-            for i in range(parts):
-                cols = slice(CHUNK // parts * i, CHUNK // parts * (i + 1))
-                nc.sync.dma_start(out=raw[:, :, cols], in_=rows[:, :, cols])
+        def w_halves(c, k):
+            return 2 if (c, k) == (0, 0) else 1
+
+        def load_w(c, k):
+            halves = w_halves(c, k)
+            raw = sbuf(("w raw", c, k), [P, halves, 4, CHUNK // halves], BF16, "four_kib", slot=PASSES * c + k)
+            rows = w[K_PASS * k : K_PASS * (k + 1), CHUNK * c : CHUNK * (c + 1)]
+            rows = rows.rearrange("(p j) (h f) -> h p j f", j=4, h=halves)
+            for half in range(halves):
+                nc.sync.dma_start(out=raw[:, half], in_=rows[half])
 
         def load_x(i):
-            codes = sbuf(("x bytes", i), [P, D], U8, "x_bytes", 8)
+            codes = sbuf(("x bytes", i), [P, D], U8, "two_kib", slot=i, name="x_bytes%d" % i)
             nc.sync.dma_start(out=codes[:], in_=x_bytes[P * i : P * (i + 1), :])
 
         def load_x_scale():
@@ -106,34 +110,46 @@ def tile_bjorckmaxmindense_kernel(tc, x_bytes, x_scale, w, d, s, t, b, out):
 
         def load_gains():
             for i, v in enumerate((t, s, b)):
-                nc.sync.dma_start(
+                nc.scalar.dma_start(
                     out=gain_rows[MEM * i : MEM * (i + 1)].rearrange("m c (a e) -> m (c a) e", e=E),
                     in_=v.rearrange("(ca m e) -> m ca e", m=MEM, e=E),
                 )
 
         def turn_gains():
-            turned = bank("gains turned", [P, CHUNKS, P], BF16)
+            turned = bank("gains turned", [P, CHUNKS, P], BF16, BANKS - 1)
             for c in range(CHUNKS):
                 nc.tensor.transpose(turned[:, c, :], gain_rows[:, c, :], ident16[:])
-            nc.scalar.copy(out=gains[:].rearrange("p c i m -> p c (i m)"), in_=turned[:, :, 0 : 3 * MEM])
+
+        def gains_out():
+            nc.scalar.copy(out=gains[:].rearrange("p c i m -> p c (i m)"), in_=tiles["gains turned"][:, :, 0 : 3 * MEM])
 
         def gain(i, c, m):
             return gains[:, c, i, m : m + 1]
 
 
-        def interleave_w(c, k):
-            grouped = sbuf(("w grouped", c, k), [P, MEM, A, E, 4], BF16, "stage", 4)
-            src = tiles["w raw", c, k][:].rearrange("p j (a m e) -> p m a e j", a=A, m=MEM)
-            split = VECTOR_BLOCKS[PASSES * c + k]
-            dst4 = grouped[:].rearrange("p m a (h i) j -> p m a h j i", i=4)
-            src4 = src.rearrange("p m a (h i) j -> p m a h j i", i=4)
-            for u in range(split):
-                blocks = slice(A // 2 * (u // MEM), A // 2 * (u // MEM + 1))
-                nc.vector.tensor_copy(out=dst4[:, u % MEM, blocks], in_=src4[:, u % MEM, blocks])
-            for m in range(MEM):
-                first = A // 2 * len(range(m, split, MEM))
-                if first < A:
-                    nc.scalar.copy(out=dst4[:, m, first:A], in_=src4[:, m, first:A])
+        def vector_eighths(c, k):
+            return {(0, 0): 6, (0, 1): 2, (1, 2): 2, (1, 3): 0}.get((c, k), 1)
+
+        def interleave_w(c, k, engine):
+            grouped = sbuf(("w grouped", c, k), [P, MEM, A, E, 4], BF16, "stage", 6)
+            dst = grouped[:].rearrange("p m a (z i) j -> p m a z j i", i=RUN)
+            raw = tiles["w raw", c, k]
+            eighths = vector_eighths(c, k)
+
+            def rows(m, first, last):
+                span = A // w_halves(c, k)
+                src = raw[:, first // span].rearrange("p j (a m z i) -> p m a z j i", m=MEM, z=E // RUN, i=RUN)
+                return src[:, m, first % span : first % span + last - first]
+
+            if engine == "vector":
+                for u in range(eighths):
+                    m, first = u % MEM, A // 2 * (u // MEM)
+                    nc.vector.tensor_copy(out=dst[:, m, first : first + A // 2], in_=rows(m, first, first + A // 2))
+            else:
+                for m in range(MEM):
+                    first = A // 2 * len(range(m, eighths, MEM))
+                    if first < A:
+                        nc.scalar.copy(out=dst[:, m, first:A], in_=rows(m, first, A))
 
         def quantise_w(c, k):
             grouped = tiles["w grouped", c, k]
@@ -148,6 +164,7 @@ def tile_bjorckmaxmindense_kernel(tc, x_bytes, x_scale, w, d, s, t, b, out):
                 op=ALU.mult,
             )
             if not last:
+                interleave_w(*divmod(PASSES * c + k + 1, PASSES), "vector")
                 quantise(("w", c, k), grouped[:].rearrange("p m a e j -> p (m a e j)"), CHUNK)
             quantise(("wd", c, k), wd[:].rearrange("p f j -> p (f j)"), CHUNK)
 
@@ -166,20 +183,22 @@ def tile_bjorckmaxmindense_kernel(tc, x_bytes, x_scale, w, d, s, t, b, out):
                 g_passes(c, n, m, range(PASSES))
 
         def gt_out(c, n, members=range(MEM)):
-            planes = sbuf(("gt planes", c, n), [P, MEM, CHUNK], BF16, "gt_planes", 3)
+            planes = sbuf(("gt planes", c, n), [P, MEM, CHUNK], BF16, "four_kib", slot=PASSES + CHUNKS * c + n)
             for m in members:
                 nc.scalar.activation(
                     out=planes[:, m, :], in_=tiles["g", c, n, m][:], func=ACT.Copy, scale=gain(0, c, m)
                 )
 
-        def interleave_gt(c, n):
-            grouped = sbuf(("gt grouped", c, n), [P, CHUNK, MEM], BF16, "stage", 4)
-            src = tiles["gt planes", c, n][:].rearrange("p m (f i) -> p f m i", i=4)
-            dst = grouped[:].rearrange("p (f i) m -> p f m i", i=4)
-            if (c, n) in GT_ON_SCALAR:
-                nc.scalar.copy(out=dst, in_=src)
-            else:
+        def interleave(dst, src, engine):
+            dst = dst[:].rearrange("p (f i) m -> p f m i", i=RUN)
+            src = src[:].rearrange("p m (f i) -> p f m i", i=RUN)
+            if engine == "vector":
                 nc.vector.tensor_copy(out=dst, in_=src)
+            else:
+                nc.scalar.copy(out=dst, in_=src)
+
+        def interleave_gt(c, n, engine):
+            interleave(sbuf(("gt grouped", c, n), [P, CHUNK, MEM], BF16, "stage", 6), tiles["gt planes", c, n], engine)
 
         def quantise_gt(c, n):
             quantise(("gt", c, n), tiles["gt grouped", c, n][:].rearrange("p f m -> p (f m)"), CHUNK)
@@ -222,46 +241,39 @@ def tile_bjorckmaxmindense_kernel(tc, x_bytes, x_scale, w, d, s, t, b, out):
 
         def p_out(q, c):
             planes = sbuf(("ps planes", q, c), [P, MEM, QUARTER], BF16, "ps_planes", 8)
-            affine = sbuf(("1.5 p + b", q, c), [P, MEM, QUARTER], F32, "four_kib", 8)
+            affine = sbuf(("1.5 p + b", q, c), [P, MEM, QUARTER], F32, "four_kib", slot=CHUNKS * q + c)
             for m in range(MEM):
                 acc = tiles["p", q, c, m // 2][:, m % 2, :]
                 nc.scalar.activation(out=planes[:, m, :], in_=acc, func=ACT.Copy, scale=gain(1, c, m))
                 nc.scalar.activation(out=affine[:, m, :], in_=acc, func=ACT.Identity, scale=1.5, bias=gain(2, c, m))
 
-        def interleave_ps(q, c):
-            grouped = sbuf(("ps grouped", q, c), [P, QUARTER, MEM], BF16, "x_bytes", 8)
-            src = tiles["ps planes", q, c][:].rearrange("p m (r i) -> p r m i", i=4)
-            dst = grouped[:].rearrange("p (r i) m -> p r m i", i=4)
-            if (q, c) in PS_ON_SCALAR:
-                nc.scalar.copy(out=dst, in_=src)
-            else:
-                nc.vector.tensor_copy(out=dst, in_=src)
+        def interleave_ps(q, c, engine):
+            grouped = sbuf(("ps grouped", q, c), [P, QUARTER, MEM], BF16, "two_kib", slot=CHUNKS * q + c)
+            interleave(grouped, tiles["ps planes", q, c], engine)
 
-        def quantise_ps(q, chunks=range(CHUNKS)):
-            for c in chunks:
+        def quantise_ps(q):
+            for c in range(CHUNKS):
                 quantise(("ps", q, c), tiles["ps grouped", q, c][:].rearrange("p r m -> p (r m)"), QUARTER)
 
 
-        def r_chunk(q, n):
-            for m in range(MEM):
-                acc = bank(("r", q, n, m // 2), [P, 2, QUARTER])
-                for c in range(CHUNKS):
-                    tok = slice(0, QUARTER)
-                    matmul(acc[:, m % 2, :], ("gt", c, n), member(m), ("ps", q, c), tok, c == 0, c == CHUNKS - 1)
+        def r_quarter(q):
+            for n in range(CHUNKS):
+                for m in range(MEM):
+                    acc = bank(("r", q, n, m // 2), [P, 2, QUARTER])
+                    for c in range(CHUNKS):
+                        tok = slice(0, QUARTER)
+                        matmul(acc[:, m % 2, :], ("gt", c, n), member(m), ("ps", q, c), tok, c == 0, c == CHUNKS - 1)
+
+        def added_on_tensor(q, n):
+            return (q, n) == (QUARTERS - 1, CHUNKS - 1)
 
         def combine(q, n):
             term = sbuf(("h", q, n), [P, MEM, QUARTER], F32, "h", 4)
             for i in range(2):
                 members = slice(2 * i, 2 * i + 2)
                 acc = tiles["r", q, n, i]
-                if q in ADDED_ON_TENSOR:
+                if added_on_tensor(q, n):
                     nc.scalar.activation(out=term[:, members, :], in_=acc[:], func=ACT.Copy, scale=-0.5)
-                elif (q, n) in ADDED_ON_GPSIMD:
-                    half_r = sbuf(("half r", q, n, i), [P, 2, QUARTER], F32, "wd", 2)
-                    nc.scalar.activation(out=half_r[:], in_=acc[:], func=ACT.Copy, scale=-0.5)
-                    nc.gpsimd.tensor_tensor(
-                        out=term[:, members, :], in0=half_r[:], in1=tiles["1.5 p + b", q, n][:, members, :], op=ALU.add
-                    )
                 else:
                     nc.vector.scalar_tensor_tensor(
                         out=term[:, members, :],
@@ -277,7 +289,7 @@ def tile_bjorckmaxmindense_kernel(tc, x_bytes, x_scale, w, d, s, t, b, out):
             q, tok = i // 2, member(i % 2)
             for n in (1, 0):
                 turned = bank(("h turned", i, n), [P, MEM, P])
-                terms = (["1.5 p + b"] if q in ADDED_ON_TENSOR else []) + ["h"]
+                terms = (["1.5 p + b"] if added_on_tensor(q, n) else []) + ["h"]
                 for m in range(MEM):
                     for z, term in enumerate(terms):
                         nc.tensor.matmul(
@@ -302,118 +314,119 @@ def tile_bjorckmaxmindense_kernel(tc, x_bytes, x_scale, w, d, s, t, b, out):
                 nc.vector.tensor_tensor(
                     out=res[:, n], in0=by_channel(tiles["h turned", i, 0]), in1=tiles["right", i][:], op=op
                 )
-                if i == N // P - 1:
-                    nc.sync.dma_start(
-                        out=out[P * i : P * (i + 1), CHUNK * n : CHUNK * (n + 1)],
-                        in_=res[:, n].rearrange("p a m e -> p (a m e)"),
-                    )
-            if i < N // P - 1:
-                nc.sync.dma_start(out=out[P * i : P * (i + 1), :], in_=res[:].rearrange("p n a m e -> p (n a m e)"))
+                nc.sync.dma_start(
+                    out=out[P * i : P * (i + 1), CHUNK * n : CHUNK * (n + 1)],
+                    in_=res[:, n].rearrange("p a m e -> p (a m e)"),
+                )
+
+
+        def turn_x(q):
+            for i in (2 * q, 2 * q + 1):
+                transpose_x(i)
+            for i in (2 * q, 2 * q + 1):
+                x_out(i)
+
+        def p_and_out(q, c):
+            p_chunk(q, c)
+            p_out(q, c)
+
+        def turn_h(blocks):
+            for i in blocks:
+                transpose_h(i)
+            for i in blocks:
+                copy_right(i)
+
+        def r_with_next_ps(q):
+            for c in range(CHUNKS):
+                interleave_ps(q + 1, c, "vector")
+            r_quarter(q)
+            combine(q, 0)
+            quantise_ps(q + 1)
+            combine(q, 1)
 
         ctx.enter_context(tc.manual_schedule())
 
-        load_w(0, 0, parts=2)
-        for k in range(1, PASSES):
-            load_w(0, k)
         load_gains()
-        for k in range(PASSES):
-            load_w(1, k)
+        for c in range(CHUNKS):
+            for k in range(PASSES):
+                load_w(c, k)
         load_x_scale()
-        for i in range(N // P):
+        for i in range(BLOCKS):
             load_x(i)
 
-        bank("gains turned", [P, CHUNKS, P], BF16)
-        interleave_w(0, 0)
+        turn_gains()
+        interleave_w(0, 0, "vector")
+        interleave_w(0, 0, "scalar")
+        interleave_w(0, 1, "scalar")
         for k in range(PASSES):
-            interleave_w(*((0, k + 1) if k + 1 < PASSES else (1, 0)))
+            interleave_w(*divmod(k + 2, PASSES), "scalar")
             quantise_w(0, k)
-            if k == 2:
-                turn_gains()
             g_sweep(0, 0, k)
+
+        gains_out()
+        gt_out(0, 0)
+        interleave_w(1, 2, "scalar")
+        interleave_w(1, 3, "scalar")
         for k in range(PASSES):
-            if k + 1 < PASSES:
-                interleave_w(1, k + 1)
-            if k == 0:
-                gt_out(0, 0)
             quantise_w(1, k)
             g_sweep(0, 1, k)
             g_sweep(1, 0, k)
+        interleave_gt(0, 0, "scalar")
 
-        interleave_gt(0, 0)
         for i in range(4):
             widen_x(i)
         gt_out(0, 1)
         g_block(1, 1, (0, 1))
         gt_out(1, 0)
-        transpose_x(0)
-        transpose_x(1)
-        x_out(0)
-        x_out(1)
+        turn_x(0)
         quantise_x(0)
         gt_out(1, 1, (0, 1))
         g_block(1, 1, (2, 3))
         gt_out(1, 1, (2, 3))
-        for q in range(3):
-            transpose_x(2 * q + 2)
-            transpose_x(2 * q + 3)
-            x_out(2 * q + 2)
-            x_out(2 * q + 3)
-            if q < 2:
+
+        for q in range(QUARTERS - 1):
+            turn_x(q + 1)
+            if q + 2 < QUARTERS:
                 widen_x(2 * q + 4)
                 widen_x(2 * q + 5)
-            if q == 2:
-                interleave_gt(1, 0)
-                interleave_gt(1, 1)
+            else:
+                interleave_gt(1, 0, "vector")
+                interleave_gt(1, 1, "vector")
                 quantise_gt(1, 0)
+                interleave_ps(0, 0, "vector")
+                interleave_ps(0, 1, "vector")
+                quantise_gt(1, 1)
+                quantise_ps(0)
             quantise_x(q + 1)
+            if q < CHUNKS:
+                quantise_gt(0, q)
             if q == 0:
-                quantise_gt(0, 0)
-                interleave_gt(0, 1)
-            if q == 1:
-                quantise_gt(0, 1)
-            p_chunk(q, 0)
-            p_out(q, 0)
-            p_chunk(q, 1)
-            p_out(q, 1)
+                interleave_gt(0, 1, "vector")
+            p_and_out(q, 0)
+            p_and_out(q, 1)
 
-        interleave_ps(0, 0)
-        interleave_ps(0, 1)
-        quantise_gt(1, 1)
-        quantise_ps(0)
-        p_chunk(3, 0)
-        interleave_ps(2, 0)
-        p_out(3, 0)
-        interleave_ps(1, 0)
-        interleave_ps(1, 1)
-        r_chunk(0, 0)
-        r_chunk(0, 1)
-        combine(0, 0)
-        quantise_ps(1)
-        combine(0, 1)
-        p_chunk(3, 1)
-        p_out(3, 1)
-        interleave_ps(3, 0)
-        interleave_ps(2, 1)
-        r_chunk(1, 0)
-        r_chunk(1, 1)
-        combine(1, 0)
-        quantise_ps(2)
-        combine(1, 1)
-        interleave_ps(3, 1)
-        for q in range(2, 4):
-            transpose_h(2 * q - 4)
-            transpose_h(2 * q - 3)
-            copy_right(2 * q - 4)
-            copy_right(2 * q - 3)
-            max_min(2 * q - 4)
-            if q == 2:
-                quantise_ps(3)
-            max_min(2 * q - 3)
-            r_chunk(q, 0)
-            r_chunk(q, 1)
-            combine(q, 0)
-            combine(q, 1)
-        for i in range(4, 8):
-            transpose_h(i)
-            copy_right(i)
+        last = QUARTERS - 1
+        r_with_next_ps(0)
+        p_and_out(last, 0)
+        r_with_next_ps(1)
+        interleave_ps(last, 0, "scalar")
+        turn_h((0, 1))
+        max_min(0)
+        max_min(1)
+        p_and_out(last, 1)
+        interleave_ps(last, 1, "scalar")
+        r_quarter(2)
+        combine(2, 0)
+        combine(2, 1)
+        quantise_ps(last)
+        turn_h((2, 3))
+        max_min(2)
+        max_min(3)
+        turn_h((4,))
+        r_quarter(last)
+        combine(last, 0)
+        combine(last, 1)
+        max_min(4)
+        for i in range(5, BLOCKS):
+            turn_h((i,))
             max_min(i)

@@ -78,16 +78,20 @@ def tile_bjorckmaxmindense_kernel(tc, x_bytes, x_scale, w, d, s, t, b, out):
             return slice(P * m, P * (m + 1))
 
         x_scale_all = sbuf("x scale", [P, D], F32)
+        d_blocks = sbuf("d blocks", [P, PASSES, E, 4], BF16)
+        gain_blocks = sbuf("gain blocks", [P, 3, CHUNKS, MEM, E], BF16)
         d_sb = sbuf("d", [P, PASSES, 4], BF16)
-        gain_rows = sbuf("gain rows", [P, CHUNKS, A * E], BF16)
-        gains = sbuf("gains", [P, CHUNKS, 3, MEM], F32)
-        ident16 = sbuf("ident16", [P, P], BF16)
+        gains = sbuf("gains", [P, 3, CHUNKS, MEM], F32)
+        padded = [sbuf(("padded identity", z), [P, P + 2 * E], BF16) for z in range(2)]
         ident = sbuf("ident", [P, P], F32)
 
-        nc.vector.memset(gain_rows[:], 0.0)
-        nc.scalar.dma_start(out=d_sb[:], in_=d.rearrange("(k p j) -> p k j", p=P, j=4))
-        make_identity(nc, ident16[:])
+        nc.vector.memset(d_blocks[:], 0.0)
+        nc.vector.memset(gain_blocks[:], 0.0)
+        nc.vector.memset(padded[1][:], 0.0)
+        nc.gpsimd.memset(padded[0][:], 0.0)
+        make_identity(nc, padded[0][:, E : E + P], nomemset=True)
         make_identity(nc, ident[:])
+        nc.vector.tensor_copy(out=padded[1][:, E + 1 : E + 1 + P], in_=padded[0][:, E : E + P])
 
 
         def w_halves(c, k):
@@ -99,6 +103,8 @@ def tile_bjorckmaxmindense_kernel(tc, x_bytes, x_scale, w, d, s, t, b, out):
             rows = w[K_PASS * k : K_PASS * (k + 1), CHUNK * c : CHUNK * (c + 1)]
             rows = rows.rearrange("(p j) (h f) -> h p j f", j=4, h=halves)
             for half in range(halves):
+                if half:
+                    load_d()
                 nc.sync.dma_start(out=raw[:, half], in_=rows[half])
 
         def load_x(i):
@@ -108,23 +114,41 @@ def tile_bjorckmaxmindense_kernel(tc, x_bytes, x_scale, w, d, s, t, b, out):
         def load_x_scale():
             nc.sync.dma_start(out=x_scale_all[:], in_=x_scale.rearrange("o k -> (o k)").partition_broadcast(P))
 
+
+        def load_d():
+            nc.sync.dma_start(
+                out=d_blocks[0:P:E].rearrange("a k e j -> a k (e j)"), in_=d.rearrange("(k a x) -> a k x", a=A, k=PASSES)
+            )
+
         def load_gains():
             for i, v in enumerate((t, s, b)):
-                nc.scalar.dma_start(
-                    out=gain_rows[MEM * i : MEM * (i + 1)].rearrange("m c (a e) -> m (c a) e", e=E),
-                    in_=v.rearrange("(ca m e) -> m ca e", m=MEM, e=E),
+                nc.sync.dma_start(
+                    out=gain_blocks[0:P:E, i].rearrange("a c m e -> a c (m e)"),
+                    in_=v.rearrange("(c a x) -> a c x", a=A, c=CHUNKS),
                 )
 
-        def turn_gains():
-            turned = bank("gains turned", [P, CHUNKS, P], BF16, BANKS - 1)
-            for c in range(CHUNKS):
-                nc.tensor.transpose(turned[:, c, :], gain_rows[:, c, :], ident16[:])
+        def deal_out(acc, values):
+            for e in range(E):
+                first = E + e % 2 - e
+                shift = padded[e % 2][:, first : first + P]
+                nc.tensor.matmul(acc, lhsT=shift, rhs=values(e), start=(e == 0), stop=(e == E - 1))
+
+        def deal_d():
+            dealt = bank("d dealt", [P, PASSES, 4], F32, BANKS - 2)
+            deal_out(dealt[:].rearrange("p k j -> p (k j)"), lambda e: d_blocks[:, :, e, :])
+
+        def d_out():
+            nc.vector.tensor_copy(out=d_sb[:], in_=tiles["d dealt"][:])
+
+        def deal_gains():
+            dealt = bank("gains dealt", [P, 3 * CHUNKS * MEM], F32, BANKS - 1)
+            deal_out(dealt[:], lambda e: gain_blocks[:].rearrange("p i c m e -> p (i c m) e")[:, :, e])
 
         def gains_out():
-            nc.scalar.copy(out=gains[:].rearrange("p c i m -> p c (i m)"), in_=tiles["gains turned"][:, :, 0 : 3 * MEM])
+            nc.scalar.copy(out=gains[:].rearrange("p i c m -> p (i c m)"), in_=tiles["gains dealt"][:])
 
         def gain(i, c, m):
-            return gains[:, c, i, m : m + 1]
+            return gains[:, i, c, m : m + 1]
 
 
         def vector_eighths(c, k):
@@ -152,9 +176,10 @@ def tile_bjorckmaxmindense_kernel(tc, x_bytes, x_scale, w, d, s, t, b, out):
                         nc.scalar.copy(out=dst[:, m, first:A], in_=rows(m, first, A))
 
         def quantise_w(c, k):
+            piece = PASSES * c + k
             grouped = tiles["w grouped", c, k]
-            last = (c, k) == (CHUNKS - 1, PASSES - 1)
-            if last:
+            w_first = piece in (0, CHUNKS * PASSES - 1)
+            if w_first:
                 quantise(("w", c, k), grouped[:].rearrange("p m a e j -> p (m a e j)"), CHUNK)
             wd = sbuf(("wd", c, k), [P, CHUNK, 4], BF16, "wd", 2)
             nc.vector.tensor_tensor(
@@ -163,8 +188,9 @@ def tile_bjorckmaxmindense_kernel(tc, x_bytes, x_scale, w, d, s, t, b, out):
                 in1=d_sb[:, k : k + 1, :].to_broadcast([P, CHUNK, 4]),
                 op=ALU.mult,
             )
-            if not last:
-                interleave_w(*divmod(PASSES * c + k + 1, PASSES), "vector")
+            if piece + 1 < CHUNKS * PASSES:
+                interleave_w(*divmod(piece + 1, PASSES), "vector")
+            if not w_first:
                 quantise(("w", c, k), grouped[:].rearrange("p m a e j -> p (m a e j)"), CHUNK)
             quantise(("wd", c, k), wd[:].rearrange("p f j -> p (f j)"), CHUNK)
 
@@ -346,22 +372,26 @@ def tile_bjorckmaxmindense_kernel(tc, x_bytes, x_scale, w, d, s, t, b, out):
 
         ctx.enter_context(tc.manual_schedule())
 
+        for k in range(PASSES):
+            load_w(0, k)
         load_gains()
-        for c in range(CHUNKS):
-            for k in range(PASSES):
-                load_w(c, k)
+        for k in range(PASSES):
+            load_w(1, k)
         load_x_scale()
         for i in range(BLOCKS):
             load_x(i)
 
-        turn_gains()
+        deal_d()
         interleave_w(0, 0, "vector")
+        d_out()
         interleave_w(0, 0, "scalar")
         interleave_w(0, 1, "scalar")
         for k in range(PASSES):
             interleave_w(*divmod(k + 2, PASSES), "scalar")
             quantise_w(0, k)
             g_sweep(0, 0, k)
+            if k == 0:
+                deal_gains()
 
         gains_out()
         gt_out(0, 0)

@@ -290,15 +290,15 @@ def tile_bjorckmaxmindense_kernel(tc, x_bytes, x_scale, w, d, s, t, b, out):
                         tok = slice(0, QUARTER)
                         matmul(acc[:, m % 2, :], ("gt", c, n), member(m), ("ps", q, c), tok, c == 0, c == CHUNKS - 1)
 
-        def added_on_tensor(q, n):
-            return (q, n) == (QUARTERS - 1, CHUNKS - 1)
+        def added_on_tensor(q):
+            return q == QUARTERS - 1
 
         def combine(q, n):
             term = sbuf(("h", q, n), [P, MEM, QUARTER], F32, "h", 4)
             for i in range(2):
                 members = slice(2 * i, 2 * i + 2)
                 acc = tiles["r", q, n, i]
-                if added_on_tensor(q, n):
+                if added_on_tensor(q):
                     nc.scalar.activation(out=term[:, members, :], in_=acc[:], func=ACT.Copy, scale=-0.5)
                 else:
                     nc.vector.scalar_tensor_tensor(
@@ -315,7 +315,7 @@ def tile_bjorckmaxmindense_kernel(tc, x_bytes, x_scale, w, d, s, t, b, out):
             q, tok = i // 2, member(i % 2)
             for n in (1, 0):
                 turned = bank(("h turned", i, n), [P, MEM, P])
-                terms = (["1.5 p + b"] if added_on_tensor(q, n) else []) + ["h"]
+                terms = (["1.5 p + b"] if added_on_tensor(q) else []) + ["h"]
                 for m in range(MEM):
                     for z, term in enumerate(terms):
                         nc.tensor.matmul(
@@ -331,7 +331,7 @@ def tile_bjorckmaxmindense_kernel(tc, x_bytes, x_scale, w, d, s, t, b, out):
             return turned[:].rearrange("p m (a e) -> p a m e", a=A)
 
         def copy_right(i):
-            right = sbuf(("right", i), [P, A, MEM, E], F32, "right", 2)
+            right = sbuf(("right", i), [P, A, MEM, E], F32, "right", 4)
             nc.scalar.copy(out=right[:], in_=by_channel(tiles["h turned", i, 1]))
 
         def max_min(i):
@@ -362,8 +362,8 @@ def tile_bjorckmaxmindense_kernel(tc, x_bytes, x_scale, w, d, s, t, b, out):
             for i in blocks:
                 copy_right(i)
 
-        def r_with_next_ps(q):
-            for c in range(CHUNKS):
+        def r_with_next_ps(q, chunks):
+            for c in chunks:
                 interleave_ps(q + 1, c, "vector")
             r_quarter(q)
             combine(q, 0)
@@ -436,9 +436,10 @@ def tile_bjorckmaxmindense_kernel(tc, x_bytes, x_scale, w, d, s, t, b, out):
             p_and_out(q, 1)
 
         last = QUARTERS - 1
-        r_with_next_ps(0)
+        r_with_next_ps(0, (0, 1))
+        interleave_ps(2, 0, "scalar")
         p_and_out(last, 0)
-        r_with_next_ps(1)
+        r_with_next_ps(1, (1,))
         interleave_ps(last, 0, "scalar")
         turn_h((0, 1))
         max_min(0)
@@ -453,10 +454,10 @@ def tile_bjorckmaxmindense_kernel(tc, x_bytes, x_scale, w, d, s, t, b, out):
         max_min(2)
         max_min(3)
         turn_h((4,))
+        max_min(4)
         r_quarter(last)
         combine(last, 0)
         combine(last, 1)
-        max_min(4)
         for i in range(5, BLOCKS):
             turn_h((i,))
             max_min(i)

@@ -151,8 +151,11 @@ def tile_bjorckmaxmindense_kernel(tc, x_bytes, x_scale, w, d, s, t, b, out):
             return gains[:, i, c, m : m + 1]
 
 
+        def spread_on_tensor(c, k):
+            return 1 <= PASSES * c + k <= 5
+
         def vector_eighths(c, k):
-            return {(0, 0): 6, (0, 1): 2, (1, 2): 2, (1, 3): 0}.get((c, k), 1)
+            return {(0, 0): 6, (1, 2): 3}.get((c, k), 0)
 
         def interleave_w(c, k, engine):
             grouped = sbuf(("w grouped", c, k), [P, MEM, A, E, 4], BF16, "stage", 6)
@@ -172,27 +175,44 @@ def tile_bjorckmaxmindense_kernel(tc, x_bytes, x_scale, w, d, s, t, b, out):
             else:
                 for m in range(MEM):
                     first = A // 2 * len(range(m, eighths, MEM))
-                    if first < A:
-                        nc.scalar.copy(out=dst[:, m, first:A], in_=rows(m, first, A))
+                    last = A // 2 if spread_on_tensor(c, k) else A
+                    if first < last:
+                        nc.scalar.copy(out=dst[:, m, first:last], in_=rows(m, first, last))
+
+        def spread_w(c, k, half=1):
+            spread = bank(("w spread", c, k, half), [P, CHUNK // 2, 4], BF16, MEM + k % 2)
+            raw = tiles["w raw", c, k]
+            for u in range(2):
+                first = CHUNK // 2 * half + P * u
+                nc.tensor.matmul(
+                    spread[:, P * u : P * (u + 1), :].rearrange("p f j -> p j f"),
+                    lhsT=padded[0][:, E : E + P],
+                    rhs=raw[:, 0, :, first : first + P],
+                    start=True,
+                    stop=True,
+                )
+
+        def spread_out(c, k, half=1):
+            grouped = sbuf(("w grouped", c, k), [P, MEM, A, E, 4], BF16, "stage", 6)
+            nc.scalar.copy(
+                out=grouped[:, :, A // 2 * half : A // 2 * (half + 1)].rearrange("p m a e j -> p m a (e j)"),
+                in_=tiles["w spread", c, k, half][:].rearrange("p (a m e) j -> p m a (e j)", m=MEM, e=E),
+            )
 
         def quantise_w(c, k):
-            piece = PASSES * c + k
-            grouped = tiles["w grouped", c, k]
-            w_first = piece in (0, CHUNKS * PASSES - 1)
-            if w_first:
-                quantise(("w", c, k), grouped[:].rearrange("p m a e j -> p (m a e j)"), CHUNK)
+            quantise(("w", c, k), tiles["w grouped", c, k][:].rearrange("p m a e j -> p (m a e j)"), CHUNK)
+
+        def scale_w(c, k):
             wd = sbuf(("wd", c, k), [P, CHUNK, 4], BF16, "wd", 2)
             nc.vector.tensor_tensor(
                 out=wd[:],
-                in0=grouped[:].rearrange("p m a e j -> p (m a e) j"),
+                in0=tiles["w grouped", c, k][:].rearrange("p m a e j -> p (m a e) j"),
                 in1=d_sb[:, k : k + 1, :].to_broadcast([P, CHUNK, 4]),
                 op=ALU.mult,
             )
-            if piece + 1 < CHUNKS * PASSES:
-                interleave_w(*divmod(piece + 1, PASSES), "vector")
-            if not w_first:
-                quantise(("w", c, k), grouped[:].rearrange("p m a e j -> p (m a e j)"), CHUNK)
-            quantise(("wd", c, k), wd[:].rearrange("p f j -> p (f j)"), CHUNK)
+
+        def quantise_wd(c, k):
+            quantise(("wd", c, k), tiles["wd", c, k][:].rearrange("p f j -> p (f j)"), CHUNK)
 
 
         def g_passes(c, n, m, passes):
@@ -385,20 +405,42 @@ def tile_bjorckmaxmindense_kernel(tc, x_bytes, x_scale, w, d, s, t, b, out):
         interleave_w(0, 0, "vector")
         d_out()
         interleave_w(0, 0, "scalar")
-        interleave_w(0, 1, "scalar")
+
+        def prepare(piece):
+            c, k = divmod(piece, PASSES)
+            if spread_on_tensor(c, k):
+                spread_w(c, k)
+            interleave_w(c, k, "scalar")
+            if spread_on_tensor(c, k):
+                spread_out(c, k)
+
+        def vector_piece(piece):
+            c, k = divmod(piece, PASSES)
+            w_first = piece in (0, CHUNKS * PASSES - 1)
+            if w_first:
+                quantise_w(c, k)
+            scale_w(c, k)
+            if piece + 1 < CHUNKS * PASSES:
+                interleave_w(*divmod(piece + 1, PASSES), "vector")
+            if not w_first:
+                quantise_w(c, k)
+            quantise_wd(c, k)
+
+        prepare(1)
+        prepare(2)
         for k in range(PASSES):
-            interleave_w(*divmod(k + 2, PASSES), "scalar")
-            quantise_w(0, k)
+            if k + 3 <= 5:
+                prepare(k + 3)
+            vector_piece(k)
             g_sweep(0, 0, k)
             if k == 0:
                 deal_gains()
-
         gains_out()
+        prepare(6)
         gt_out(0, 0)
-        interleave_w(1, 2, "scalar")
-        interleave_w(1, 3, "scalar")
+        prepare(7)
         for k in range(PASSES):
-            quantise_w(1, k)
+            vector_piece(PASSES + k)
             g_sweep(0, 1, k)
             g_sweep(1, 0, k)
         interleave_gt(0, 0, "scalar")

@@ -77,7 +77,7 @@ def tile_bjorckmaxmindense_kernel(tc, x_bytes, x_scale, w, d, s, t, b, out):
         def member(m):
             return slice(P * m, P * (m + 1))
 
-        x_scale_all = sbuf("x scale", [P, D], F32)
+        x_scale_sb = sbuf("x scale", [P, PASSES, 1, 2, 2], F32)
         d_blocks = sbuf("d blocks", [P, PASSES, E, 4], BF16)
         gain_blocks = sbuf("gain blocks", [P, 3, CHUNKS, MEM, E], BF16)
         d_sb = sbuf("d", [P, PASSES, 4], BF16)
@@ -112,7 +112,10 @@ def tile_bjorckmaxmindense_kernel(tc, x_bytes, x_scale, w, d, s, t, b, out):
             nc.sync.dma_start(out=codes[:], in_=x_bytes[P * i : P * (i + 1), :])
 
         def load_x_scale():
-            nc.sync.dma_start(out=x_scale_all[:], in_=x_scale.rearrange("o k -> (o k)").partition_broadcast(P))
+            nc.sync.dma_start(
+                out=x_scale_sb[:].rearrange("p k o u e -> p k (o u e)"),
+                in_=x_scale.rearrange("o (k p j) -> p (o k) j", p=P, j=4),
+            )
 
 
         def load_d():
@@ -228,54 +231,59 @@ def tile_bjorckmaxmindense_kernel(tc, x_bytes, x_scale, w, d, s, t, b, out):
             for m in members:
                 g_passes(c, n, m, range(PASSES))
 
-        def gt_out(c, n, members=range(MEM)):
+        def gt_out(c, n, members=range(MEM), engine="scalar"):
             planes = sbuf(("gt planes", c, n), [P, MEM, CHUNK], BF16, "four_kib", slot=PASSES + CHUNKS * c + n)
             for m in members:
-                nc.scalar.activation(
-                    out=planes[:, m, :], in_=tiles["g", c, n, m][:], func=ACT.Copy, scale=gain(0, c, m)
-                )
+                acc = tiles["g", c, n, m][:]
+                if engine == "vector":
+                    nc.vector.tensor_scalar(out=planes[:, m, :], in0=acc, scalar1=gain(0, c, m), scalar2=None, op0=ALU.mult)
+                else:
+                    nc.scalar.activation(out=planes[:, m, :], in_=acc, func=ACT.Copy, scale=gain(0, c, m))
 
         def interleave(dst, src, engine):
             dst = dst[:].rearrange("p (f i) m -> p f m i", i=RUN)
             src = src[:].rearrange("p m (f i) -> p f m i", i=RUN)
             if engine == "vector":
                 nc.vector.tensor_copy(out=dst, in_=src)
+            elif engine == "gpsimd":
+                nc.gpsimd.tensor_scalar(out=dst, in0=src, scalar1=1.0, scalar2=0.0, op0=ALU.mult, op1=ALU.add)
             else:
                 nc.scalar.copy(out=dst, in_=src)
 
-        def interleave_gt(c, n, engine):
-            interleave(sbuf(("gt grouped", c, n), [P, CHUNK, MEM], BF16, "stage", 6), tiles["gt planes", c, n], engine)
+        def interleave_gt(c, n, engine, ring="stage", slot=None):
+            grouped = sbuf(("gt grouped", c, n), [P, CHUNK, MEM], BF16, ring, 6, slot)
+            interleave(grouped, tiles["gt planes", c, n], engine)
 
         def quantise_gt(c, n):
             quantise(("gt", c, n), tiles["gt grouped", c, n][:].rearrange("p f m -> p (f m)"), CHUNK)
 
 
         def widen_x(i):
-            x16 = sbuf(("x", i), [P, D], BF16, "x", 4)
-            nc.vector.tensor_tensor(
-                out=x16[:], in0=tiles["x bytes", i][:].bitcast(FP8), in1=x_scale_all[:], op=ALU.mult
-            )
+            x16 = sbuf(("x", i), [P, D], BF16, "x", 6)
+            nc.scalar.copy(out=x16[:], in_=tiles["x bytes", i][:].bitcast(FP8))
 
-        def transpose_x(i):
-            words = tiles["x", i][:].bitcast(F32)
-            for y in range(2):
-                turned = bank(("x turned", i, y), [P, 2, 2, P])
+        def transpose_x(q, passes=range(PASSES)):
+            for k in passes:
+                turned = bank(("x turned", q, k), [P, 2, 2, P])
+                w0 = K_PASS // 2 * k
                 for z in range(2):
-                    w0 = K_PASS // 2 * (2 * y + z)
+                    words = tiles["x", 2 * q + z][:].bitcast(F32)
                     for u in range(2):
-                        nc.tensor.transpose(turned[:, z, u, :], words[:, w0 + u : w0 + K_PASS // 2 : 2], ident[:])
+                        nc.tensor.transpose(turned[:, u, z, :], words[:, w0 + u : w0 + K_PASS // 2 : 2], ident[:])
 
-        def x_out(i):
-            grouped = sbuf(("x grouped", i // 2), [P, PASSES, QUARTER, 4], BF16, "x_grouped", 2)
-            r0 = P * (i % 2)
-            for y in range(2):
-                nc.scalar.copy(
-                    out=grouped[:].bitcast(F32)[:, 2 * y : 2 * y + 2, r0 : r0 + P, :],
-                    in_=tiles["x turned", i, y][:].rearrange("p z u r -> p z r u"),
+        def x_out(q, passes=range(PASSES)):
+            grouped = sbuf(("x grouped", q), [P, PASSES, QUARTER, 2, 2], BF16, "x_grouped", slot=q % 2)
+            for k in passes:
+                pairs = tiles["x turned", q, k][:].rearrange("p u z r -> p u (z r)").bitcast(BF16)
+                nc.vector.tensor_tensor(
+                    out=grouped[:, k],
+                    in0=pairs.rearrange("p u (r e) -> p r u e", e=2),
+                    in1=x_scale_sb[:, k].to_broadcast([P, QUARTER, 2, 2]),
+                    op=ALU.mult,
                 )
 
         def quantise_x(q):
-            quantise(("x", q), tiles["x grouped", q][:].rearrange("p k r j -> p (k r j)"), PASSES * QUARTER, "xq", 2)
+            quantise(("x", q), tiles["x grouped", q][:].rearrange("p k r u e -> p (k r u e)"), PASSES * QUARTER, "xq", 2)
 
 
         def p_chunk(q, c):
@@ -293,32 +301,36 @@ def tile_bjorckmaxmindense_kernel(tc, x_bytes, x_scale, w, d, s, t, b, out):
                 nc.scalar.activation(out=planes[:, m, :], in_=acc, func=ACT.Copy, scale=gain(1, c, m))
                 nc.scalar.activation(out=affine[:, m, :], in_=acc, func=ACT.Identity, scale=1.5, bias=gain(2, c, m))
 
-        def interleave_ps(q, c, engine):
-            grouped = sbuf(("ps grouped", q, c), [P, QUARTER, MEM], BF16, "two_kib", slot=CHUNKS * q + c)
-            interleave(grouped, tiles["ps planes", q, c], engine)
+        def interleave_ps(q, c, engine, ring="stage", slot=None):
+            grouped = sbuf(("ps grouped", q), [P, CHUNKS, QUARTER, MEM], BF16, ring, 6, slot)
+            interleave(grouped[:, c], tiles["ps planes", q, c], engine)
 
         def quantise_ps(q):
             for c in range(CHUNKS):
-                quantise(("ps", q, c), tiles["ps grouped", q, c][:].rearrange("p r m -> p (r m)"), QUARTER)
+                quantise(("ps", q, c), tiles["ps grouped", q][:, c].rearrange("p r m -> p (r m)"), QUARTER)
 
+
+        def r_bank(q, n, i):
+            acc = bank(("r", q, n, i), [P, 2, QUARTER])
+            for m in (2 * i, 2 * i + 1):
+                for c in range(CHUNKS):
+                    tok = slice(0, QUARTER)
+                    matmul(acc[:, m % 2, :], ("gt", c, n), member(m), ("ps", q, c), tok, c == 0, c == CHUNKS - 1)
 
         def r_quarter(q):
             for n in range(CHUNKS):
-                for m in range(MEM):
-                    acc = bank(("r", q, n, m // 2), [P, 2, QUARTER])
-                    for c in range(CHUNKS):
-                        tok = slice(0, QUARTER)
-                        matmul(acc[:, m % 2, :], ("gt", c, n), member(m), ("ps", q, c), tok, c == 0, c == CHUNKS - 1)
+                for i in range(2):
+                    r_bank(q, n, i)
 
-        def added_on_tensor(q):
-            return q == QUARTERS - 1
+        def added_on_tensor(q, n, i):
+            return q == 3
 
-        def combine(q, n):
+        def combine(q, n, pairs=range(2)):
             term = sbuf(("h", q, n), [P, MEM, QUARTER], F32, "h", 4)
-            for i in range(2):
+            for i in pairs:
                 members = slice(2 * i, 2 * i + 2)
                 acc = tiles["r", q, n, i]
-                if added_on_tensor(q):
+                if added_on_tensor(q, n, i):
                     nc.scalar.activation(out=term[:, members, :], in_=acc[:], func=ACT.Copy, scale=-0.5)
                 else:
                     nc.vector.scalar_tensor_tensor(
@@ -331,46 +343,68 @@ def tile_bjorckmaxmindense_kernel(tc, x_bytes, x_scale, w, d, s, t, b, out):
                     )
 
 
+        def turn(turned, q, n, m, tok):
+            terms = (["1.5 p + b"] if added_on_tensor(q, n, m // 2) else []) + ["h"]
+            for z, term in enumerate(terms):
+                nc.tensor.matmul(
+                    turned,
+                    lhsT=tiles[term, q, n][:, m, tok],
+                    rhs=ident[:],
+                    start=(z == 0),
+                    stop=(z == len(terms) - 1),
+                    is_transpose=True,
+                )
+
         def transpose_h(i):
-            q, tok = i // 2, member(i % 2)
             for n in (1, 0):
                 turned = bank(("h turned", i, n), [P, MEM, P])
-                terms = (["1.5 p + b"] if added_on_tensor(q) else []) + ["h"]
                 for m in range(MEM):
-                    for z, term in enumerate(terms):
-                        nc.tensor.matmul(
-                            turned[:, m, :],
-                            lhsT=tiles[term, q, n][:, m, tok],
-                            rhs=ident[:],
-                            start=(z == 0),
-                            stop=(z == len(terms) - 1),
-                            is_transpose=True,
-                        )
+                    turn(turned[:, m, :], i // 2, n, m, member(i % 2))
+
+        def transpose_pair(q, n, i):
+            turned = bank(("pair turned", q, n, i), [P, 2, 2, P])
+            for z in range(2):
+                for m in range(2):
+                    turn(turned[:, z, m, :], q, n, 2 * i + m, member(z))
+
+        def copy_right_pair(q, i):
+            right = sbuf(("right pair", q, i), [P, 2, 2, P], F32, "right", 4)
+            nc.scalar.copy(out=right[:], in_=tiles["pair turned", q, 1, i][:])
+
+        def max_min_pair(q, i):
+            for z in range(2):
+                res = sbuf(("result", 2 * q + z), [P, 2, A, MEM, E], F32, "x", 6)
+                for n, op in enumerate((ALU.max, ALU.min)):
+                    nc.vector.tensor_tensor(
+                        out=res[:, n, :, 2 * i : 2 * i + 2, :],
+                        in0=by_channel(tiles["pair turned", q, 0, i][:, z]),
+                        in1=by_channel(tiles["right pair", q, i][:, z]),
+                        op=op,
+                    )
+                    if i == 1:
+                        store(2 * q + z, n)
+
+        def store(i, n):
+            nc.sync.dma_start(
+                out=out[P * i : P * (i + 1), CHUNK * n : CHUNK * (n + 1)],
+                in_=tiles["result", i][:, n].rearrange("p a m e -> p (a m e)"),
+            )
 
         def by_channel(turned):
-            return turned[:].rearrange("p m (a e) -> p a m e", a=A)
+            return turned.rearrange("p m (a e) -> p a m e", a=A)
 
         def copy_right(i):
             right = sbuf(("right", i), [P, A, MEM, E], F32, "right", 4)
-            nc.scalar.copy(out=right[:], in_=by_channel(tiles["h turned", i, 1]))
+            nc.scalar.copy(out=right[:], in_=by_channel(tiles["h turned", i, 1][:]))
 
         def max_min(i):
-            res = sbuf(("result", i), [P, 2, A, MEM, E], F32, "x", 4)
+            res = sbuf(("result", i), [P, 2, A, MEM, E], F32, "x", 6)
             for n, op in enumerate((ALU.max, ALU.min)):
                 nc.vector.tensor_tensor(
-                    out=res[:, n], in0=by_channel(tiles["h turned", i, 0]), in1=tiles["right", i][:], op=op
+                    out=res[:, n], in0=by_channel(tiles["h turned", i, 0][:]), in1=tiles["right", i][:], op=op
                 )
-                nc.sync.dma_start(
-                    out=out[P * i : P * (i + 1), CHUNK * n : CHUNK * (n + 1)],
-                    in_=res[:, n].rearrange("p a m e -> p (a m e)"),
-                )
+                store(i, n)
 
-
-        def turn_x(q):
-            for i in (2 * q, 2 * q + 1):
-                transpose_x(i)
-            for i in (2 * q, 2 * q + 1):
-                x_out(i)
 
         def p_and_out(q, c):
             p_chunk(q, c)
@@ -381,14 +415,6 @@ def tile_bjorckmaxmindense_kernel(tc, x_bytes, x_scale, w, d, s, t, b, out):
                 transpose_h(i)
             for i in blocks:
                 copy_right(i)
-
-        def r_with_next_ps(q, chunks):
-            for c in chunks:
-                interleave_ps(q + 1, c, "vector")
-            r_quarter(q)
-            combine(q, 0)
-            quantise_ps(q + 1)
-            combine(q, 1)
 
         ctx.enter_context(tc.manual_schedule())
 
@@ -443,45 +469,63 @@ def tile_bjorckmaxmindense_kernel(tc, x_bytes, x_scale, w, d, s, t, b, out):
             vector_piece(PASSES + k)
             g_sweep(0, 1, k)
             g_sweep(1, 0, k)
-        interleave_gt(0, 0, "scalar")
-
-        for i in range(4):
-            widen_x(i)
+        widen_x(0)
+        widen_x(1)
+        interleave_gt(0, 0, "vector")
+        widen_x(2)
         gt_out(0, 1)
-        g_block(1, 1, (0, 1))
-        gt_out(1, 0)
-        turn_x(0)
+        gt_out(1, 0, (0, 1), engine="vector")
+        quantise_gt(0, 0)
+        widen_x(3)
+        transpose_x(0)
+        gt_out(1, 0, (2, 3))
+        g_block(1, 1, range(MEM))
+        x_out(0)
+        interleave_gt(0, 1, "scalar")
+        gt_out(1, 1)
+        quantise_gt(0, 1)
         quantise_x(0)
-        gt_out(1, 1, (0, 1))
-        g_block(1, 1, (2, 3))
-        gt_out(1, 1, (2, 3))
-
-        for q in range(QUARTERS - 1):
-            turn_x(q + 1)
-            if q + 2 < QUARTERS:
-                widen_x(2 * q + 4)
-                widen_x(2 * q + 5)
-            else:
-                interleave_gt(1, 0, "vector")
-                interleave_gt(1, 1, "vector")
-                quantise_gt(1, 0)
-                interleave_ps(0, 0, "vector")
-                interleave_ps(0, 1, "vector")
-                quantise_gt(1, 1)
-                quantise_ps(0)
-            quantise_x(q + 1)
-            if q < CHUNKS:
-                quantise_gt(0, q)
-            if q == 0:
-                interleave_gt(0, 1, "vector")
-            p_and_out(q, 0)
-            p_and_out(q, 1)
+        transpose_x(1)
+        widen_x(4)
+        widen_x(5)
+        x_out(1)
+        p_and_out(0, 0)
+        p_and_out(0, 1)
+        interleave_gt(1, 0, "vector")
+        quantise_x(1)
+        transpose_x(2)
+        widen_x(6)
+        widen_x(7)
+        x_out(2)
+        p_and_out(1, 0)
+        p_and_out(1, 1)
+        quantise_gt(1, 0)
+        quantise_x(2)
+        transpose_x(3)
+        interleave_gt(1, 1, "vector")
+        interleave_ps(0, 0, "scalar")
+        interleave_ps(0, 1, "scalar")
+        x_out(3)
+        p_and_out(2, 0)
+        p_and_out(2, 1)
+        quantise_gt(1, 1)
+        quantise_ps(0)
+        quantise_x(3)
 
         last = QUARTERS - 1
-        r_with_next_ps(0, (0, 1))
+        interleave_ps(1, 0, "vector")
+        interleave_ps(1, 1, "vector")
+        r_quarter(0)
+        combine(0, 0)
+        quantise_ps(1)
+        combine(0, 1)
         interleave_ps(2, 0, "scalar")
         p_and_out(last, 0)
-        r_with_next_ps(1, (1,))
+        interleave_ps(2, 1, "vector")
+        r_quarter(1)
+        combine(1, 0)
+        quantise_ps(2)
+        combine(1, 1)
         interleave_ps(last, 0, "scalar")
         turn_h((0, 1))
         max_min(0)

@@ -241,12 +241,14 @@ def tile_bjorckmaxmindense_kernel(tc, x_bytes, x_scale, w, d, s, t, b, out):
                     nc.scalar.activation(out=planes[:, m, :], in_=acc, func=ACT.Copy, scale=gain(0, c, m))
 
         def interleave(dst, src, engine):
+            if engine == "gpsimd":
+                src = src[:].rearrange("p m f -> p f m")
+                nc.gpsimd.tensor_scalar(out=dst[:], in0=src, scalar1=1.0, scalar2=0.0, op0=ALU.mult, op1=ALU.add)
+                return
             dst = dst[:].rearrange("p (f i) m -> p f m i", i=RUN)
             src = src[:].rearrange("p m (f i) -> p f m i", i=RUN)
             if engine == "vector":
                 nc.vector.tensor_copy(out=dst, in_=src)
-            elif engine == "gpsimd":
-                nc.gpsimd.tensor_scalar(out=dst, in0=src, scalar1=1.0, scalar2=0.0, op0=ALU.mult, op1=ALU.add)
             else:
                 nc.scalar.copy(out=dst, in_=src)
 
@@ -262,14 +264,25 @@ def tile_bjorckmaxmindense_kernel(tc, x_bytes, x_scale, w, d, s, t, b, out):
             x16 = sbuf(("x", i), [P, D], BF16, "x", 6)
             nc.scalar.copy(out=x16[:], in_=tiles["x bytes", i][:].bitcast(FP8))
 
+        def split(i):
+            return i >= 4
+
+        def split_x(i):
+            halves = sbuf(("x split", i), [P, 2, D // 4], F32, "x", 6)
+            nc.scalar.copy(out=halves[:], in_=tiles["x", i][:].bitcast(F32).rearrange("p (w u) -> p u w", u=2))
+
         def transpose_x(q, passes=range(PASSES)):
             for k in passes:
                 turned = bank(("x turned", q, k), [P, 2, 2, P])
                 w0 = K_PASS // 2 * k
                 for z in range(2):
-                    words = tiles["x", 2 * q + z][:].bitcast(F32)
+                    i = 2 * q + z
                     for u in range(2):
-                        nc.tensor.transpose(turned[:, u, z, :], words[:, w0 + u : w0 + K_PASS // 2 : 2], ident[:])
+                        if split(i):
+                            pairs = tiles["x split", i][:, u, P * k : P * (k + 1)]
+                        else:
+                            pairs = tiles["x", i][:].bitcast(F32)[:, w0 + u : w0 + K_PASS // 2 : 2]
+                        nc.tensor.transpose(turned[:, u, z, :], pairs, ident[:])
 
         def x_out(q, passes=range(PASSES)):
             grouped = sbuf(("x grouped", q), [P, PASSES, QUARTER, 2, 2], BF16, "x_grouped", slot=q % 2)
@@ -474,41 +487,45 @@ def tile_bjorckmaxmindense_kernel(tc, x_bytes, x_scale, w, d, s, t, b, out):
         interleave_gt(0, 0, "vector")
         widen_x(2)
         gt_out(0, 1)
+        interleave_gt(0, 1, "gpsimd")
         gt_out(1, 0, (0, 1), engine="vector")
-        quantise_gt(0, 0)
         widen_x(3)
         transpose_x(0)
         gt_out(1, 0, (2, 3))
         g_block(1, 1, range(MEM))
         x_out(0)
-        interleave_gt(0, 1, "scalar")
-        gt_out(1, 1)
-        quantise_gt(0, 1)
-        quantise_x(0)
-        transpose_x(1)
         widen_x(4)
         widen_x(5)
+        gt_out(1, 1)
+        quantise_gt(0, 0)
+        quantise_x(0)
+        transpose_x(1)
+        interleave_gt(1, 0, "gpsimd", "x_grouped", 0)
+        split_x(4)
+        split_x(5)
+        widen_x(6)
         x_out(1)
         p_and_out(0, 0)
         p_and_out(0, 1)
-        interleave_gt(1, 0, "vector")
+        quantise_gt(0, 1)
+        quantise_gt(1, 0)
         quantise_x(1)
         transpose_x(2)
-        widen_x(6)
+        interleave_gt(1, 1, "gpsimd", "x_grouped", 1)
         widen_x(7)
+        split_x(6)
+        split_x(7)
         x_out(2)
         p_and_out(1, 0)
         p_and_out(1, 1)
-        quantise_gt(1, 0)
+        quantise_gt(1, 1)
         quantise_x(2)
         transpose_x(3)
-        interleave_gt(1, 1, "vector")
-        interleave_ps(0, 0, "scalar")
-        interleave_ps(0, 1, "scalar")
+        interleave_ps(0, 0, "gpsimd", "x_grouped", 0)
+        interleave_ps(0, 1, "gpsimd", "x_grouped", 0)
         x_out(3)
         p_and_out(2, 0)
         p_and_out(2, 1)
-        quantise_gt(1, 1)
         quantise_ps(0)
         quantise_x(3)
 

@@ -58,10 +58,10 @@ def tile_bjorckmaxmindense_kernel(tc, x_bytes, x_scale, w, d, s, t, b, out):
                 tiles[key] = tile
             return tiles[key]
 
-        def quantise(key, src, width, ring=None, slots=1):
+        def quantise(key, src, width, ring=None, slots=1, cols=slice(None)):
             codes = sbuf((key, "codes"), [P, width], U32, ring and ring + "_codes", slots)
             scales = sbuf((key, "scales"), [P, width], U8, ring and ring + "_scales", slots)
-            nc.vector.quantize_mx(out=codes[:].bitcast(FP8X4), scales=scales[:], in_=src)
+            nc.vector.quantize_mx(out=codes[:, cols].bitcast(FP8X4), scales=scales[:, cols], in_=src)
 
         def matmul(acc, left, left_cols, right, right_cols, start, stop):
             nc.tensor.matmul_mx(
@@ -80,7 +80,7 @@ def tile_bjorckmaxmindense_kernel(tc, x_bytes, x_scale, w, d, s, t, b, out):
         x_scale_sb = sbuf("x scale", [P, PASSES, 1, 2, 2], F32)
         d_blocks = sbuf("d blocks", [P, PASSES, E, 4], BF16)
         gain_blocks = sbuf("gain blocks", [P, 3, CHUNKS, MEM, E], BF16)
-        d_sb = sbuf("d", [P, PASSES, 4], BF16)
+        d_sb = sbuf("d", [P, PASSES, 1, 4], BF16)
         gains = sbuf("gains", [P, 3, CHUNKS, MEM], F32)
         padded = [sbuf(("padded identity", z), [P, P + 2 * E], BF16) for z in range(2)]
         ident = sbuf("ident", [P, P], F32)
@@ -141,7 +141,7 @@ def tile_bjorckmaxmindense_kernel(tc, x_bytes, x_scale, w, d, s, t, b, out):
             deal_out(dealt[:].rearrange("p k j -> p (k j)"), lambda e: d_blocks[:, :, e, :])
 
         def d_out():
-            nc.vector.tensor_copy(out=d_sb[:], in_=tiles["d dealt"][:])
+            nc.vector.tensor_copy(out=d_sb[:, :, 0], in_=tiles["d dealt"][:])
 
         def deal_gains():
             dealt = bank("gains dealt", [P, 3 * CHUNKS * MEM], F32, BANKS - 1)
@@ -155,12 +155,12 @@ def tile_bjorckmaxmindense_kernel(tc, x_bytes, x_scale, w, d, s, t, b, out):
 
 
         def spread_on_tensor(c, k):
-            return 1 <= PASSES * c + k <= 5
+            return PASSES * c + k in (1, 2, 3, 4)
 
         def vector_eighths(c, k):
-            return {(0, 0): 6, (1, 2): 3}.get((c, k), 0)
+            return {(0, 0): 6, (0, 1): 2, (1, 2): 2}.get((c, k), 0)
 
-        def interleave_w(c, k, engine):
+        def interleave_w(c, k, engine, members=range(MEM)):
             grouped = sbuf(("w grouped", c, k), [P, MEM, A, E, 4], BF16, "stage", 6)
             dst = grouped[:].rearrange("p m a (z i) j -> p m a z j i", i=RUN)
             raw = tiles["w raw", c, k]
@@ -173,49 +173,55 @@ def tile_bjorckmaxmindense_kernel(tc, x_bytes, x_scale, w, d, s, t, b, out):
 
             if engine == "vector":
                 for u in range(eighths):
+                    if (c, k, u) == (0, 0, MEM):
+                        d_out()
                     m, first = u % MEM, A // 2 * (u // MEM)
                     nc.vector.tensor_copy(out=dst[:, m, first : first + A // 2], in_=rows(m, first, first + A // 2))
             else:
-                for m in range(MEM):
+                for m in members:
                     first = A // 2 * len(range(m, eighths, MEM))
                     last = A // 2 if spread_on_tensor(c, k) else A
                     if first < last:
                         nc.scalar.copy(out=dst[:, m, first:last], in_=rows(m, first, last))
 
-        def spread_w(c, k, half=1):
-            spread = bank(("w spread", c, k, half), [P, CHUNK // 2, 4], BF16, MEM + k % 2)
+        def spread_w(c, k):
             raw = tiles["w raw", c, k]
             for u in range(2):
-                first = CHUNK // 2 * half + P * u
+                spread = bank(("w spread", c, k, u), [P, P, 4], BF16, MEM + (2 * k + u) % MEM)
+                first = CHUNK // 2 + P * u
                 nc.tensor.matmul(
-                    spread[:, P * u : P * (u + 1), :].rearrange("p f j -> p j f"),
+                    spread[:].rearrange("p f j -> p j f"),
                     lhsT=padded[0][:, E : E + P],
                     rhs=raw[:, 0, :, first : first + P],
                     start=True,
                     stop=True,
                 )
 
-        def spread_out(c, k, half=1):
-            grouped = sbuf(("w grouped", c, k), [P, MEM, A, E, 4], BF16, "stage", 6)
-            nc.scalar.copy(
-                out=grouped[:, :, A // 2 * half : A // 2 * (half + 1)].rearrange("p m a e j -> p m a (e j)"),
-                in_=tiles["w spread", c, k, half][:].rearrange("p (a m e) j -> p m a (e j)", m=MEM, e=E),
-            )
+        def spread_out(c, k):
+            grouped = tiles["w grouped", c, k]
+            for u in range(2):
+                first = A // 2 + A // 4 * u
+                nc.scalar.copy(
+                    out=grouped[:, :, first : first + A // 4].rearrange("p m a e j -> p m a (e j)"),
+                    in_=tiles["w spread", c, k, u][:].rearrange("p (a m e) j -> p m a (e j)", m=MEM, e=E),
+                )
 
         def quantise_w(c, k):
             quantise(("w", c, k), tiles["w grouped", c, k][:].rearrange("p m a e j -> p (m a e j)"), CHUNK)
 
-        def scale_w(c, k):
-            wd = sbuf(("wd", c, k), [P, CHUNK, 4], BF16, "wd", 2)
+        def scale_w(c, k, members=slice(0, MEM), blocks=slice(0, A)):
+            wd = sbuf(("wd", c, k), [P, MEM, A, E, 4], BF16, "wd", slot=k % 2)
+            src = tiles["w grouped", c, k][:, members, blocks].rearrange("p m a e j -> p m (a e) j")
             nc.vector.tensor_tensor(
-                out=wd[:],
-                in0=tiles["w grouped", c, k][:].rearrange("p m a e j -> p (m a e) j"),
-                in1=d_sb[:, k : k + 1, :].to_broadcast([P, CHUNK, 4]),
+                out=wd[:, members, blocks].rearrange("p m a e j -> p m (a e) j"),
+                in0=src,
+                in1=d_sb[:, k : k + 1].to_broadcast(list(src.shape)),
                 op=ALU.mult,
             )
 
-        def quantise_wd(c, k):
-            quantise(("wd", c, k), tiles["wd", c, k][:].rearrange("p f j -> p (f j)"), CHUNK)
+        def quantise_wd(c, k, members=slice(0, MEM)):
+            src = tiles["wd", c, k][:, members].rearrange("p m a e j -> p (m a e j)")
+            quantise(("wd", c, k), src, CHUNK, cols=slice(P * members.start, P * members.stop))
 
 
         def g_passes(c, n, m, passes):
@@ -442,7 +448,6 @@ def tile_bjorckmaxmindense_kernel(tc, x_bytes, x_scale, w, d, s, t, b, out):
 
         deal_d()
         interleave_w(0, 0, "vector")
-        d_out()
         interleave_w(0, 0, "scalar")
 
         def prepare(piece):
@@ -453,45 +458,47 @@ def tile_bjorckmaxmindense_kernel(tc, x_bytes, x_scale, w, d, s, t, b, out):
             if spread_on_tensor(c, k):
                 spread_out(c, k)
 
-        def vector_piece(piece):
-            c, k = divmod(piece, PASSES)
-            w_first = piece in (0, CHUNKS * PASSES - 1)
-            if w_first:
-                quantise_w(c, k)
-            scale_w(c, k)
-            if piece + 1 < CHUNKS * PASSES:
-                interleave_w(*divmod(piece + 1, PASSES), "vector")
-            if not w_first:
-                quantise_w(c, k)
-            quantise_wd(c, k)
-
         prepare(1)
-        prepare(2)
-        for k in range(PASSES):
-            if k + 3 <= 5:
-                prepare(k + 3)
-            vector_piece(k)
+        scale_w(0, 0, blocks=slice(0, A // 2))
+        scale_w(0, 0, blocks=slice(A // 2, A))
+        interleave_w(0, 1, "vector")
+        quantise_w(0, 0)
+        quantise_wd(0, 0)
+        for piece in range(2, 6):
+            prepare(piece)
+        g_sweep(0, 0, 0)
+        deal_gains()
+        for k in range(1, PASSES):
+            scale_w(0, k)
+            quantise_w(0, k)
+            quantise_wd(0, k)
             g_sweep(0, 0, k)
-            if k == 0:
-                deal_gains()
         gains_out()
-        prepare(6)
+        interleave_w(1, 2, "scalar", range(2))
         gt_out(0, 0)
+        interleave_w(1, 2, "scalar", range(2, MEM))
         prepare(7)
         for k in range(PASSES):
-            vector_piece(PASSES + k)
+            quantise_w(1, k)
+            for i in range(2):
+                scale_w(1, k, slice(2 * i, 2 * i + 2))
+            if k + 1 < PASSES:
+                interleave_w(1, k + 1, "vector")
+            for i in range(2):
+                quantise_wd(1, k, slice(2 * i, 2 * i + 2))
             g_sweep(0, 1, k)
             g_sweep(1, 0, k)
         widen_x(0)
         widen_x(1)
-        interleave_gt(0, 0, "vector")
+        interleave_gt(0, 0, "gpsimd", "wd", 1)
         widen_x(2)
-        gt_out(0, 1)
+        gt_out(0, 1, (0, 1))
+        gt_out(0, 1, (2, 3), engine="vector")
         interleave_gt(0, 1, "gpsimd")
-        gt_out(1, 0, (0, 1), engine="vector")
         widen_x(3)
-        transpose_x(0)
         gt_out(1, 0, (2, 3))
+        gt_out(1, 0, (0, 1), engine="vector")
+        transpose_x(0)
         g_block(1, 1, range(MEM))
         x_out(0)
         widen_x(4)

@@ -23,6 +23,8 @@ QUARTER = 256
 QUARTERS = N // QUARTER
 BLOCKS = N // P
 BANKS = 8
+STAGES = 6
+X_BUFFERS = 6
 RUN = 4
 FLOPS = 2 * N * D * F + 2 * D * F * F + 2 * N * F * F
 
@@ -144,7 +146,7 @@ def tile_bjorckmaxmindense_kernel(tc, x_bytes, x_scale, w, d, s, t, b, out):
             nc.vector.tensor_copy(out=d_sb[:, :, 0], in_=tiles["d dealt"][:])
 
         def deal_gains():
-            dealt = bank("gains dealt", [P, 3 * CHUNKS * MEM], F32, BANKS - 1)
+            dealt = bank("gains dealt", [P, 3 * CHUNKS * MEM], F32, MEM - 1)
             deal_out(dealt[:], lambda e: gain_blocks[:].rearrange("p i c m e -> p (i c m) e")[:, :, e])
 
         def gains_out():
@@ -155,13 +157,13 @@ def tile_bjorckmaxmindense_kernel(tc, x_bytes, x_scale, w, d, s, t, b, out):
 
 
         def spread_on_tensor(c, k):
-            return PASSES * c + k in (1, 2, 3, 4)
+            return 1 <= PASSES * c + k <= 5
 
         def vector_eighths(c, k):
-            return {(0, 0): 6, (0, 1): 2, (1, 2): 2}.get((c, k), 0)
+            return {(0, 0): 6, (0, 1): 1, (1, 2): 2}.get((c, k), 0)
 
         def interleave_w(c, k, engine, members=range(MEM)):
-            grouped = sbuf(("w grouped", c, k), [P, MEM, A, E, 4], BF16, "stage", 6)
+            grouped = sbuf(("w grouped", c, k), [P, MEM, A, E, 4], BF16, "stage", STAGES)
             dst = grouped[:].rearrange("p m a (z i) j -> p m a z j i", i=RUN)
             raw = tiles["w raw", c, k]
             eighths = vector_eighths(c, k)
@@ -233,8 +235,8 @@ def tile_bjorckmaxmindense_kernel(tc, x_bytes, x_scale, w, d, s, t, b, out):
             for m in range(MEM):
                 g_passes(c, n, m, (k,))
 
-        def g_block(c, n, members):
-            for m in members:
+        def g_block(c, n):
+            for m in range(MEM):
                 g_passes(c, n, m, range(PASSES))
 
         def gt_out(c, n, members=range(MEM), engine="scalar"):
@@ -258,8 +260,9 @@ def tile_bjorckmaxmindense_kernel(tc, x_bytes, x_scale, w, d, s, t, b, out):
             else:
                 nc.scalar.copy(out=dst, in_=src)
 
-        def interleave_gt(c, n, engine, ring="stage", slot=None):
-            grouped = sbuf(("gt grouped", c, n), [P, CHUNK, MEM], BF16, ring, 6, slot)
+
+        def interleave_gt(c, n, engine, ring="handover"):
+            grouped = sbuf(("gt grouped", c, n), [P, CHUNK, MEM], BF16, ring, STAGES if ring == "stage" else 1)
             interleave(grouped, tiles["gt planes", c, n], engine)
 
         def quantise_gt(c, n):
@@ -267,18 +270,18 @@ def tile_bjorckmaxmindense_kernel(tc, x_bytes, x_scale, w, d, s, t, b, out):
 
 
         def widen_x(i):
-            x16 = sbuf(("x", i), [P, D], BF16, "x", 6)
+            x16 = sbuf(("x", i), [P, D], BF16, "x", X_BUFFERS)
             nc.scalar.copy(out=x16[:], in_=tiles["x bytes", i][:].bitcast(FP8))
 
         def split(i):
-            return i >= 4
+            return i in (4, 5, 6)
 
         def split_x(i):
-            halves = sbuf(("x split", i), [P, 2, D // 4], F32, "x", 6)
+            halves = sbuf(("x split", i), [P, 2, D // 4], F32, "x", X_BUFFERS)
             nc.scalar.copy(out=halves[:], in_=tiles["x", i][:].bitcast(F32).rearrange("p (w u) -> p u w", u=2))
 
-        def transpose_x(q, passes=range(PASSES)):
-            for k in passes:
+        def transpose_x(q):
+            for k in range(PASSES):
                 turned = bank(("x turned", q, k), [P, 2, 2, P])
                 w0 = K_PASS // 2 * k
                 for z in range(2):
@@ -290,9 +293,9 @@ def tile_bjorckmaxmindense_kernel(tc, x_bytes, x_scale, w, d, s, t, b, out):
                             pairs = tiles["x", i][:].bitcast(F32)[:, w0 + u : w0 + K_PASS // 2 : 2]
                         nc.tensor.transpose(turned[:, u, z, :], pairs, ident[:])
 
-        def x_out(q, passes=range(PASSES)):
+        def x_out(q):
             grouped = sbuf(("x grouped", q), [P, PASSES, QUARTER, 2, 2], BF16, "x_grouped", slot=q % 2)
-            for k in passes:
+            for k in range(PASSES):
                 pairs = tiles["x turned", q, k][:].rearrange("p u z r -> p u (z r)").bitcast(BF16)
                 nc.vector.tensor_tensor(
                     out=grouped[:, k],
@@ -313,16 +316,21 @@ def tile_bjorckmaxmindense_kernel(tc, x_bytes, x_scale, w, d, s, t, b, out):
                     matmul(acc[:, m % 2, :], ("w", c, k), member(m), ("x", q), tok, k == 0, k == PASSES - 1)
 
         def p_out(q, c):
-            planes = sbuf(("ps planes", q, c), [P, MEM, QUARTER], BF16, "ps_planes", 8)
+            planes = sbuf(("ps planes", q), [P, CHUNKS, MEM, QUARTER], BF16, "ps_planes", 4)[:, c]
             affine = sbuf(("1.5 p + b", q, c), [P, MEM, QUARTER], F32, "four_kib", slot=CHUNKS * q + c)
             for m in range(MEM):
                 acc = tiles["p", q, c, m // 2][:, m % 2, :]
                 nc.scalar.activation(out=planes[:, m, :], in_=acc, func=ACT.Copy, scale=gain(1, c, m))
                 nc.scalar.activation(out=affine[:, m, :], in_=acc, func=ACT.Identity, scale=1.5, bias=gain(2, c, m))
 
-        def interleave_ps(q, c, engine, ring="stage", slot=None):
-            grouped = sbuf(("ps grouped", q), [P, CHUNKS, QUARTER, MEM], BF16, ring, 6, slot)
-            interleave(grouped[:, c], tiles["ps planes", q, c], engine)
+        def interleave_ps(q, c, engine):
+            grouped = sbuf(("ps grouped", q), [P, CHUNKS, QUARTER, MEM], BF16, "stage", STAGES)
+            interleave(grouped[:, c], tiles["ps planes", q][:, c], engine)
+
+        def interleave_ps_on_gpsimd(q):
+            grouped = sbuf(("ps grouped", q), [P, CHUNKS, QUARTER, MEM], BF16, "handover")
+            src = tiles["ps planes", q][:].rearrange("p c m r -> p c r m")
+            nc.gpsimd.tensor_scalar(out=grouped[:], in0=src, scalar1=1.0, scalar2=0.0, op0=ALU.mult, op1=ALU.add)
 
         def quantise_ps(q):
             for c in range(CHUNKS):
@@ -336,20 +344,20 @@ def tile_bjorckmaxmindense_kernel(tc, x_bytes, x_scale, w, d, s, t, b, out):
                     tok = slice(0, QUARTER)
                     matmul(acc[:, m % 2, :], ("gt", c, n), member(m), ("ps", q, c), tok, c == 0, c == CHUNKS - 1)
 
-        def r_quarter(q):
-            for n in range(CHUNKS):
+        def r_quarter(q, chunks=range(CHUNKS)):
+            for n in chunks:
                 for i in range(2):
                     r_bank(q, n, i)
 
-        def added_on_tensor(q, n, i):
-            return q == 3
+        def added_on_tensor(q):
+            return q == QUARTERS - 1
 
-        def combine(q, n, pairs=range(2)):
+        def combine(q, n):
             term = sbuf(("h", q, n), [P, MEM, QUARTER], F32, "h", 4)
-            for i in pairs:
+            for i in range(2):
                 members = slice(2 * i, 2 * i + 2)
                 acc = tiles["r", q, n, i]
-                if added_on_tensor(q, n, i):
+                if added_on_tensor(q):
                     nc.scalar.activation(out=term[:, members, :], in_=acc[:], func=ACT.Copy, scale=-0.5)
                 else:
                     nc.vector.scalar_tensor_tensor(
@@ -363,7 +371,7 @@ def tile_bjorckmaxmindense_kernel(tc, x_bytes, x_scale, w, d, s, t, b, out):
 
 
         def turn(turned, q, n, m, tok):
-            terms = (["1.5 p + b"] if added_on_tensor(q, n, m // 2) else []) + ["h"]
+            terms = (["1.5 p + b"] if added_on_tensor(q) else []) + ["h"]
             for z, term in enumerate(terms):
                 nc.tensor.matmul(
                     turned,
@@ -374,40 +382,11 @@ def tile_bjorckmaxmindense_kernel(tc, x_bytes, x_scale, w, d, s, t, b, out):
                     is_transpose=True,
                 )
 
-        def transpose_h(i):
-            for n in (1, 0):
+        def transpose_h(i, chunks=(1, 0)):
+            for n in chunks:
                 turned = bank(("h turned", i, n), [P, MEM, P])
                 for m in range(MEM):
                     turn(turned[:, m, :], i // 2, n, m, member(i % 2))
-
-        def transpose_pair(q, n, i):
-            turned = bank(("pair turned", q, n, i), [P, 2, 2, P])
-            for z in range(2):
-                for m in range(2):
-                    turn(turned[:, z, m, :], q, n, 2 * i + m, member(z))
-
-        def copy_right_pair(q, i):
-            right = sbuf(("right pair", q, i), [P, 2, 2, P], F32, "right", 4)
-            nc.scalar.copy(out=right[:], in_=tiles["pair turned", q, 1, i][:])
-
-        def max_min_pair(q, i):
-            for z in range(2):
-                res = sbuf(("result", 2 * q + z), [P, 2, A, MEM, E], F32, "x", 6)
-                for n, op in enumerate((ALU.max, ALU.min)):
-                    nc.vector.tensor_tensor(
-                        out=res[:, n, :, 2 * i : 2 * i + 2, :],
-                        in0=by_channel(tiles["pair turned", q, 0, i][:, z]),
-                        in1=by_channel(tiles["right pair", q, i][:, z]),
-                        op=op,
-                    )
-                    if i == 1:
-                        store(2 * q + z, n)
-
-        def store(i, n):
-            nc.sync.dma_start(
-                out=out[P * i : P * (i + 1), CHUNK * n : CHUNK * (n + 1)],
-                in_=tiles["result", i][:, n].rearrange("p a m e -> p (a m e)"),
-            )
 
         def by_channel(turned):
             return turned.rearrange("p m (a e) -> p a m e", a=A)
@@ -417,13 +396,24 @@ def tile_bjorckmaxmindense_kernel(tc, x_bytes, x_scale, w, d, s, t, b, out):
             nc.scalar.copy(out=right[:], in_=by_channel(tiles["h turned", i, 1][:]))
 
         def max_min(i):
-            res = sbuf(("result", i), [P, 2, A, MEM, E], F32, "x", 6)
+            res = sbuf(("result", i), [P, 2, A, MEM, E], F32, "x", X_BUFFERS)
             for n, op in enumerate((ALU.max, ALU.min)):
                 nc.vector.tensor_tensor(
                     out=res[:, n], in0=by_channel(tiles["h turned", i, 0][:]), in1=tiles["right", i][:], op=op
                 )
-                store(i, n)
+                nc.sync.dma_start(
+                    out=out[P * i : P * (i + 1), CHUNK * n : CHUNK * (n + 1)],
+                    in_=res[:, n].rearrange("p a m e -> p (a m e)"),
+                )
 
+
+        def prepare(piece):
+            c, k = divmod(piece, PASSES)
+            if spread_on_tensor(c, k):
+                spread_w(c, k)
+            interleave_w(c, k, "scalar")
+            if spread_on_tensor(c, k):
+                spread_out(c, k)
 
         def p_and_out(q, c):
             p_chunk(q, c)
@@ -449,65 +439,68 @@ def tile_bjorckmaxmindense_kernel(tc, x_bytes, x_scale, w, d, s, t, b, out):
         deal_d()
         interleave_w(0, 0, "vector")
         interleave_w(0, 0, "scalar")
-
-        def prepare(piece):
-            c, k = divmod(piece, PASSES)
-            if spread_on_tensor(c, k):
-                spread_w(c, k)
-            interleave_w(c, k, "scalar")
-            if spread_on_tensor(c, k):
-                spread_out(c, k)
-
         prepare(1)
         scale_w(0, 0, blocks=slice(0, A // 2))
         scale_w(0, 0, blocks=slice(A // 2, A))
         interleave_w(0, 1, "vector")
         quantise_w(0, 0)
         quantise_wd(0, 0)
-        for piece in range(2, 6):
-            prepare(piece)
-        g_sweep(0, 0, 0)
+        prepare(2)
+        prepare(3)
         deal_gains()
+        gains_out()
+        prepare(4)
+        g_sweep(0, 0, 0)
         for k in range(1, PASSES):
             scale_w(0, k)
             quantise_w(0, k)
             quantise_wd(0, k)
             g_sweep(0, 0, k)
-        gains_out()
-        interleave_w(1, 2, "scalar", range(2))
+            if k == 1:
+                prepare(5)
+
+        interleave_w(1, 2, "scalar", range(MEM - 1))
         gt_out(0, 0)
-        interleave_w(1, 2, "scalar", range(2, MEM))
+        interleave_w(1, 2, "scalar", (MEM - 1,))
         prepare(7)
-        for k in range(PASSES):
+        quantise_w(1, 0)
+        scale_w(1, 0)
+        quantise_w(1, 1)
+        quantise_wd(1, 0)
+        scale_w(1, 1)
+        interleave_w(1, 2, "vector")
+        quantise_wd(1, 1)
+        for c, n in ((0, 1), (1, 0)):
+            for k in range(2):
+                g_sweep(c, n, k)
+        for k in range(2, PASSES):
             quantise_w(1, k)
             for i in range(2):
                 scale_w(1, k, slice(2 * i, 2 * i + 2))
-            if k + 1 < PASSES:
-                interleave_w(1, k + 1, "vector")
             for i in range(2):
                 quantise_wd(1, k, slice(2 * i, 2 * i + 2))
             g_sweep(0, 1, k)
             g_sweep(1, 0, k)
-        widen_x(0)
-        widen_x(1)
-        interleave_gt(0, 0, "gpsimd", "wd", 1)
-        widen_x(2)
-        gt_out(0, 1, (0, 1))
-        gt_out(0, 1, (2, 3), engine="vector")
-        interleave_gt(0, 1, "gpsimd")
-        widen_x(3)
-        gt_out(1, 0, (2, 3))
-        gt_out(1, 0, (0, 1), engine="vector")
+
+        for i in range(3):
+            widen_x(i)
+        gt_out(0, 1, (0, 1), engine="vector")
+        gt_out(0, 1, (2, 3))
+        interleave_gt(0, 0, "vector")
+        interleave_gt(0, 1, "gpsimd", "stage")
         transpose_x(0)
-        g_block(1, 1, range(MEM))
+        gt_out(1, 0)
+        widen_x(3)
+        g_block(1, 1)
         x_out(0)
         widen_x(4)
         widen_x(5)
         gt_out(1, 1)
         quantise_gt(0, 0)
         quantise_x(0)
+
         transpose_x(1)
-        interleave_gt(1, 0, "gpsimd", "x_grouped", 0)
+        interleave_gt(1, 0, "gpsimd")
         split_x(4)
         split_x(5)
         widen_x(6)
@@ -517,19 +510,19 @@ def tile_bjorckmaxmindense_kernel(tc, x_bytes, x_scale, w, d, s, t, b, out):
         quantise_gt(0, 1)
         quantise_gt(1, 0)
         quantise_x(1)
+
         transpose_x(2)
-        interleave_gt(1, 1, "gpsimd", "x_grouped", 1)
+        interleave_gt(1, 1, "gpsimd")
         widen_x(7)
         split_x(6)
-        split_x(7)
         x_out(2)
         p_and_out(1, 0)
         p_and_out(1, 1)
         quantise_gt(1, 1)
         quantise_x(2)
+
         transpose_x(3)
-        interleave_ps(0, 0, "gpsimd", "x_grouped", 0)
-        interleave_ps(0, 1, "gpsimd", "x_grouped", 0)
+        interleave_ps_on_gpsimd(0)
         x_out(3)
         p_and_out(2, 0)
         p_and_out(2, 1)
@@ -550,8 +543,8 @@ def tile_bjorckmaxmindense_kernel(tc, x_bytes, x_scale, w, d, s, t, b, out):
         combine(1, 0)
         quantise_ps(2)
         combine(1, 1)
-        interleave_ps(last, 0, "scalar")
         turn_h((0, 1))
+        interleave_ps(last, 0, "scalar")
         max_min(0)
         max_min(1)
         p_and_out(last, 1)
@@ -564,10 +557,14 @@ def tile_bjorckmaxmindense_kernel(tc, x_bytes, x_scale, w, d, s, t, b, out):
         max_min(2)
         max_min(3)
         turn_h((4,))
+        transpose_h(5, (1,))
+        copy_right(5)
         max_min(4)
-        r_quarter(last)
-        combine(last, 0)
+        r_quarter(last, (1, 0))
         combine(last, 1)
-        for i in range(5, BLOCKS):
+        combine(last, 0)
+        transpose_h(5, (0,))
+        max_min(5)
+        for i in range(2 * last, BLOCKS):
             turn_h((i,))
             max_min(i)

@@ -33,6 +33,7 @@ def tile_bjorckmaxmindense_kernel(tc, x_bytes, x_scale, w, d, s, t, b, out):
     nc = tc.nc
     with ExitStack() as ctx:
         pool = ctx.enter_context(tc.tile_pool(name="pool", bufs=1))
+        reused = ctx.enter_context(tc.tile_pool(name="reused", bufs=1))
         psum = ctx.enter_context(tc.psum_pool(name="psum", bufs=1))
         tiles = {}
         taken = {}
@@ -47,6 +48,13 @@ def tile_bjorckmaxmindense_kernel(tc, x_bytes, x_scale, w, d, s, t, b, out):
                 else:
                     tag = "%s%d" % (ring, slot)
                 tile = pool.tile(shape, dtype, name=name or tag, tag=tag, align_bytes=64)
+                tiles[key] = tile
+            return tiles[key]
+
+        def placed(key, shape, dtype, slot):
+            if key not in tiles:
+                tag = "placed%d" % len(tiles)
+                tile = reused.tile(shape, dtype, name=tag, tag=tag, align_bytes=64, offset=4096 * slot)
                 tiles[key] = tile
             return tiles[key]
 
@@ -101,7 +109,7 @@ def tile_bjorckmaxmindense_kernel(tc, x_bytes, x_scale, w, d, s, t, b, out):
 
         def load_w(c, k):
             halves = w_halves(c, k)
-            raw = sbuf(("w raw", c, k), [P, halves, 4, CHUNK // halves], BF16, "four_kib", slot=PASSES * c + k)
+            raw = placed(("w raw", c, k), [P, halves, 4, CHUNK // halves], BF16, PASSES * c + k)
             rows = w[K_PASS * k : K_PASS * (k + 1), CHUNK * c : CHUNK * (c + 1)]
             rows = rows.rearrange("(p j) (h f) -> h p j f", j=4, h=halves)
             for half in range(halves):
@@ -150,7 +158,9 @@ def tile_bjorckmaxmindense_kernel(tc, x_bytes, x_scale, w, d, s, t, b, out):
             deal_out(dealt[:], lambda e: gain_blocks[:].rearrange("p i c m e -> p (i c m) e")[:, :, e])
 
         def gains_out():
-            nc.scalar.copy(out=gains[:].rearrange("p i c m -> p (i c m)"), in_=tiles["gains dealt"][:])
+            dealt = tiles["gains dealt"][:].rearrange("p (i x) -> p i x", i=3)
+            for i, factor in enumerate((1.0, -1.0 / 3.0, -2.0)):
+                nc.scalar.activation(out=gains[:, i].rearrange("p c m -> p (c m)"), in_=dealt[:, i], func=ACT.Copy, scale=factor)
 
         def gain(i, c, m):
             return gains[:, i, c, m : m + 1]
@@ -240,7 +250,7 @@ def tile_bjorckmaxmindense_kernel(tc, x_bytes, x_scale, w, d, s, t, b, out):
                 g_passes(c, n, m, range(PASSES))
 
         def gt_out(c, n, members=range(MEM), engine="scalar"):
-            planes = sbuf(("gt planes", c, n), [P, MEM, CHUNK], BF16, "four_kib", slot=PASSES + CHUNKS * c + n)
+            planes = placed(("gt planes", c, n), [P, MEM, CHUNK], BF16, PASSES + CHUNKS * c + n)
             for m in members:
                 acc = tiles["g", c, n, m][:]
                 if engine == "vector":
@@ -274,7 +284,7 @@ def tile_bjorckmaxmindense_kernel(tc, x_bytes, x_scale, w, d, s, t, b, out):
             nc.scalar.copy(out=x16[:], in_=tiles["x bytes", i][:].bitcast(FP8))
 
         def split(i):
-            return i in (4, 5, 6)
+            return i in (0, 4, 5, 6, 7)
 
         def split_x(i):
             halves = sbuf(("x split", i), [P, 2, D // 4], F32, "x", X_BUFFERS)
@@ -316,24 +326,27 @@ def tile_bjorckmaxmindense_kernel(tc, x_bytes, x_scale, w, d, s, t, b, out):
                     matmul(acc[:, m % 2, :], ("w", c, k), member(m), ("x", q), tok, k == 0, k == PASSES - 1)
 
         def p_out(q, c):
-            planes = sbuf(("ps planes", q), [P, CHUNKS, MEM, QUARTER], BF16, "ps_planes", 4)[:, c]
-            affine = sbuf(("1.5 p + b", q, c), [P, MEM, QUARTER], F32, "four_kib", slot=CHUNKS * q + c)
-            for m in range(MEM):
-                acc = tiles["p", q, c, m // 2][:, m % 2, :]
-                nc.scalar.activation(out=planes[:, m, :], in_=acc, func=ACT.Copy, scale=gain(1, c, m))
-                nc.scalar.activation(out=affine[:, m, :], in_=acc, func=ACT.Identity, scale=1.5, bias=gain(2, c, m))
+            kept = placed(("-3 p", q), [P, CHUNKS, MEM, QUARTER], F32, CHUNKS * q)
+            for i in range(2):
+                nc.scalar.activation(out=kept[:, c, 2 * i : 2 * i + 2], in_=tiles["p", q, c, i][:], func=ACT.Copy, scale=-3.0)
 
-        def interleave_ps(q, c, engine):
-            grouped = sbuf(("ps grouped", q), [P, CHUNKS, QUARTER, MEM], BF16, "stage", STAGES)
+        def ps_planes(q, c):
+            planes = sbuf(("ps planes", q), [P, CHUNKS, MEM, QUARTER], BF16, "ps_planes", 2)[:, c]
+            for m in range(MEM):
+                nc.scalar.activation(out=planes[:, m, :], in_=tiles["-3 p", q][:, c, m, :], func=ACT.Copy, scale=gain(1, c, m))
+
+        def interleave_ps(q, c, engine, ring="stage"):
+            grouped = sbuf(("ps grouped", q), [P, CHUNKS, QUARTER, MEM], BF16, ring, STAGES if ring == "stage" else 1)
             interleave(grouped[:, c], tiles["ps planes", q][:, c], engine)
 
-        def interleave_ps_on_gpsimd(q):
-            grouped = sbuf(("ps grouped", q), [P, CHUNKS, QUARTER, MEM], BF16, "handover")
-            src = tiles["ps planes", q][:].rearrange("p c m r -> p c r m")
-            nc.gpsimd.tensor_scalar(out=grouped[:], in0=src, scalar1=1.0, scalar2=0.0, op0=ALU.mult, op1=ALU.add)
+        def make_ps(q, engine, chunks=slice(0, CHUNKS), ring="handover", tok=slice(0, QUARTER)):
+            grouped = sbuf(("ps grouped", q), [P, CHUNKS, QUARTER, MEM], BF16, ring, STAGES if ring == "stage" else 1)
+            src = tiles["-3 p", q][:, chunks, :, tok].rearrange("p c m r -> p c r m")
+            factor = gains[:, 1, chunks].unsqueeze(2).to_broadcast(list(src.shape))
+            engine.tensor_tensor(out=grouped[:, chunks, tok], in0=src, in1=factor, op=ALU.mult)
 
-        def quantise_ps(q):
-            for c in range(CHUNKS):
+        def quantise_ps(q, chunks=range(CHUNKS)):
+            for c in chunks:
                 quantise(("ps", q, c), tiles["ps grouped", q][:, c].rearrange("p r m -> p (r m)"), QUARTER)
 
 
@@ -349,33 +362,32 @@ def tile_bjorckmaxmindense_kernel(tc, x_bytes, x_scale, w, d, s, t, b, out):
                 for i in range(2):
                     r_bank(q, n, i)
 
-        def added_on_tensor(q):
+        def added_on_tensor(q, n):
             return q == QUARTERS - 1
 
         def combine(q, n):
             term = sbuf(("h", q, n), [P, MEM, QUARTER], F32, "h", 4)
-            for i in range(2):
-                members = slice(2 * i, 2 * i + 2)
-                acc = tiles["r", q, n, i]
-                if added_on_tensor(q):
-                    nc.scalar.activation(out=term[:, members, :], in_=acc[:], func=ACT.Copy, scale=-0.5)
+            for m in range(MEM):
+                acc = tiles["r", q, n, m // 2][:, m % 2, :]
+                if added_on_tensor(q, n):
+                    nc.scalar.activation(out=term[:, m, :], in_=acc, func=ACT.Identity, scale=1.0, bias=gain(2, n, m))
                 else:
                     nc.vector.scalar_tensor_tensor(
-                        out=term[:, members, :],
-                        in0=acc[:],
-                        scalar=-0.5,
-                        in1=tiles["1.5 p + b", q, n][:, members, :],
-                        op0=ALU.mult,
+                        out=term[:, m, :],
+                        in0=acc,
+                        scalar=gain(2, n, m),
+                        in1=tiles["-3 p", q][:, n, m, :],
+                        op0=ALU.add,
                         op1=ALU.add,
                     )
 
 
         def turn(turned, q, n, m, tok):
-            terms = (["1.5 p + b"] if added_on_tensor(q) else []) + ["h"]
+            terms = ([tiles["-3 p", q][:, n]] if added_on_tensor(q, n) else []) + [tiles["h", q, n]]
             for z, term in enumerate(terms):
                 nc.tensor.matmul(
                     turned,
-                    lhsT=tiles[term, q, n][:, m, tok],
+                    lhsT=term[:, m, tok],
                     rhs=ident[:],
                     start=(z == 0),
                     stop=(z == len(terms) - 1),
@@ -384,27 +396,23 @@ def tile_bjorckmaxmindense_kernel(tc, x_bytes, x_scale, w, d, s, t, b, out):
 
         def transpose_h(i, chunks=(1, 0)):
             for n in chunks:
-                turned = bank(("h turned", i, n), [P, MEM, P])
+                turned = bank(("h turned", i, n), [P, A, MEM, E])
                 for m in range(MEM):
-                    turn(turned[:, m, :], i // 2, n, m, member(i % 2))
-
-        def by_channel(turned):
-            return turned.rearrange("p m (a e) -> p a m e", a=A)
+                    turn(turned[:, :, m, :], i // 2, n, m, member(i % 2))
 
         def copy_right(i):
-            right = sbuf(("right", i), [P, A, MEM, E], F32, "right", 4)
-            nc.scalar.copy(out=right[:], in_=by_channel(tiles["h turned", i, 1][:]))
+            right = sbuf(("right", i), [P, CHUNK], F32, "right", 4)
+            turned = tiles["h turned", i, 1][:].rearrange("p a m e -> p (a m e)")
+            nc.scalar.activation(out=right[:], in_=turned, func=ACT.Copy, scale=-0.5)
 
         def max_min(i):
-            res = sbuf(("result", i), [P, 2, A, MEM, E], F32, "x", X_BUFFERS)
+            res = sbuf(("result", i), [P, 2, CHUNK], F32, "x", X_BUFFERS)
+            turned = tiles["h turned", i, 0][:].rearrange("p a m e -> p (a m e)")
             for n, op in enumerate((ALU.max, ALU.min)):
-                nc.vector.tensor_tensor(
-                    out=res[:, n], in0=by_channel(tiles["h turned", i, 0][:]), in1=tiles["right", i][:], op=op
+                nc.vector.scalar_tensor_tensor(
+                    out=res[:, n], in0=turned, scalar=-0.5, in1=tiles["right", i][:], op0=ALU.mult, op1=op
                 )
-                nc.sync.dma_start(
-                    out=out[P * i : P * (i + 1), CHUNK * n : CHUNK * (n + 1)],
-                    in_=res[:, n].rearrange("p a m e -> p (a m e)"),
-                )
+                nc.sync.dma_start(out=out[P * i : P * (i + 1), CHUNK * n : CHUNK * (n + 1)], in_=res[:, n])
 
 
         def prepare(piece):
@@ -482,72 +490,79 @@ def tile_bjorckmaxmindense_kernel(tc, x_bytes, x_scale, w, d, s, t, b, out):
             g_sweep(0, 1, k)
             g_sweep(1, 0, k)
 
-        for i in range(3):
-            widen_x(i)
+        widen_x(0)
+        widen_x(1)
+        split_x(0)
         gt_out(0, 1, (0, 1), engine="vector")
         gt_out(0, 1, (2, 3))
         interleave_gt(0, 0, "vector")
         interleave_gt(0, 1, "gpsimd", "stage")
         transpose_x(0)
         gt_out(1, 0)
+        widen_x(2)
         widen_x(3)
         g_block(1, 1)
         x_out(0)
         widen_x(4)
-        widen_x(5)
         gt_out(1, 1)
         quantise_gt(0, 0)
         quantise_x(0)
 
         transpose_x(1)
         interleave_gt(1, 0, "gpsimd")
+        widen_x(5)
         split_x(4)
-        split_x(5)
-        widen_x(6)
         x_out(1)
         p_and_out(0, 0)
+        split_x(5)
         p_and_out(0, 1)
         quantise_gt(0, 1)
         quantise_gt(1, 0)
         quantise_x(1)
 
         transpose_x(2)
-        interleave_gt(1, 1, "gpsimd")
+        make_ps(0, nc.gpsimd, tok=slice(0, 192))
+        widen_x(6)
         widen_x(7)
         split_x(6)
+        split_x(7)
         x_out(2)
+        make_ps(0, nc.vector, tok=slice(192, 256))
         p_and_out(1, 0)
         p_and_out(1, 1)
-        quantise_gt(1, 1)
         quantise_x(2)
+        quantise_ps(0)
 
         transpose_x(3)
-        interleave_ps_on_gpsimd(0)
+        interleave_gt(1, 1, "gpsimd")
         x_out(3)
+        ps_planes(1, 0)
+        ps_planes(1, 1)
+        interleave_ps(1, 0, "scalar", "handover2")
         p_and_out(2, 0)
+        interleave_ps(1, 1, "scalar", "handover2")
         p_and_out(2, 1)
-        quantise_ps(0)
+        quantise_gt(1, 1)
         quantise_x(3)
+        quantise_ps(1)
 
         last = QUARTERS - 1
-        interleave_ps(1, 0, "vector")
-        interleave_ps(1, 1, "vector")
+        make_ps(2, nc.gpsimd, ring="handover2")
         r_quarter(0)
         combine(0, 0)
-        quantise_ps(1)
         combine(0, 1)
-        interleave_ps(2, 0, "scalar")
         p_and_out(last, 0)
-        interleave_ps(2, 1, "vector")
+        ps_planes(last, 0)
+        interleave_ps(last, 0, "scalar")
         r_quarter(1)
         combine(1, 0)
-        quantise_ps(2)
         combine(1, 1)
         turn_h((0, 1))
-        interleave_ps(last, 0, "scalar")
+        quantise_ps(2)
         max_min(0)
         max_min(1)
         p_and_out(last, 1)
+        ps_planes(last, 1)
         interleave_ps(last, 1, "scalar")
         r_quarter(2)
         combine(2, 0)

@@ -26,6 +26,7 @@ BANKS = 8
 STAGES = 6
 X_BUFFERS = 6
 RUN = 4
+VBANKS = ()
 FLOPS = 2 * N * D * F + 2 * D * F * F + 2 * N * F * F
 
 
@@ -91,7 +92,7 @@ def tile_bjorckmaxmindense_kernel(tc, x_bytes, x_scale, w, d, s, t, b, out):
         d_blocks = sbuf("d blocks", [P, PASSES, E, 4], BF16)
         gain_blocks = sbuf("gain blocks", [P, 3, CHUNKS, MEM, E], BF16)
         d_sb = sbuf("d", [P, PASSES, 1, 4], BF16)
-        gains = sbuf("gains", [P, 3, CHUNKS, MEM], F32)
+        gains = sbuf("gains", [P, 4, CHUNKS, MEM], F32)
         padded = [sbuf(("padded identity", z), [P, P + 2 * E], BF16) for z in range(2)]
         ident = sbuf("ident", [P, P], F32)
 
@@ -159,8 +160,8 @@ def tile_bjorckmaxmindense_kernel(tc, x_bytes, x_scale, w, d, s, t, b, out):
 
         def gains_out():
             dealt = tiles["gains dealt"][:].rearrange("p (i x) -> p i x", i=3)
-            for i, factor in enumerate((1.0, -1.0 / 3.0, -2.0)):
-                nc.scalar.activation(out=gains[:, i].rearrange("p c m -> p (c m)"), in_=dealt[:, i], func=ACT.Copy, scale=factor)
+            for i, (source, factor) in enumerate(((0, 1.0), (1, -1.0 / 3.0), (2, -2.0), (1, 1.0))):
+                nc.scalar.activation(out=gains[:, i].rearrange("p c m -> p (c m)"), in_=dealt[:, source], func=ACT.Copy, scale=factor)
 
         def gain(i, c, m):
             return gains[:, i, c, m : m + 1]
@@ -169,32 +170,16 @@ def tile_bjorckmaxmindense_kernel(tc, x_bytes, x_scale, w, d, s, t, b, out):
         def spread_on_tensor(c, k):
             return 1 <= PASSES * c + k <= 5
 
-        def vector_eighths(c, k):
-            return {(0, 0): 6, (0, 1): 1, (1, 2): 2}.get((c, k), 0)
-
-        def interleave_w(c, k, engine, members=range(MEM)):
+        def interleave_blocks(c, k, engine, first, last):
             grouped = sbuf(("w grouped", c, k), [P, MEM, A, E, 4], BF16, "stage", STAGES)
-            dst = grouped[:].rearrange("p m a (z i) j -> p m a z j i", i=RUN)
-            raw = tiles["w raw", c, k]
-            eighths = vector_eighths(c, k)
-
-            def rows(m, first, last):
-                span = A // w_halves(c, k)
-                src = raw[:, first // span].rearrange("p j (a m z i) -> p m a z j i", m=MEM, z=E // RUN, i=RUN)
-                return src[:, m, first % span : first % span + last - first]
-
+            span = A // w_halves(c, k)
+            src = tiles["w raw", c, k][:, first // span].rearrange("p j (a m e) -> p m a j e", m=MEM, e=E)
+            src = src[:, :, first % span : first % span + last - first]
+            dst = grouped[:].rearrange("p m a e j -> p m a j e")[:, :, first:last]
             if engine == "vector":
-                for u in range(eighths):
-                    if (c, k, u) == (0, 0, MEM):
-                        d_out()
-                    m, first = u % MEM, A // 2 * (u // MEM)
-                    nc.vector.tensor_copy(out=dst[:, m, first : first + A // 2], in_=rows(m, first, first + A // 2))
+                nc.vector.tensor_copy(out=dst, in_=src)
             else:
-                for m in members:
-                    first = A // 2 * len(range(m, eighths, MEM))
-                    last = A // 2 if spread_on_tensor(c, k) else A
-                    if first < last:
-                        nc.scalar.copy(out=dst[:, m, first:last], in_=rows(m, first, last))
+                nc.scalar.copy(out=dst, in_=src)
 
         def spread_w(c, k):
             raw = tiles["w raw", c, k]
@@ -325,15 +310,24 @@ def tile_bjorckmaxmindense_kernel(tc, x_bytes, x_scale, w, d, s, t, b, out):
                     tok = slice(QUARTER * k, QUARTER * (k + 1))
                     matmul(acc[:, m % 2, :], ("w", c, k), member(m), ("x", q), tok, k == 0, k == PASSES - 1)
 
-        def p_out(q, c):
+        def p_out(q, c, banks=range(2), engine="scalar"):
             kept = placed(("-3 p", q), [P, CHUNKS, MEM, QUARTER], F32, CHUNKS * q)
-            for i in range(2):
-                nc.scalar.activation(out=kept[:, c, 2 * i : 2 * i + 2], in_=tiles["p", q, c, i][:], func=ACT.Copy, scale=-3.0)
+            for i in banks:
+                dst, acc = kept[:, c, 2 * i : 2 * i + 2], tiles["p", q, c, i][:]
+                if engine == "vector":
+                    nc.vector.tensor_scalar(out=dst, in0=acc, scalar1=-3.0, scalar2=None, op0=ALU.mult)
+                else:
+                    nc.scalar.activation(out=dst, in_=acc, func=ACT.Copy, scale=-3.0)
 
         def ps_planes(q, c):
             planes = sbuf(("ps planes", q), [P, CHUNKS, MEM, QUARTER], BF16, "ps_planes", 2)[:, c]
             for m in range(MEM):
                 nc.scalar.activation(out=planes[:, m, :], in_=tiles["-3 p", q][:, c, m, :], func=ACT.Copy, scale=gain(1, c, m))
+
+        def ps_out(q, c):
+            planes = sbuf(("ps planes", q), [P, CHUNKS, MEM, QUARTER], BF16, "ps_planes", 2)[:, c]
+            for m in range(MEM):
+                nc.scalar.activation(out=planes[:, m, :], in_=tiles["p", q, c, m // 2][:, m % 2, :], func=ACT.Copy, scale=gain(3, c, m))
 
         def interleave_ps(q, c, engine, ring="stage"):
             grouped = sbuf(("ps grouped", q), [P, CHUNKS, QUARTER, MEM], BF16, ring, STAGES if ring == "stage" else 1)
@@ -345,31 +339,31 @@ def tile_bjorckmaxmindense_kernel(tc, x_bytes, x_scale, w, d, s, t, b, out):
             factor = gains[:, 1, chunks].unsqueeze(2).to_broadcast(list(src.shape))
             engine.tensor_tensor(out=grouped[:, chunks, tok], in0=src, in1=factor, op=ALU.mult)
 
-        def quantise_ps(q, chunks=range(CHUNKS)):
-            for c in chunks:
-                quantise(("ps", q, c), tiles["ps grouped", q][:, c].rearrange("p r m -> p (r m)"), QUARTER)
+        def quantise_ps(q, chunks=slice(0, CHUNKS)):
+            src = tiles["ps grouped", q][:, chunks].rearrange("p c r m -> p (c r m)")
+            quantise(("ps", q), src, CHUNKS * QUARTER, cols=slice(QUARTER * chunks.start, QUARTER * chunks.stop))
 
 
         def r_bank(q, n, i):
             acc = bank(("r", q, n, i), [P, 2, QUARTER])
             for m in (2 * i, 2 * i + 1):
                 for c in range(CHUNKS):
-                    tok = slice(0, QUARTER)
-                    matmul(acc[:, m % 2, :], ("gt", c, n), member(m), ("ps", q, c), tok, c == 0, c == CHUNKS - 1)
+                    tok = slice(QUARTER * c, QUARTER * (c + 1))
+                    matmul(acc[:, m % 2, :], ("gt", c, n), member(m), ("ps", q), tok, c == 0, c == CHUNKS - 1)
 
         def r_quarter(q, chunks=range(CHUNKS)):
             for n in chunks:
                 for i in range(2):
                     r_bank(q, n, i)
 
-        def added_on_tensor(q, n):
-            return q == QUARTERS - 1
+        def added_on_tensor(q, n, m):
+            return q == QUARTERS - 1 and (n, m // 2) not in VBANKS
 
-        def combine(q, n):
+        def combine(q, n, members=range(MEM)):
             term = sbuf(("h", q, n), [P, MEM, QUARTER], F32, "h", 4)
-            for m in range(MEM):
+            for m in members:
                 acc = tiles["r", q, n, m // 2][:, m % 2, :]
-                if added_on_tensor(q, n):
+                if added_on_tensor(q, n, m):
                     nc.scalar.activation(out=term[:, m, :], in_=acc, func=ACT.Identity, scale=1.0, bias=gain(2, n, m))
                 else:
                     nc.vector.scalar_tensor_tensor(
@@ -383,7 +377,7 @@ def tile_bjorckmaxmindense_kernel(tc, x_bytes, x_scale, w, d, s, t, b, out):
 
 
         def turn(turned, q, n, m, tok):
-            terms = ([tiles["-3 p", q][:, n]] if added_on_tensor(q, n) else []) + [tiles["h", q, n]]
+            terms = ([tiles["-3 p", q][:, n]] if added_on_tensor(q, n, m) else []) + [tiles["h", q, n]]
             for z, term in enumerate(terms):
                 nc.tensor.matmul(
                     turned,
@@ -412,14 +406,36 @@ def tile_bjorckmaxmindense_kernel(tc, x_bytes, x_scale, w, d, s, t, b, out):
                 nc.vector.scalar_tensor_tensor(
                     out=res[:, n], in0=turned, scalar=-0.5, in1=tiles["right", i][:], op0=ALU.mult, op1=op
                 )
-                nc.sync.dma_start(out=out[P * i : P * (i + 1), CHUNK * n : CHUNK * (n + 1)], in_=res[:, n])
+                if i == BLOCKS - 1:
+                    nc.sync.dma_start(out=out[P * i : P * (i + 1), CHUNK * n : CHUNK * (n + 1)], in_=res[:, n])
+            if i < BLOCKS - 1:
+                nc.sync.dma_start(out=out[P * i : P * (i + 1), :], in_=res[:].rearrange("p n f -> p (n f)"))
+
+        def last_block(i):
+            res = sbuf(("result", i), [P, 2, A, 2, 2 * E], F32, "x", X_BUFFERS)
+            right = tiles["right", i][:].rearrange("p (a u x) -> p a u x", a=A, u=2)
+            for u in range(2):
+                turned = bank(("h turned", i, 0, u), [P, A, 2, E])
+                for m in (2 * u, 2 * u + 1):
+                    turn(turned[:, :, m % 2, :], i // 2, 0, m, member(i % 2))
+            for u in range(2):
+                turned = tiles["h turned", i, 0, u][:].rearrange("p a m e -> p a (m e)")
+                for n, op in enumerate((ALU.max, ALU.min)):
+                    nc.vector.scalar_tensor_tensor(
+                        out=res[:, n, :, u], in0=turned, scalar=-0.5, in1=right[:, :, u], op0=ALU.mult, op1=op
+                    )
+                    if u:
+                        nc.sync.dma_start(
+                            out=out[P * i : P * (i + 1), CHUNK * n : CHUNK * (n + 1)],
+                            in_=res[:, n].rearrange("p a u x -> p (a u x)"),
+                        )
 
 
         def prepare(piece):
             c, k = divmod(piece, PASSES)
             if spread_on_tensor(c, k):
                 spread_w(c, k)
-            interleave_w(c, k, "scalar")
+            interleave_blocks(c, k, "scalar", 2 if piece == 1 else 0, A // 2 if spread_on_tensor(c, k) else A)
             if spread_on_tensor(c, k):
                 spread_out(c, k)
 
@@ -445,12 +461,14 @@ def tile_bjorckmaxmindense_kernel(tc, x_bytes, x_scale, w, d, s, t, b, out):
             load_x(i)
 
         deal_d()
-        interleave_w(0, 0, "vector")
-        interleave_w(0, 0, "scalar")
+        interleave_blocks(0, 0, "vector", 0, 8)
+        d_out()
+        interleave_blocks(0, 0, "vector", 8, 12)
+        interleave_blocks(0, 0, "scalar", 12, 16)
         prepare(1)
         scale_w(0, 0, blocks=slice(0, A // 2))
         scale_w(0, 0, blocks=slice(A // 2, A))
-        interleave_w(0, 1, "vector")
+        interleave_blocks(0, 1, "vector", 0, 2)
         quantise_w(0, 0)
         quantise_wd(0, 0)
         prepare(2)
@@ -467,16 +485,16 @@ def tile_bjorckmaxmindense_kernel(tc, x_bytes, x_scale, w, d, s, t, b, out):
             if k == 1:
                 prepare(5)
 
-        interleave_w(1, 2, "scalar", range(MEM - 1))
+        interleave_blocks(1, 2, "scalar", 4, 12)
         gt_out(0, 0)
-        interleave_w(1, 2, "scalar", (MEM - 1,))
+        interleave_blocks(1, 2, "scalar", 12, 16)
         prepare(7)
         quantise_w(1, 0)
         scale_w(1, 0)
         quantise_w(1, 1)
         quantise_wd(1, 0)
         scale_w(1, 1)
-        interleave_w(1, 2, "vector")
+        interleave_blocks(1, 2, "vector", 0, 4)
         quantise_wd(1, 1)
         for c, n in ((0, 1), (1, 0)):
             for k in range(2):

@@ -26,7 +26,8 @@ BANKS = 8
 STAGES = 6
 X_BUFFERS = 6
 RUN = 4
-VBANKS = ()
+WHOLE_ROWS = 4
+VBANKS = ((0, 1),)
 FLOPS = 2 * N * D * F + 2 * D * F * F + 2 * N * F * F
 
 
@@ -68,6 +69,9 @@ def tile_bjorckmaxmindense_kernel(tc, x_bytes, x_scale, w, d, s, t, b, out):
                 tile = psum.tile(shape, dtype, name=tag, tag=tag)
                 tiles[key] = tile
             return tiles[key]
+
+        def pass_bank():
+            taken["bank"] = taken["bank"] + 1
 
         def quantise(key, src, width, ring=None, slots=1, cols=slice(None)):
             codes = sbuf((key, "codes"), [P, width], U32, ring and ring + "_codes", slots)
@@ -324,9 +328,9 @@ def tile_bjorckmaxmindense_kernel(tc, x_bytes, x_scale, w, d, s, t, b, out):
             for m in range(MEM):
                 nc.scalar.activation(out=planes[:, m, :], in_=tiles["-3 p", q][:, c, m, :], func=ACT.Copy, scale=gain(1, c, m))
 
-        def ps_out(q, c):
+        def ps_out(q, c, members=range(MEM)):
             planes = sbuf(("ps planes", q), [P, CHUNKS, MEM, QUARTER], BF16, "ps_planes", 2)[:, c]
-            for m in range(MEM):
+            for m in members:
                 nc.scalar.activation(out=planes[:, m, :], in_=tiles["p", q, c, m // 2][:, m % 2, :], func=ACT.Copy, scale=gain(3, c, m))
 
         def interleave_ps(q, c, engine, ring="stage"):
@@ -406,9 +410,9 @@ def tile_bjorckmaxmindense_kernel(tc, x_bytes, x_scale, w, d, s, t, b, out):
                 nc.vector.scalar_tensor_tensor(
                     out=res[:, n], in0=turned, scalar=-0.5, in1=tiles["right", i][:], op0=ALU.mult, op1=op
                 )
-                if i == BLOCKS - 1:
+                if i >= WHOLE_ROWS:
                     nc.sync.dma_start(out=out[P * i : P * (i + 1), CHUNK * n : CHUNK * (n + 1)], in_=res[:, n])
-            if i < BLOCKS - 1:
+            if i < WHOLE_ROWS:
                 nc.sync.dma_start(out=out[P * i : P * (i + 1), :], in_=res[:].rearrange("p n f -> p (n f)"))
 
         def last_block(i):
@@ -539,13 +543,13 @@ def tile_bjorckmaxmindense_kernel(tc, x_bytes, x_scale, w, d, s, t, b, out):
         quantise_x(1)
 
         transpose_x(2)
-        make_ps(0, nc.gpsimd, tok=slice(0, 192))
+        make_ps(0, nc.gpsimd, tok=slice(0, 160))
         widen_x(6)
         widen_x(7)
         split_x(6)
         split_x(7)
         x_out(2)
-        make_ps(0, nc.vector, tok=slice(192, 256))
+        make_ps(0, nc.vector, tok=slice(160, 256))
         p_and_out(1, 0)
         p_and_out(1, 1)
         quantise_x(2)
@@ -565,22 +569,25 @@ def tile_bjorckmaxmindense_kernel(tc, x_bytes, x_scale, w, d, s, t, b, out):
         quantise_ps(1)
 
         last = QUARTERS - 1
-        make_ps(2, nc.gpsimd, ring="handover2")
+        make_ps(2, nc.gpsimd, slice(0, 1), ring="handover2")
+        ps_planes(2, 1)
+        interleave_ps(2, 1, "scalar")
         r_quarter(0)
         combine(0, 0)
         combine(0, 1)
         p_and_out(last, 0)
-        ps_planes(last, 0)
-        interleave_ps(last, 0, "scalar")
         r_quarter(1)
         combine(1, 0)
         combine(1, 1)
         turn_h((0, 1))
         quantise_ps(2)
+        make_ps(last, nc.gpsimd, slice(0, 1), ring="handover2")
         max_min(0)
         max_min(1)
-        p_and_out(last, 1)
-        ps_planes(last, 1)
+        p_chunk(last, 1)
+        for i in range(2):
+            ps_out(last, 1, (2 * i, 2 * i + 1))
+            p_out(last, 1, (i,))
         interleave_ps(last, 1, "scalar")
         r_quarter(2)
         combine(2, 0)
@@ -588,16 +595,19 @@ def tile_bjorckmaxmindense_kernel(tc, x_bytes, x_scale, w, d, s, t, b, out):
         quantise_ps(last)
         turn_h((2, 3))
         max_min(2)
-        max_min(3)
         turn_h((4,))
-        transpose_h(5, (1,))
-        copy_right(5)
-        max_min(4)
+        max_min(3)
+        turn_h((5,))
         r_quarter(last, (1, 0))
+        max_min(4)
         combine(last, 1)
-        combine(last, 0)
-        transpose_h(5, (0,))
+        combine(last, 0, (0, 1))
+        combine(last, 0, (2, 3))
         max_min(5)
-        for i in range(2 * last, BLOCKS):
-            turn_h((i,))
-            max_min(i)
+        turn_h((6,))
+        max_min(6)
+        transpose_h(7, (1,))
+        copy_right(7)
+        pass_bank()
+        transpose_h(7, (0,))
+        max_min(7)

@@ -26,8 +26,8 @@ BANKS = 8
 STAGES = 6
 X_BUFFERS = 6
 RUN = 4
-WHOLE_ROWS = 4
-VBANKS = ((0, 1),)
+WHOLE_ROWS = 0
+VBANKS = ((3, 0), (3, 1))
 FLOPS = 2 * N * D * F + 2 * D * F * F + 2 * N * F * F
 
 
@@ -324,18 +324,43 @@ def tile_bjorckmaxmindense_kernel(tc, x_bytes, x_scale, w, d, s, t, b, out):
                     nc.scalar.activation(out=dst, in_=acc, func=ACT.Copy, scale=-3.0)
 
         def ps_planes(q, c):
-            planes = sbuf(("ps planes", q), [P, CHUNKS, MEM, QUARTER], BF16, "ps_planes", 2)[:, c]
+            planes = sbuf(("ps planes", q), [P, CHUNKS, MEM, QUARTER], BF16, "ps_planes", 3)[:, c]
             for m in range(MEM):
                 nc.scalar.activation(out=planes[:, m, :], in_=tiles["-3 p", q][:, c, m, :], func=ACT.Copy, scale=gain(1, c, m))
 
         def ps_out(q, c, members=range(MEM)):
-            planes = sbuf(("ps planes", q), [P, CHUNKS, MEM, QUARTER], BF16, "ps_planes", 2)[:, c]
+            planes = sbuf(("ps planes", q), [P, CHUNKS, MEM, QUARTER], BF16, "ps_planes", 3)[:, c]
             for m in members:
                 nc.scalar.activation(out=planes[:, m, :], in_=tiles["p", q, c, m // 2][:, m % 2, :], func=ACT.Copy, scale=gain(3, c, m))
 
         def interleave_ps(q, c, engine, ring="stage"):
             grouped = sbuf(("ps grouped", q), [P, CHUNKS, QUARTER, MEM], BF16, ring, STAGES if ring == "stage" else 1)
             interleave(grouped[:, c], tiles["ps planes", q][:, c], engine)
+
+        def interleave_ps_on_gpsimd(q, ring="handover"):
+            grouped = sbuf(("ps grouped", q), [P, CHUNKS, QUARTER, MEM], BF16, ring)
+            src = tiles["ps planes", q][:].rearrange("p c m r -> p c r m")
+            nc.gpsimd.tensor_scalar(out=grouped[:], in0=src, scalar1=1.0, scalar2=0.0, op0=ALU.mult, op1=ALU.add)
+
+        def p_both(q, c):
+            kept = placed(("-3 p", q), [P, CHUNKS, MEM, QUARTER], F32, CHUNKS * q)
+            for m in range(MEM):
+                ps_out(q, c, (m,))
+                acc = tiles["p", q, c, m // 2][:, m % 2, :]
+                nc.scalar.activation(out=kept[:, c, m], in_=acc, func=ACT.Identity, scale=-3.0, bias=gain(2, c, m))
+
+        def out_banks(q, n):
+            term = sbuf(("h", q, n), [P, MEM, QUARTER], F32, "h", 4)
+            for i in range(2):
+                nc.scalar.copy(out=term[:, 2 * i : 2 * i + 2], in_=tiles["r", q, n, i][:])
+
+        def combine_banks(q, n):
+            term = sbuf(("h", q, n), [P, MEM, QUARTER], F32, "h", 4)
+            for i in range(2):
+                members = slice(2 * i, 2 * i + 2)
+                nc.vector.tensor_tensor(
+                    out=term[:, members], in0=tiles["r", q, n, i][:], in1=tiles["-3 p", q][:, n, members], op=ALU.add
+                )
 
         def make_ps(q, engine, chunks=slice(0, CHUNKS), ring="handover", tok=slice(0, QUARTER)):
             grouped = sbuf(("ps grouped", q), [P, CHUNKS, QUARTER, MEM], BF16, ring, STAGES if ring == "stage" else 1)
@@ -361,7 +386,7 @@ def tile_bjorckmaxmindense_kernel(tc, x_bytes, x_scale, w, d, s, t, b, out):
                     r_bank(q, n, i)
 
         def added_on_tensor(q, n, m):
-            return q == QUARTERS - 1 and (n, m // 2) not in VBANKS
+            return (q, n) in VBANKS
 
         def combine(q, n, members=range(MEM)):
             term = sbuf(("h", q, n), [P, MEM, QUARTER], F32, "h", 4)
@@ -543,23 +568,23 @@ def tile_bjorckmaxmindense_kernel(tc, x_bytes, x_scale, w, d, s, t, b, out):
         quantise_x(1)
 
         transpose_x(2)
-        make_ps(0, nc.gpsimd, tok=slice(0, 160))
+        make_ps(0, nc.gpsimd)
         widen_x(6)
         widen_x(7)
         split_x(6)
         split_x(7)
         x_out(2)
-        make_ps(0, nc.vector, tok=slice(160, 256))
-        p_and_out(1, 0)
-        p_and_out(1, 1)
+        p_chunk(1, 0)
+        p_both(1, 0)
+        p_chunk(1, 1)
+        p_both(1, 1)
         quantise_x(2)
         quantise_ps(0)
 
         transpose_x(3)
         interleave_gt(1, 1, "gpsimd")
         x_out(3)
-        ps_planes(1, 0)
-        ps_planes(1, 1)
+
         interleave_ps(1, 0, "scalar", "handover2")
         p_and_out(2, 0)
         interleave_ps(1, 1, "scalar", "handover2")
@@ -569,45 +594,39 @@ def tile_bjorckmaxmindense_kernel(tc, x_bytes, x_scale, w, d, s, t, b, out):
         quantise_ps(1)
 
         last = QUARTERS - 1
-        make_ps(2, nc.gpsimd, slice(0, 1), ring="handover2")
-        ps_planes(2, 1)
-        interleave_ps(2, 1, "scalar")
+        make_ps(2, nc.gpsimd, ring="handover2")
         r_quarter(0)
         combine(0, 0)
         combine(0, 1)
-        p_and_out(last, 0)
+        p_chunk(last, 0)
+        p_both(last, 0)
+        interleave_ps(last, 0, "scalar")
         r_quarter(1)
-        combine(1, 0)
-        combine(1, 1)
+        combine_banks(1, 0)
+        combine_banks(1, 1)
         turn_h((0, 1))
-        quantise_ps(2)
-        make_ps(last, nc.gpsimd, slice(0, 1), ring="handover2")
         max_min(0)
+        quantise_ps(2)
         max_min(1)
         p_chunk(last, 1)
-        for i in range(2):
-            ps_out(last, 1, (2 * i, 2 * i + 1))
-            p_out(last, 1, (i,))
+        p_both(last, 1)
         interleave_ps(last, 1, "scalar")
-        r_quarter(2)
-        combine(2, 0)
+        r_quarter(2, (1, 0))
         combine(2, 1)
+        combine(2, 0)
         quantise_ps(last)
         turn_h((2, 3))
         max_min(2)
-        turn_h((4,))
         max_min(3)
-        turn_h((5,))
-        r_quarter(last, (1, 0))
+        turn_h((4,))
+        transpose_h(5, (1,))
+        copy_right(5)
         max_min(4)
-        combine(last, 1)
-        combine(last, 0, (0, 1))
-        combine(last, 0, (2, 3))
+        r_quarter(last, (1, 0))
+        out_banks(last, 1)
+        out_banks(last, 0)
+        transpose_h(5, (0,))
         max_min(5)
-        turn_h((6,))
-        max_min(6)
-        transpose_h(7, (1,))
-        copy_right(7)
-        pass_bank()
-        transpose_h(7, (0,))
-        max_min(7)
+        for i in range(2 * last, BLOCKS):
+            turn_h((i,))
+            max_min(i)

@@ -93,14 +93,12 @@ def tile_bjorckmaxmindense_kernel(tc, x_bytes, x_scale, w, d, s, t, b, out):
             return slice(P * m, P * (m + 1))
 
         x_scale_sb = sbuf("x scale", [P, PASSES, 1, 2, 2], F32)
-        d_blocks = sbuf("d blocks", [P, PASSES, E, 4], BF16)
         gain_blocks = sbuf("gain blocks", [P, 3, CHUNKS, MEM, E], BF16)
-        d_sb = sbuf("d", [P, PASSES, 1, 4], BF16)
+        d_sb = [sbuf(("d", z), [P, n, 1, 16], BF16) for z, n in enumerate((1, PASSES - 1))]
         gains = sbuf("gains", [P, 4, CHUNKS, MEM], F32)
         padded = [sbuf(("padded identity", z), [P, P + 2 * E], BF16) for z in range(2)]
         ident = sbuf("ident", [P, P], F32)
 
-        nc.vector.memset(d_blocks[:], 0.0)
         nc.vector.memset(gain_blocks[:], 0.0)
         nc.vector.memset(padded[1][:], 0.0)
         nc.gpsimd.memset(padded[0][:], 0.0)
@@ -119,7 +117,7 @@ def tile_bjorckmaxmindense_kernel(tc, x_bytes, x_scale, w, d, s, t, b, out):
             rows = rows.rearrange("(p j) (h f) -> h p j f", j=4, h=halves)
             for half in range(halves):
                 if half:
-                    load_d()
+                    load_d(0)
                 nc.sync.dma_start(out=raw[:, half], in_=rows[half])
 
         def load_x(i):
@@ -133,9 +131,10 @@ def tile_bjorckmaxmindense_kernel(tc, x_bytes, x_scale, w, d, s, t, b, out):
             )
 
 
-        def load_d():
+        def load_d(z):
+            first, last = ((0, 1), (1, PASSES))[z]
             nc.sync.dma_start(
-                out=d_blocks[0:P:E].rearrange("a k e j -> a k (e j)"), in_=d.rearrange("(k a x) -> a k x", a=A, k=PASSES)
+                out=d_sb[z][:, :, 0, 0:4], in_=d[K_PASS * first : K_PASS * last].rearrange("(k p j) -> p k j", p=P, j=4)
             )
 
         def load_gains():
@@ -150,13 +149,6 @@ def tile_bjorckmaxmindense_kernel(tc, x_bytes, x_scale, w, d, s, t, b, out):
                 first = E + e % 2 - e
                 shift = padded[e % 2][:, first : first + P]
                 nc.tensor.matmul(acc, lhsT=shift, rhs=values(e), start=(e == 0), stop=(e == E - 1))
-
-        def deal_d():
-            dealt = bank("d dealt", [P, PASSES, 4], F32, BANKS - 2)
-            deal_out(dealt[:].rearrange("p k j -> p (k j)"), lambda e: d_blocks[:, :, e, :])
-
-        def d_out():
-            nc.vector.tensor_copy(out=d_sb[:, :, 0], in_=tiles["d dealt"][:])
 
         def deal_gains():
             dealt = bank("gains dealt", [P, 3 * CHUNKS * MEM], F32, MEM - 1)
@@ -216,7 +208,7 @@ def tile_bjorckmaxmindense_kernel(tc, x_bytes, x_scale, w, d, s, t, b, out):
             nc.vector.tensor_tensor(
                 out=wd[:, members, blocks].rearrange("p m a e j -> p m (a e) j"),
                 in0=src,
-                in1=d_sb[:, k : k + 1].to_broadcast(list(src.shape)),
+                in1=d_sb[min(k, 1)][:, max(k - 1, 0) : max(k, 1), :, 0:4].to_broadcast(list(src.shape)),
                 op=ALU.mult,
             )
 
@@ -480,8 +472,11 @@ def tile_bjorckmaxmindense_kernel(tc, x_bytes, x_scale, w, d, s, t, b, out):
 
         ctx.enter_context(tc.manual_schedule())
 
-        for k in range(PASSES):
-            load_w(0, k)
+        load_w(0, 0)
+        load_w(0, 1)
+        load_d(1)
+        load_w(0, 2)
+        load_w(0, 3)
         load_gains()
         for k in range(PASSES):
             load_w(1, k)
@@ -489,16 +484,16 @@ def tile_bjorckmaxmindense_kernel(tc, x_bytes, x_scale, w, d, s, t, b, out):
         for i in range(BLOCKS):
             load_x(i)
 
-        deal_d()
         interleave_blocks(0, 0, "vector", 0, 8)
-        d_out()
         interleave_blocks(0, 0, "vector", 8, 12)
         interleave_blocks(0, 0, "scalar", 12, 16)
-        prepare(1)
         scale_w(0, 0, blocks=slice(0, A // 2))
+        spread_w(0, 1)
+        interleave_blocks(0, 1, "scalar", 4, 8)
+        spread_out(0, 1)
         scale_w(0, 0, blocks=slice(A // 2, A))
-        interleave_blocks(0, 1, "vector", 0, 2)
         quantise_w(0, 0)
+        interleave_blocks(0, 1, "vector", 0, 4)
         quantise_wd(0, 0)
         prepare(2)
         prepare(3)
@@ -513,7 +508,6 @@ def tile_bjorckmaxmindense_kernel(tc, x_bytes, x_scale, w, d, s, t, b, out):
             g_sweep(0, 0, k)
             if k == 1:
                 prepare(5)
-
         interleave_blocks(1, 2, "scalar", 4, 12)
         gt_out(0, 0)
         interleave_blocks(1, 2, "scalar", 12, 16)
@@ -584,7 +578,6 @@ def tile_bjorckmaxmindense_kernel(tc, x_bytes, x_scale, w, d, s, t, b, out):
         transpose_x(3)
         interleave_gt(1, 1, "gpsimd")
         x_out(3)
-
         interleave_ps(1, 0, "scalar", "handover2")
         p_and_out(2, 0)
         interleave_ps(1, 1, "scalar", "handover2")

from contextlib import ExitStack

import concourse.mybir as mybir
from concourse.masks import make_identity

F32 = mybir.dt.float32
BF16 = mybir.dt.bfloat16
U32 = mybir.dt.uint32
U8 = mybir.dt.uint8
FP8 = mybir.dt.float8_e4m3fn
FP8X4 = mybir.dt.float8_e4m3fn_x4
ALU = mybir.AluOpType
ACT = mybir.ActivationFunctionType

P = 128
N, D, F = 1024, 2048, 1024
K_PASS = 512
PASSES = D // K_PASS
CHUNK = 512
CHUNKS = F // CHUNK
A, MEM, E = 16, 4, 8
QUARTER = 256
QUARTERS = N // QUARTER
BLOCKS = N // P
BANKS = 8
STAGES = 6
X_BUFFERS = 6
RUN = 4
WHOLE_ROWS = 0
VBANKS = ((3, 0), (3, 1))
FLOPS = 2 * N * D * F + 2 * D * F * F + 2 * N * F * F


def tile_bjorckmaxmindense_kernel(tc, x_bytes, x_scale, w, d, s, t, b, out):
    nc = tc.nc
    with ExitStack() as ctx:
        pool = ctx.enter_context(tc.tile_pool(name="pool", bufs=1))
        reused = ctx.enter_context(tc.tile_pool(name="reused", bufs=1))
        psum = ctx.enter_context(tc.psum_pool(name="psum", bufs=1))
        tiles = {}
        taken = {}

        def sbuf(key, shape, dtype, ring=None, slots=1, slot=None, name=None):
            if key not in tiles:
                if ring is None:
                    tag = "keep%d" % len(tiles)
                elif slot is None:
                    tag = "%s%d" % (ring, taken.get(ring, 0) % slots)
                    taken[ring] = taken.get(ring, 0) + 1
                else:
                    tag = "%s%d" % (ring, slot)
                tile = pool.tile(shape, dtype, name=name or tag, tag=tag, align_bytes=64)
                tiles[key] = tile
            return tiles[key]

        def placed(key, shape, dtype, slot):
            if key not in tiles:
                tag = "placed%d" % len(tiles)
                tile = reused.tile(shape, dtype, name=tag, tag=tag, align_bytes=64, offset=4096 * slot)
                tiles[key] = tile
            return tiles[key]

        def bank(key, shape, dtype=F32, slot=None):
            if key not in tiles:
                if slot is None:
                    slot = taken.get("bank", 0) % BANKS
                    taken["bank"] = slot + 1
                tag = "bank%d" % slot
                tile = psum.tile(shape, dtype, name=tag, tag=tag)
                tiles[key] = tile
            return tiles[key]

        def pass_bank():
            taken["bank"] = taken["bank"] + 1

        def quantise(key, src, width, ring=None, slots=1, cols=slice(None)):
            codes = sbuf((key, "codes"), [P, width], U32, ring and ring + "_codes", slots)
            scales = sbuf((key, "scales"), [P, width], U8, ring and ring + "_scales", slots)
            nc.vector.quantize_mx(out=codes[:, cols].bitcast(FP8X4), scales=scales[:, cols], in_=src)

        def matmul(acc, left, left_cols, right, right_cols, start, stop):
            nc.tensor.matmul_mx(
                out=acc,
                lhsT=tiles[left, "codes"][:, left_cols].bitcast(FP8X4),
                lhsT_scale=tiles[left, "scales"][:, left_cols],
                rhs=tiles[right, "codes"][:, right_cols].bitcast(FP8X4),
                rhs_scale=tiles[right, "scales"][:, right_cols],
                start=start,
                stop=stop,
            )

        def member(m):
            return slice(P * m, P * (m + 1))

        x_scale_sb = sbuf("x scale", [P, PASSES, 1, 2, 2], F32)
        gain_blocks = sbuf("gain blocks", [P, 3, CHUNKS, MEM, E], BF16)
        d_sb = [sbuf(("d", z), [P, n, 1, 16], BF16) for z, n in enumerate((1, PASSES - 1))]
        gains = sbuf("gains", [P, 4, CHUNKS, MEM], F32)
        padded = [sbuf(("padded identity", z), [P, P + 2 * E], BF16) for z in range(2)]
        ident = sbuf("ident", [P, P], F32)

        nc.vector.memset(gain_blocks[:], 0.0)
        nc.vector.memset(padded[1][:], 0.0)
        nc.gpsimd.memset(padded[0][:], 0.0)
        make_identity(nc, padded[0][:, E : E + P], nomemset=True)
        make_identity(nc, ident[:])
        nc.vector.tensor_copy(out=padded[1][:, E + 1 : E + 1 + P], in_=padded[0][:, E : E + P])


        def w_halves(c, k):
            return 2 if (c, k) == (0, 0) else 1

        def load_w(c, k):
            halves = w_halves(c, k)
            raw = placed(("w raw", c, k), [P, halves, 4, CHUNK // halves], BF16, PASSES * c + k)
            rows = w[K_PASS * k : K_PASS * (k + 1), CHUNK * c : CHUNK * (c + 1)]
            rows = rows.rearrange("(p j) (h f) -> h p j f", j=4, h=halves)
            for half in range(halves):
                if half:
                    load_d(0)
                nc.sync.dma_start(out=raw[:, half], in_=rows[half])

        def load_x(i):
            codes = sbuf(("x bytes", i), [P, D], U8, "two_kib", slot=i, name="x_bytes%d" % i)
            nc.sync.dma_start(out=codes[:], in_=x_bytes[P * i : P * (i + 1), :])

        def load_x_scale():
            nc.sync.dma_start(
                out=x_scale_sb[:].rearrange("p k o u e -> p k (o u e)"),
                in_=x_scale.rearrange("o (k p j) -> p (o k) j", p=P, j=4),
            )


        def load_d(z):
            first, last = ((0, 1), (1, PASSES))[z]
            nc.sync.dma_start(
                out=d_sb[z][:, :, 0, 0:4], in_=d[K_PASS * first : K_PASS * last].rearrange("(k p j) -> p k j", p=P, j=4)
            )

        def load_gains():
            for i, v in enumerate((t, s, b)):
                nc.sync.dma_start(
                    out=gain_blocks[0:P:E, i].rearrange("a c m e -> a c (m e)"),
                    in_=v.rearrange("(c a x) -> a c x", a=A, c=CHUNKS),
                )

        def deal_out(acc, values):
            for e in range(E):
                first = E + e % 2 - e
                shift = padded[e % 2][:, first : first + P]
                nc.tensor.matmul(acc, lhsT=shift, rhs=values(e), start=(e == 0), stop=(e == E - 1))

        def deal_gains():
            dealt = bank("gains dealt", [P, 3 * CHUNKS * MEM], F32, MEM - 1)
            deal_out(dealt[:], lambda e: gain_blocks[:].rearrange("p i c m e -> p (i c m) e")[:, :, e])

        def gains_out():
            dealt = tiles["gains dealt"][:].rearrange("p (i x) -> p i x", i=3)
            for i, (source, factor) in enumerate(((0, 1.0), (1, -1.0 / 3.0), (2, -2.0), (1, 1.0))):
                nc.scalar.activation(out=gains[:, i].rearrange("p c m -> p (c m)"), in_=dealt[:, source], func=ACT.Copy, scale=factor)

        def gain(i, c, m):
            return gains[:, i, c, m : m + 1]


        def spread_on_tensor(c, k):
            return 1 <= PASSES * c + k <= 5

        def interleave_blocks(c, k, engine, first, last):
            grouped = sbuf(("w grouped", c, k), [P, MEM, A, E, 4], BF16, "stage", STAGES)
            span = A // w_halves(c, k)
            src = tiles["w raw", c, k][:, first // span].rearrange("p j (a m e) -> p m a j e", m=MEM, e=E)
            src = src[:, :, first % span : first % span + last - first]
            dst = grouped[:].rearrange("p m a e j -> p m a j e")[:, :, first:last]
            if engine == "vector":
                nc.vector.tensor_copy(out=dst, in_=src)
            else:
                nc.scalar.copy(out=dst, in_=src)

        def spread_w(c, k):
            raw = tiles["w raw", c, k]
            for u in range(2):
                spread = bank(("w spread", c, k, u), [P, P, 4], BF16, MEM + (2 * k + u) % MEM)
                first = CHUNK // 2 + P * u
                nc.tensor.matmul(
                    spread[:].rearrange("p f j -> p j f"),
                    lhsT=padded[0][:, E : E + P],
                    rhs=raw[:, 0, :, first : first + P],
                    start=True,
                    stop=True,
                )

        def spread_out(c, k):
            grouped = tiles["w grouped", c, k]
            for u in range(2):
                first = A // 2 + A // 4 * u
                nc.scalar.copy(
                    out=grouped[:, :, first : first + A // 4].rearrange("p m a e j -> p m a (e j)"),
                    in_=tiles["w spread", c, k, u][:].rearrange("p (a m e) j -> p m a (e j)", m=MEM, e=E),
                )

        def quantise_w(c, k):
            quantise(("w", c, k), tiles["w grouped", c, k][:].rearrange("p m a e j -> p (m a e j)"), CHUNK)

        def scale_w(c, k, members=slice(0, MEM), blocks=slice(0, A)):
            wd = sbuf(("wd", c, k), [P, MEM, A, E, 4], BF16, "wd", slot=k % 2)
            src = tiles["w grouped", c, k][:, members, blocks].rearrange("p m a e j -> p m (a e) j")
            nc.vector.tensor_tensor(
                out=wd[:, members, blocks].rearrange("p m a e j -> p m (a e) j"),
                in0=src,
                in1=d_sb[min(k, 1)][:, max(k - 1, 0) : max(k, 1), :, 0:4].to_broadcast(list(src.shape)),
                op=ALU.mult,
            )

        def quantise_wd(c, k, members=slice(0, MEM)):
            src = tiles["wd", c, k][:, members].rearrange("p m a e j -> p (m a e j)")
            quantise(("wd", c, k), src, CHUNK, cols=slice(P * members.start, P * members.stop))


        def g_passes(c, n, m, passes):
            acc = bank(("g", c, n, m), [P, CHUNK])
            for k in passes:
                matmul(acc[:], ("wd", c, k), member(m), ("w", n, k), slice(0, CHUNK), k == 0, k == PASSES - 1)

        def g_sweep(c, n, k):
            for m in range(MEM):
                g_passes(c, n, m, (k,))

        def g_block(c, n):
            for m in range(MEM):
                g_passes(c, n, m, range(PASSES))

        def gt_out(c, n, members=range(MEM), engine="scalar"):
            planes = placed(("gt planes", c, n), [P, MEM, CHUNK], BF16, PASSES + CHUNKS * c + n)
            for m in members:
                acc = tiles["g", c, n, m][:]
                if engine == "vector":
                    nc.vector.tensor_scalar(out=planes[:, m, :], in0=acc, scalar1=gain(0, c, m), scalar2=None, op0=ALU.mult)
                else:
                    nc.scalar.activation(out=planes[:, m, :], in_=acc, func=ACT.Copy, scale=gain(0, c, m))

        def interleave(dst, src, engine):
            if engine == "gpsimd":
                src = src[:].rearrange("p m f -> p f m")
                nc.gpsimd.tensor_scalar(out=dst[:], in0=src, scalar1=1.0, scalar2=0.0, op0=ALU.mult, op1=ALU.add)
                return
            dst = dst[:].rearrange("p (f i) m -> p f m i", i=RUN)
            src = src[:].rearrange("p m (f i) -> p f m i", i=RUN)
            if engine == "vector":
                nc.vector.tensor_copy(out=dst, in_=src)
            else:
                nc.scalar.copy(out=dst, in_=src)


        def interleave_gt(c, n, engine, ring="handover"):
            grouped = sbuf(("gt grouped", c, n), [P, CHUNK, MEM], BF16, ring, STAGES if ring == "stage" else 1)
            interleave(grouped, tiles["gt planes", c, n], engine)

        def quantise_gt(c, n):
            quantise(("gt", c, n), tiles["gt grouped", c, n][:].rearrange("p f m -> p (f m)"), CHUNK)


        def widen_x(i):
            x16 = sbuf(("x", i), [P, D], BF16, "x", X_BUFFERS)
            nc.scalar.copy(out=x16[:], in_=tiles["x bytes", i][:].bitcast(FP8))

        def split(i):
            return i in (0, 4, 5, 6, 7)

        def split_x(i):
            halves = sbuf(("x split", i), [P, 2, D // 4], F32, "x", X_BUFFERS)
            nc.scalar.copy(out=halves[:], in_=tiles["x", i][:].bitcast(F32).rearrange("p (w u) -> p u w", u=2))

        def transpose_x(q):
            for k in range(PASSES):
                turned = bank(("x turned", q, k), [P, 2, 2, P])
                w0 = K_PASS // 2 * k
                for z in range(2):
                    i = 2 * q + z
                    for u in range(2):
                        if split(i):
                            pairs = tiles["x split", i][:, u, P * k : P * (k + 1)]
                        else:
                            pairs = tiles["x", i][:].bitcast(F32)[:, w0 + u : w0 + K_PASS // 2 : 2]
                        nc.tensor.transpose(turned[:, u, z, :], pairs, ident[:])

        def x_out(q):
            grouped = sbuf(("x grouped", q), [P, PASSES, QUARTER, 2, 2], BF16, "x_grouped", slot=q % 2)
            for k in range(PASSES):
                pairs = tiles["x turned", q, k][:].rearrange("p u z r -> p u (z r)").bitcast(BF16)
                nc.vector.tensor_tensor(
                    out=grouped[:, k],
                    in0=pairs.rearrange("p u (r e) -> p r u e", e=2),
                    in1=x_scale_sb[:, k].to_broadcast([P, QUARTER, 2, 2]),
                    op=ALU.mult,
                )

        def quantise_x(q):
            quantise(("x", q), tiles["x grouped", q][:].rearrange("p k r u e -> p (k r u e)"), PASSES * QUARTER, "xq", 2)


        def p_chunk(q, c):
            for m in range(MEM):
                acc = bank(("p", q, c, m // 2), [P, 2, QUARTER])
                for k in range(PASSES):
                    tok = slice(QUARTER * k, QUARTER * (k + 1))
                    matmul(acc[:, m % 2, :], ("w", c, k), member(m), ("x", q), tok, k == 0, k == PASSES - 1)

        def p_out(q, c, banks=range(2), engine="scalar"):
            kept = placed(("-3 p", q), [P, CHUNKS, MEM, QUARTER], F32, CHUNKS * q)
            for i in banks:
                dst, acc = kept[:, c, 2 * i : 2 * i + 2], tiles["p", q, c, i][:]
                if engine == "vector":
                    nc.vector.tensor_scalar(out=dst, in0=acc, scalar1=-3.0, scalar2=None, op0=ALU.mult)
                else:
                    nc.scalar.activation(out=dst, in_=acc, func=ACT.Copy, scale=-3.0)

        def ps_planes(q, c):
            planes = sbuf(("ps planes", q), [P, CHUNKS, MEM, QUARTER], BF16, "ps_planes", 3)[:, c]
            for m in range(MEM):
                nc.scalar.activation(out=planes[:, m, :], in_=tiles["-3 p", q][:, c, m, :], func=ACT.Copy, scale=gain(1, c, m))

        def ps_out(q, c, members=range(MEM)):
            planes = sbuf(("ps planes", q), [P, CHUNKS, MEM, QUARTER], BF16, "ps_planes", 3)[:, c]
            for m in members:
                nc.scalar.activation(out=planes[:, m, :], in_=tiles["p", q, c, m // 2][:, m % 2, :], func=ACT.Copy, scale=gain(3, c, m))

        def interleave_ps(q, c, engine, ring="stage"):
            grouped = sbuf(("ps grouped", q), [P, CHUNKS, QUARTER, MEM], BF16, ring, STAGES if ring == "stage" else 1)
            interleave(grouped[:, c], tiles["ps planes", q][:, c], engine)

        def interleave_ps_on_gpsimd(q, ring="handover"):
            grouped = sbuf(("ps grouped", q), [P, CHUNKS, QUARTER, MEM], BF16, ring)
            src = tiles["ps planes", q][:].rearrange("p c m r -> p c r m")
            nc.gpsimd.tensor_scalar(out=grouped[:], in0=src, scalar1=1.0, scalar2=0.0, op0=ALU.mult, op1=ALU.add)

        def p_both(q, c):
            kept = placed(("-3 p", q), [P, CHUNKS, MEM, QUARTER], F32, CHUNKS * q)
            for m in range(MEM):
                ps_out(q, c, (m,))
                acc = tiles["p", q, c, m // 2][:, m % 2, :]
                nc.scalar.activation(out=kept[:, c, m], in_=acc, func=ACT.Identity, scale=-3.0, bias=gain(2, c, m))

        def out_banks(q, n):
            term = sbuf(("h", q, n), [P, MEM, QUARTER], F32, "h", 4)
            for i in range(2):
                nc.scalar.copy(out=term[:, 2 * i : 2 * i + 2], in_=tiles["r", q, n, i][:])

        def combine_banks(q, n):
            term = sbuf(("h", q, n), [P, MEM, QUARTER], F32, "h", 4)
            for i in range(2):
                members = slice(2 * i, 2 * i + 2)
                nc.vector.tensor_tensor(
                    out=term[:, members], in0=tiles["r", q, n, i][:], in1=tiles["-3 p", q][:, n, members], op=ALU.add
                )

        def make_ps(q, engine, chunks=slice(0, CHUNKS), ring="handover", tok=slice(0, QUARTER)):
            grouped = sbuf(("ps grouped", q), [P, CHUNKS, QUARTER, MEM], BF16, ring, STAGES if ring == "stage" else 1)
            src = tiles["-3 p", q][:, chunks, :, tok].rearrange("p c m r -> p c r m")
            factor = gains[:, 1, chunks].unsqueeze(2).to_broadcast(list(src.shape))
            engine.tensor_tensor(out=grouped[:, chunks, tok], in0=src, in1=factor, op=ALU.mult)

        def quantise_ps(q, chunks=slice(0, CHUNKS)):
            src = tiles["ps grouped", q][:, chunks].rearrange("p c r m -> p (c r m)")
            quantise(("ps", q), src, CHUNKS * QUARTER, cols=slice(QUARTER * chunks.start, QUARTER * chunks.stop))


        def r_bank(q, n, i):
            acc = bank(("r", q, n, i), [P, 2, QUARTER])
            for m in (2 * i, 2 * i + 1):
                for c in range(CHUNKS):
                    tok = slice(QUARTER * c, QUARTER * (c + 1))
                    matmul(acc[:, m % 2, :], ("gt", c, n), member(m), ("ps", q), tok, c == 0, c == CHUNKS - 1)

        def r_quarter(q, chunks=range(CHUNKS)):
            for n in chunks:
                for i in range(2):
                    r_bank(q, n, i)

        def added_on_tensor(q, n, m):
            return (q, n) in VBANKS

        def combine(q, n, members=range(MEM)):
            term = sbuf(("h", q, n), [P, MEM, QUARTER], F32, "h", 4)
            for m in members:
                acc = tiles["r", q, n, m // 2][:, m % 2, :]
                if added_on_tensor(q, n, m):
                    nc.scalar.activation(out=term[:, m, :], in_=acc, func=ACT.Identity, scale=1.0, bias=gain(2, n, m))
                else:
                    nc.vector.scalar_tensor_tensor(
                        out=term[:, m, :],
                        in0=acc,
                        scalar=gain(2, n, m),
                        in1=tiles["-3 p", q][:, n, m, :],
                        op0=ALU.add,
                        op1=ALU.add,
                    )


        def turn(turned, q, n, m, tok):
            terms = ([tiles["-3 p", q][:, n]] if added_on_tensor(q, n, m) else []) + [tiles["h", q, n]]
            for z, term in enumerate(terms):
                nc.tensor.matmul(
                    turned,
                    lhsT=term[:, m, tok],
                    rhs=ident[:],
                    start=(z == 0),
                    stop=(z == len(terms) - 1),
                    is_transpose=True,
                )

        def transpose_h(i, chunks=(1, 0)):
            for n in chunks:
                turned = bank(("h turned", i, n), [P, A, MEM, E])
                for m in range(MEM):
                    turn(turned[:, :, m, :], i // 2, n, m, member(i % 2))

        def copy_right(i):
            right = sbuf(("right", i), [P, CHUNK], F32, "right", 4)
            turned = tiles["h turned", i, 1][:].rearrange("p a m e -> p (a m e)")
            nc.scalar.activation(out=right[:], in_=turned, func=ACT.Copy, scale=-0.5)

        def max_min(i):
            res = sbuf(("result", i), [P, 2, CHUNK], F32, "x", X_BUFFERS)
            turned = tiles["h turned", i, 0][:].rearrange("p a m e -> p (a m e)")
            for n, op in enumerate((ALU.max, ALU.min)):
                nc.vector.scalar_tensor_tensor(
                    out=res[:, n], in0=turned, scalar=-0.5, in1=tiles["right", i][:], op0=ALU.mult, op1=op
                )
                if i >= WHOLE_ROWS:
                    nc.sync.dma_start(out=out[P * i : P * (i + 1), CHUNK * n : CHUNK * (n + 1)], in_=res[:, n])
            if i < WHOLE_ROWS:
                nc.sync.dma_start(out=out[P * i : P * (i + 1), :], in_=res[:].rearrange("p n f -> p (n f)"))

        def last_block(i):
            res = sbuf(("result", i), [P, 2, A, 2, 2 * E], F32, "x", X_BUFFERS)
            right = tiles["right", i][:].rearrange("p (a u x) -> p a u x", a=A, u=2)
            for u in range(2):
                turned = bank(("h turned", i, 0, u), [P, A, 2, E])
                for m in (2 * u, 2 * u + 1):
                    turn(turned[:, :, m % 2, :], i // 2, 0, m, member(i % 2))
            for u in range(2):
                turned = tiles["h turned", i, 0, u][:].rearrange("p a m e -> p a (m e)")
                for n, op in enumerate((ALU.max, ALU.min)):
                    nc.vector.scalar_tensor_tensor(
                        out=res[:, n, :, u], in0=turned, scalar=-0.5, in1=right[:, :, u], op0=ALU.mult, op1=op
                    )
                    if u:
                        nc.sync.dma_start(
                            out=out[P * i : P * (i + 1), CHUNK * n : CHUNK * (n + 1)],
                            in_=res[:, n].rearrange("p a u x -> p (a u x)"),
                        )


        def prepare(piece):
            c, k = divmod(piece, PASSES)
            if spread_on_tensor(c, k):
                spread_w(c, k)
            interleave_blocks(c, k, "scalar", 2 if piece == 1 else 0, A // 2 if spread_on_tensor(c, k) else A)
            if spread_on_tensor(c, k):
                spread_out(c, k)

        def p_and_out(q, c):
            p_chunk(q, c)
            p_out(q, c)

        def turn_h(blocks):
            for i in blocks:
                transpose_h(i)
            for i in blocks:
                copy_right(i)

        ctx.enter_context(tc.manual_schedule())

        load_w(0, 0)
        load_w(0, 1)
        load_d(1)
        load_w(0, 2)
        load_w(0, 3)
        load_gains()
        for k in range(PASSES):
            load_w(1, k)
        load_x_scale()
        for i in range(BLOCKS):
            load_x(i)

        interleave_blocks(0, 0, "vector", 0, 8)
        interleave_blocks(0, 0, "vector", 8, 12)
        interleave_blocks(0, 0, "scalar", 12, 16)
        scale_w(0, 0, blocks=slice(0, A // 2))
        spread_w(0, 1)
        interleave_blocks(0, 1, "scalar", 4, 8)
        spread_out(0, 1)
        scale_w(0, 0, blocks=slice(A // 2, A))
        quantise_w(0, 0)
        interleave_blocks(0, 1, "vector", 0, 4)
        quantise_wd(0, 0)
        prepare(2)
        prepare(3)
        deal_gains()
        gains_out()
        prepare(4)
        g_sweep(0, 0, 0)
        for k in range(1, PASSES):
            scale_w(0, k)
            quantise_w(0, k)
            quantise_wd(0, k)
            g_sweep(0, 0, k)
            if k == 1:
                prepare(5)
        interleave_blocks(1, 2, "scalar", 4, 12)
        gt_out(0, 0)
        interleave_blocks(1, 2, "scalar", 12, 16)
        prepare(7)
        quantise_w(1, 0)
        scale_w(1, 0)
        quantise_w(1, 1)
        quantise_wd(1, 0)
        scale_w(1, 1)
        interleave_blocks(1, 2, "vector", 0, 4)
        quantise_wd(1, 1)
        for c, n in ((0, 1), (1, 0)):
            for k in range(2):
                g_sweep(c, n, k)
        for k in range(2, PASSES):
            quantise_w(1, k)
            for i in range(2):
                scale_w(1, k, slice(2 * i, 2 * i + 2))
            for i in range(2):
                quantise_wd(1, k, slice(2 * i, 2 * i + 2))
            g_sweep(0, 1, k)
            g_sweep(1, 0, k)

        widen_x(0)
        widen_x(1)
        split_x(0)
        gt_out(0, 1, (0, 1), engine="vector")
        gt_out(0, 1, (2, 3))
        interleave_gt(0, 0, "vector")
        interleave_gt(0, 1, "gpsimd", "stage")
        transpose_x(0)
        gt_out(1, 0)
        widen_x(2)
        widen_x(3)
        g_block(1, 1)
        x_out(0)
        widen_x(4)
        gt_out(1, 1)
        quantise_gt(0, 0)
        quantise_x(0)

        transpose_x(1)
        interleave_gt(1, 0, "gpsimd")
        widen_x(5)
        split_x(4)
        x_out(1)
        p_and_out(0, 0)
        split_x(5)
        p_and_out(0, 1)
        quantise_gt(0, 1)
        quantise_gt(1, 0)
        quantise_x(1)

        transpose_x(2)
        make_ps(0, nc.gpsimd)
        widen_x(6)
        widen_x(7)
        split_x(6)
        split_x(7)
        x_out(2)
        p_chunk(1, 0)
        p_both(1, 0)
        p_chunk(1, 1)
        p_both(1, 1)
        quantise_x(2)
        quantise_ps(0)

        transpose_x(3)
        interleave_gt(1, 1, "gpsimd")
        x_out(3)
        interleave_ps(1, 0, "scalar", "handover2")
        p_and_out(2, 0)
        interleave_ps(1, 1, "scalar", "handover2")
        p_and_out(2, 1)
        quantise_gt(1, 1)
        quantise_x(3)
        quantise_ps(1)

        last = QUARTERS - 1
        make_ps(2, nc.gpsimd, ring="handover2")
        r_quarter(0)
        combine(0, 0)
        combine(0, 1)
        p_chunk(last, 0)
        p_both(last, 0)
        interleave_ps(last, 0, "scalar")
        r_quarter(1)
        combine_banks(1, 0)
        combine_banks(1, 1)
        turn_h((0, 1))
        max_min(0)
        quantise_ps(2)
        max_min(1)
        p_chunk(last, 1)
        p_both(last, 1)
        interleave_ps(last, 1, "scalar")
        r_quarter(2, (1, 0))
        combine(2, 1)
        combine(2, 0)
        quantise_ps(last)
        turn_h((2, 3))
        max_min(2)
        max_min(3)
        turn_h((4,))
        transpose_h(5, (1,))
        copy_right(5)
        max_min(4)
        r_quarter(last, (1, 0))
        out_banks(last, 1)
        out_banks(last, 0)
        transpose_h(5, (0,))
        max_min(5)
        for i in range(2 * last, BLOCKS):
            turn_h((i,))
            max_min(i)
